import numpy as np
import ml_dtypes


def mxq(x, axis, fmt="e4m3"):
    dtype, down = {"e4m3": (ml_dtypes.float8_e4m3fn, 7), "e5m2": (ml_dtypes.float8_e5m2, 14)}[fmt]
    v = np.moveaxis(np.asarray(x, np.float32).astype(ml_dtypes.bfloat16).astype(np.float64), axis, -1)
    blocks = v.reshape(v.shape[:-1] + (-1, 32))
    amax = np.abs(blocks).max(-1, keepdims=True)
    byte = np.maximum(np.where(amax > 0, np.frexp(amax)[1] - 1 + 127, 0) - down, 1)
    scale = np.exp2(byte - 127.0)
    codes = (blocks / scale).astype(np.float32).astype(dtype).astype(np.float64)
    return np.moveaxis((codes * scale).reshape(v.shape), -1, axis)


WIDE = False


def mx_kscale(k):
    if not WIDE:
        return np.ones(k)
    levels = np.array([10, -10, 5, -5, 0])
    if k % 512:
        return np.exp2(np.random.permutation(np.resize(levels, k // 32))).repeat(32)
    a = np.empty((k // 512, 16))
    for p in range(k // 512):
        a[p, :8] = np.random.permutation(np.resize(levels, 8))
        for g in range(8):
            far = levels[np.abs(levels - a[p, g]) >= 10]
            a[p, g + 8] = far[np.random.randint(len(far))]
    return np.exp2(a.ravel()).repeat(32)


BF16 = ml_dtypes.bfloat16


def bf(x):
    return np.asarray(x, np.float32).astype(BF16)


def f64(x):
    return np.asarray(x).astype(np.float64)


N1, N2, D, T = 6144, 256, 512, 2


def draw0():
    s, t = mx_kscale(D), mx_kscale(D)
    return {"e1": bf(np.random.standard_normal((N1, D)) * s),
            "e2": bf(np.random.standard_normal((N2, D)) / t),
            "w": bf(np.random.standard_normal((T, D, D)) / np.sqrt(D) / s[:, None] * t),
            "v": bf(np.random.standard_normal((T, D)) * 0.5 * t),
            "b": bf(0.3 + 0.1 * np.random.standard_normal(T)),
            "u": bf(np.random.uniform(0.5, 1.5, T))}


def core(e1, e2, w, v, b, u):
    scale = 1.0 / np.sqrt(e1.shape[1])
    t = mxq(f64(e1), 1, "e4m3") @ mxq(f64(w), 1, "e4m3")
    h = t + f64(v)[:, None, :]
    s = scale * (mxq(h, 2, "e4m3") @ mxq(f64(e2), 1, "e4m3").T)
    z = np.tanh(s + f64(b)[:, None, None])
    return np.sum(f64(u)[:, None, None] * z, axis=0)


def e4m3fn_bytes(y):
    return np.clip(np.asarray(y, np.float64), -448.0, 448.0).astype(np.float32).astype(ml_dtypes.float8_e4m3fn).view(np.uint8)


def e4m3fn_values(b):
    return np.asarray(b, np.uint8).view(ml_dtypes.float8_e4m3fn).astype(np.float64)


def setup_inputs():
    d = draw0()
    x0 = np.asarray(d['e1']).astype(np.float64)
    s = (np.max(np.abs(x0), axis=(0,), keepdims=True) / 448.0).astype(np.float32)
    out = {}
    for k, v in d.items():
        if k == 'e1':
            out['e1_bytes'] = e4m3fn_bytes(x0 / s.astype(np.float64))
            out['e1_scale'] = s
        else:
            out[k] = v
    return out


def reference(e1_bytes, e1_scale, e2, w, v, b, u):
    return core(e4m3fn_values(e1_bytes) * e1_scale.astype(np.float64), e2, w, v, b, u)

@@ -1,0 +1,293 @@
+from contextlib import ExitStack
+
+import concourse.mybir as mybir
+from concourse.masks import make_identity
+
+N1, N2, D, T = 6144, 256, 512, 2
+FLOPS = 2 * N1 * D * D * T + 2 * N1 * D * N2 * T
+
+F32 = mybir.dt.float32
+BF16 = mybir.dt.bfloat16
+U32 = mybir.dt.uint32
+U8 = mybir.dt.uint8
+FP8 = mybir.dt.float8_e4m3fn
+FP8X4 = mybir.dt.float8_e4m3fn_x4
+ADD = mybir.AluOpType.add
+MULT = mybir.AluOpType.mult
+ACT = mybir.ActivationFunctionType
+
+P = 128
+PACK = 4
+GROUP = 512
+GROUPS = N1 // GROUP
+HALF = 256
+
+
+def tile_pairwiseneuraltensorscorer_t_kernel(tc, e1_bytes, e1_scale, e2, w, v, b, u, out):
+    nc = tc.nc
+    with ExitStack() as ctx:
+        const = ctx.enter_context(tc.tile_pool(name="const", bufs=1))
+        work = ctx.enter_context(tc.tile_pool(name="work", bufs=3))
+        psum = ctx.enter_context(tc.psum_pool(name="psum", bufs=2))
+        single = ctx.enter_context(tc.psum_pool(name="single", bufs=2))
+
+        ctx.enter_context(tc.manual_schedule())
+
+        e1_rows = e1_bytes.rearrange("(g p j) k -> g p (j k)", p=P, j=4)
+        out_rows = out.rearrange("(g p j) n -> g p j n", p=P, j=4)
+
+        bytes_sb = []
+        for g in range(GROUPS):
+            bytes_tile = const.tile([P, 4 * D], U8, name=f"bytes_sb{g}", align_bytes=64)
+            bytes_sb.append(bytes_tile)
+        scale_sb = const.tile([P, 2, D], F32, name="scale_sb", align_bytes=64)
+        nc.sync.dma_start(out=scale_sb[:, 0, :], in_=e1_scale.rearrange("o k -> (o k)").partition_broadcast(P))
+        nc.sync.dma_start(out=bytes_sb[0][:], in_=e1_rows[0])
+        w_raw = []
+        for s in range(T):
+            w_tile = const.tile([P, PACK, D], BF16, name=f"w_raw{s}", align_bytes=64)
+            nc.sync.dma_start(out=w_tile[:], in_=w[s].rearrange("(p j) c -> p j c", j=PACK))
+            w_raw.append(w_tile)
+        v_sb = const.tile([P, T, PACK], BF16, name="v_sb", align_bytes=64)
+        nc.sync.dma_start(out=v_sb[:], in_=v.rearrange("s (p t) -> p s t", t=PACK))
+        e2_sb = const.tile([P, 2, D], BF16, name="e2_sb", align_bytes=64)
+        nc.sync.dma_start(out=e2_sb[:], in_=e2.rearrange("(r p) k -> p r k", p=P))
+        b_sb = const.tile([P, T], BF16, name="b_sb", align_bytes=64)
+        nc.sync.dma_start(out=b_sb[:], in_=b.partition_broadcast(P))
+        u_sb = const.tile([P, T], BF16, name="u_sb", align_bytes=64)
+        nc.sync.dma_start(out=u_sb[:], in_=u.partition_broadcast(P))
+        for g in range(1, GROUPS):
+            nc.sync.dma_start(out=bytes_sb[g][:], in_=e1_rows[g])
+
+        u_f32 = const.tile([P, T], F32, name="u_f32", align_bytes=64)
+        warm = const.tile([P, 1], F32, name="warm")
+        nc.vector.memset(warm[:], 0.0)
+        warm_out = const.tile([P, 1], F32, name="warm_out")
+        nc.scalar.activation(out=warm_out[:], in_=warm[:], func=ACT.Tanh)
+        ident = const.tile([P, P], F32, name="ident", align_bytes=64)
+        make_identity(nc, ident[:])
+        ident_bf = const.tile([P, P], BF16, name="ident_bf", align_bytes=64)
+        make_identity(nc, ident_bf[:])
+
+        wq, wq_sc = [], []
+        for s in range(T):
+            wq_tile = const.tile([P, D], U32, name=f"wq{s}", align_bytes=64)
+            wq_sc_tile = const.tile([P, D], U8, name=f"wq_sc{s}", align_bytes=64)
+            wq.append(wq_tile)
+            wq_sc.append(wq_sc_tile)
+        e2q = const.tile([P, N2], U32, name="e2q", align_bytes=64)
+        e2q_sc = const.tile([P, N2], U8, name="e2q_sc", align_bytes=64)
+        w_grouped = {}
+        e2_grouped = const.tile([P, N2, PACK], BF16, name="e2_grouped", align_bytes=64)
+
+        def w_interleave(s, engine_copy):
+            grouped = const.tile([P, D, PACK], BF16, name=f"w_grouped{s}", align_bytes=64)
+            w_grouped[s] = grouped
+            engine_copy(
+                out=grouped[:].rearrange("p (t m) j -> p t m j", t=PACK),
+                in_=w_raw[s][:].rearrange("p j (m t) -> p t m j", t=PACK),
+            )
+
+        def w_quantize(s):
+            nc.vector.quantize_mx(out=wq[s][:].bitcast(FP8X4), scales=wq_sc[s][:],
+                                  in_=w_grouped[s][:].rearrange("p c j -> p (c j)"))
+
+        word_bank, xg = {}, {}
+
+        def e2_turn():
+            bank = single.tile([P, 2, HALF], F32, name="words", tag="flex")
+            word_bank["e2", 0] = bank
+            for r in range(2):
+                words = e2_sb[:, r, :].bitcast(F32)
+                for h in range(2):
+                    nc.tensor.transpose(bank[:, h, r * P : (r + 1) * P], words[:, h : 2 * P : 2], ident[:])
+
+        def e2_exit():
+            nc.scalar.copy(out=e2_grouped[:].rearrange("p n j -> p (n j)").bitcast(F32).rearrange("p (n h) -> p n h", h=2),
+                           in_=word_bank["e2", 0][:].rearrange("p h n -> p n h"))
+
+        def e2_quantize():
+            nc.vector.quantize_mx(out=e2q[:].bitcast(FP8X4), scales=e2q_sc[:], in_=e2_grouped[:].rearrange("p n j -> p (n j)"))
+
+        x, eq, eq_sc, banks_v, banks_s, hg, planes, hi, hq, hq_sc, sbank, z, zw, woven, o_sb = ({} for n in range(15))
+
+        def spread_scale():
+            nc.scalar.copy(out=scale_sb[:, 1, :], in_=scale_sb[:, 0, :])
+
+        def prod(g, h):
+            x_tile = work.tile([P, 2, D], BF16, name="x", tag="x", align_bytes=64)
+            x[g, h] = x_tile
+            flat = x_tile[:].rearrange("p j k -> p (j k)")
+            width = D if (g, h) == (0, 0) else 2 * D
+            for c in range(0, 2 * D, width):
+                col = h * 2 * D + c
+                nc.vector.tensor_tensor(out=flat[:, c : c + width], in0=bytes_sb[g][:, col : col + width].bitcast(FP8),
+                                        in1=scale_sb[:].rearrange("p j k -> p (j k)")[:, 0:width], op=MULT)
+
+        def turn(g, h):
+            bank = single.tile([P, 2, HALF], F32, name="words", tag="flex")
+            word_bank[g, h] = bank
+            for j in range(2):
+                words = x[g, h][:, j, :].bitcast(F32)
+                for e in range(2):
+                    nc.tensor.transpose(bank[:, e, j * P : (j + 1) * P], words[:, e : 2 * P : 2], ident[:])
+
+        def word_exit(g, h):
+            if h == 0:
+                grouped = work.tile([P, GROUP, PACK], BF16, name="e_grouped", tag="e_grouped", align_bytes=64)
+                xg[g] = grouped
+            half = xg[g][:, h * HALF : (h + 1) * HALF, :]
+            nc.scalar.copy(out=half.rearrange("p n j -> p (n j)").bitcast(F32).rearrange("p (n e) -> p n e", e=2),
+                           in_=word_bank[g, h][:].rearrange("p e n -> p n e"))
+
+        def quantize_e(g):
+            codes = work.tile([P, GROUP], U32, name="eq", tag="eq", align_bytes=64)
+            sc = work.tile([P, GROUP], U8, name="eq_sc", tag="eq_sc", align_bytes=64)
+            eq[g], eq_sc[g] = codes, sc
+            nc.vector.quantize_mx(out=codes[:].bitcast(FP8X4), scales=sc[:], in_=xg[g][:].rearrange("p n j -> p (n j)"))
+
+        def left_v(g, j):
+            bank = psum.tile([P, PACK, P], F32, name="bank_v", tag="bank_v")
+            banks_v[g, j] = bank
+            cols = slice(j * P, (j + 1) * P)
+            for t in range(PACK):
+                rows = slice(t * P, (t + 1) * P)
+                nc.tensor.matmul_mx(out=bank[:, t, :], lhsT=wq[0][:, rows].bitcast(FP8X4), lhsT_scale=wq_sc[0][:, rows],
+                                    rhs=eq[g][:, cols].bitcast(FP8X4), rhs_scale=eq_sc[g][:, cols], start=True, stop=True)
+
+        def left_s(g, t):
+            bank = psum.tile([P, GROUP], F32, name="bank_s", tag="bank_s")
+            banks_s[g, t] = bank
+            rows = slice(t * P, (t + 1) * P)
+            nc.tensor.matmul_mx(out=bank[:], lhsT=wq[1][:, rows].bitcast(FP8X4), lhsT_scale=wq_sc[1][:, rows],
+                                rhs=eq[g][:].bitcast(FP8X4), rhs_scale=eq_sc[g][:], start=True, stop=True)
+
+        def exit_v(g, j):
+            if j == 0:
+                grouped = work.tile([P, GROUP, PACK], BF16, name="hg", tag="hg", align_bytes=64)
+                hg[g] = grouped
+            nc.vector.tensor_tensor(out=hg[g][:, j * P : (j + 1) * P, :], in0=banks_v[g, j][:].rearrange("p t n -> p n t"),
+                                    in1=v_sb[:, 0, :].unsqueeze(1).to_broadcast([P, P, PACK]), op=ADD)
+
+        def exit_s(g, t):
+            if t == 0:
+                planes_tile = work.tile([P, PACK, GROUP], BF16, name="planes", tag="planes", align_bytes=64)
+                planes[g] = planes_tile
+            nc.scalar.activation(out=planes[g][:, t, :], in_=banks_s[g, t][:], func=ACT.Identity, bias=v_sb[:, 1, t : t + 1])
+
+        def weave(g, h):
+            if h == 1 and g % 2 == 1:
+                return
+            bank = single.tile([P, HALF, PACK], BF16, name="woven", tag="flex")
+            woven[g, h] = bank
+            for j in range(2):
+                cols = slice((2 * h + j) * P, (2 * h + j + 1) * P)
+                nc.tensor.matmul(out=bank[:, j * P : (j + 1) * P, :].rearrange("p n t -> p t n"), lhsT=ident_bf[:],
+                                 rhs=planes[g][:, :, cols], start=True, stop=True)
+
+        def weave_exit(g, h):
+            if h == 0:
+                grouped = work.tile([P, GROUP, PACK], BF16, name="hi", tag="hi", align_bytes=64)
+                hi[g] = grouped
+            cols = slice(h * HALF, (h + 1) * HALF)
+            if (g, h) in woven:
+                nc.scalar.copy(out=hi[g][:, cols, :], in_=woven[g, h][:])
+            else:
+                nc.scalar.copy(out=hi[g][:, cols, :].rearrange("p (c i) t -> p c t i", i=4),
+                               in_=planes[g][:, :, cols].rearrange("p t (c i) -> p c t i", i=4))
+
+        def quantize_h(g, s):
+            codes = work.tile([P, GROUP], U32, name=f"hq{s}", tag=f"hq{s}", align_bytes=64)
+            sc = work.tile([P, GROUP], U8, name=f"hq_sc{s}", tag=f"hq_sc{s}", align_bytes=64)
+            hq[g, s], hq_sc[g, s] = codes, sc
+            src = (hg, hi)[s][g]
+            nc.vector.quantize_mx(out=codes[:].bitcast(FP8X4), scales=sc[:], in_=src[:].rearrange("p n j -> p (n j)"))
+
+        def right(g, s, h):
+            bank = psum.tile([P, 2, N2], F32, name="sbank", tag="sbank")
+            sbank[g, s, h] = bank
+            for j in range(2):
+                cols = slice((2 * h + j) * P, (2 * h + j + 1) * P)
+                nc.tensor.matmul_mx(out=bank[:, j, :], lhsT=hq[g, s][:, cols].bitcast(FP8X4), lhsT_scale=hq_sc[g, s][:, cols],
+                                    rhs=e2q[:].bitcast(FP8X4), rhs_scale=e2q_sc[:], start=True, stop=True)
+
+        def tanh(g, s, h):
+            z_tile = work.tile([P, 2 * N2], F32, name=f"z{s}{h}", tag=f"z{s}{h}", align_bytes=64)
+            z[g, s, h] = z_tile
+            nc.scalar.activation(out=z_tile[:], in_=sbank[g, s, h][:].rearrange("p j n -> p (j n)"), func=ACT.Tanh,
+                                 bias=b_sb[:, s : s + 1], scale=D ** -0.5)
+
+        def weigh(g, h):
+            zw_tile = const.tile([P, 2 * N2], F32, name=f"zw{h}", tag=f"zw{h}", align_bytes=64)
+            zw[g, h] = zw_tile
+            nc.gpsimd.tensor_scalar(out=zw_tile[:], in0=z[g, 0, h][:], scalar1=u_f32[:, 0:1], scalar2=0.0, op0=MULT, op1=ADD)
+
+        def combine(g, h):
+            o = work.tile([P, 2 * N2], F32, name=f"o{h}", tag=f"o{h}", align_bytes=64)
+            nc.vector.scalar_tensor_tensor(out=o[:], in0=z[g, 1, h][:], scalar=u_f32[:, 1:2], in1=zw[g, h][:], op0=MULT, op1=ADD)
+            nc.sync.dma_start(out=out_rows[g][:, 2 * h : 2 * h + 2, :], in_=o[:].rearrange("p (j n) -> p j n", n=N2))
+
+        def run(f, g, *args):
+            if 0 <= g < GROUPS:
+                f(g, *args)
+
+        for i in range(-3, GROUPS + 3):
+            run(weigh, i - 2, 1)
+            if i == -1:
+                e2_turn()
+            if i == -3:
+                spread_scale()
+            if i == 1:
+                e2_quantize()
+            run(word_exit, i + 1, 1)
+            run(quantize_e, i + 1)
+            run(left_v, i, 0)
+            run(tanh, i - 2, 0, 0)
+            run(left_s, i, 1)
+            run(exit_s, i, 2)
+            run(weave, i - 1, 1)
+            run(combine, i - 3, 0)
+            run(tanh, i - 2, 1, 1)
+            run(left_v, i, 1)
+            run(exit_s, i, 1)
+            if i == -2:
+                w_interleave(0, nc.vector.tensor_copy)
+            run(quantize_h, i - 1, 0)
+            run(turn, i + 2, 0)
+            if i == -1:
+                e2_exit()
+            run(weave_exit, i - 1, 1)
+            run(exit_v, i, 0)
+            run(right, i - 2, 1, 0)
+            run(left_s, i + 1, 0)
+            if i == -2:
+                w_interleave(1, nc.scalar.copy)
+            run(left_s, i + 1, 3)
+            run(exit_v, i, 1)
+            run(word_exit, i + 2, 0)
+            run(prod, i + 3, 1)
+            if i == -1:
+                w_quantize(0)
+            run(right, i - 1, 0, 1)
+            run(tanh, i - 2, 1, 0)
+            run(exit_s, i + 1, 0)
+            run(combine, i - 2, 1)
+            run(left_v, i, 3)
+            run(tanh, i - 1, 0, 1)
+            run(exit_s, i + 1, 3)
+            run(weave, i, 0)
+            run(weave_exit, i, 0)
+            run(turn, i + 2, 1)
+            run(quantize_h, i - 1, 1)
+            run(right, i - 1, 0, 0)
+            run(left_v, i, 2)
+            run(exit_v, i, 3)
+            if i == 0:
+                nc.gpsimd.tensor_copy(out=u_f32[:], in_=u_sb[:])
+            run(prod, i + 3, 0)
+            run(left_s, i + 1, 2)
+            run(weigh, i - 2, 0)
+            if i == -2:
+                w_quantize(1)
+            run(exit_v, i, 2)
+            run(right, i - 1, 1, 1)

@@ -21,273 +21,358 @@ PACK = 4
 GROUP = 512
 GROUPS = N1 // GROUP
 HALF = 256
+ROW = PACK * D
+BANK = 512
+SCALED_HALVES = 1
+
+
+def vector_blocks(g):
+    return VB[g]
+
+VB = [4, 3, 3, 2, 3, 3, 2, 3, 2, 2, 3, 3]
+WS = {2: 832, 3: 832, 4: 1280, 5: 832, 6: 832, 7: 832}
+WG = {-1: 2048, 0: 1280, 1: 512, 2: 1472, 3: 320, 4: 1472, 5: 1472, 6: 320, 7: 1472, 8: 1280}
+LEAD = {0: 1, 1: 3, **{n: 1 for n in range(2, 10)}}
+SPACE = {0: 2, 1: 2}
+TURNED_GROUPS = 8
+EARLY = 2
+SW = {10: 128, 11: 128}
 
 
 def tile_pairwiseneuraltensorscorer_t_kernel(tc, e1_bytes, e1_scale, e2, w, v, b, u, out):
     nc = tc.nc
     with ExitStack() as ctx:
-        const = ctx.enter_context(tc.tile_pool(name="const", bufs=1))
-        work = ctx.enter_context(tc.tile_pool(name="work", bufs=3))
-        psum = ctx.enter_context(tc.psum_pool(name="psum", bufs=2))
-        single = ctx.enter_context(tc.psum_pool(name="single", bufs=2))
-
+        sb = ctx.enter_context(tc.tile_pool(name="sb", bufs=1))
+        ps = ctx.enter_context(tc.psum_pool(name="ps", bufs=1))
         ctx.enter_context(tc.manual_schedule())
 
-        e1_rows = e1_bytes.rearrange("(g p j) k -> g p (j k)", p=P, j=4)
-        out_rows = out.rearrange("(g p j) n -> g p j n", p=P, j=4)
+        def tiles(name, count, shape, dtype):
+            return [sb.tile(shape, dtype, name=f"{name}{n}", align_bytes=64) for n in range(count)]
 
-        bytes_sb = []
-        for g in range(GROUPS):
-            bytes_tile = const.tile([P, 4 * D], U8, name=f"bytes_sb{g}", align_bytes=64)
-            bytes_sb.append(bytes_tile)
-        scale_sb = const.tile([P, 2, D], F32, name="scale_sb", align_bytes=64)
-        nc.sync.dma_start(out=scale_sb[:, 0, :], in_=e1_scale.rearrange("o k -> (o k)").partition_broadcast(P))
-        nc.sync.dma_start(out=bytes_sb[0][:], in_=e1_rows[0])
-        w_raw = []
-        for s in range(T):
-            w_tile = const.tile([P, PACK, D], BF16, name=f"w_raw{s}", align_bytes=64)
-            nc.sync.dma_start(out=w_tile[:], in_=w[s].rearrange("(p j) c -> p j c", j=PACK))
-            w_raw.append(w_tile)
-        v_sb = const.tile([P, T, PACK], BF16, name="v_sb", align_bytes=64)
+        e1_rows = e1_bytes.rearrange("(g p j) k -> g p (j k)", p=P, j=PACK)
+        out_rows = out.rearrange("(g p j) n -> g p (j n)", p=P, j=PACK)
+
+        raw = tiles("raw", GROUPS, [P, ROW], U8)
+        wide = tiles("wide", GROUPS, [P, ROW], BF16)
+        w_raw = tiles("w_raw", T, [P, ROW], BF16)
+        w_woven = tiles("w_woven", T, [P, ROW], BF16)
+        wq = tiles("wq", T, [P, D], U32)
+        wq_sc = tiles("wq_sc", T, [P, D], U8)
+        (scale_sb,) = tiles("scale_sb", 1, [P, PACK], F32)
+        (v_sb,) = tiles("v_sb", 1, [P, T, PACK], BF16)
+        (b_sb,) = tiles("b_sb", 1, [P, T], BF16)
+        (u_sb,) = tiles("u_sb", 1, [P, T], BF16)
+        (u_f32,) = tiles("u_f32", 1, [P, T], F32)
+        e2_sb = tiles("e2_sb", 2, [P, D], BF16)
+        (e2_woven,) = tiles("e2_woven", 1, [P, N2 * PACK], BF16)
+        (e2q,) = tiles("e2q", 1, [P, N2], U32)
+        (e2q_sc,) = tiles("e2q_sc", 1, [P, N2], U8)
+        (ident,) = tiles("ident", 1, [P, P], F32)
+        (diag,) = tiles("diag", 1, [P, P], F32)
+        e_woven = [wide[2]] + tiles("e_woven", 1, [P, ROW], BF16) * (GROUPS - 1)
+        eq = tiles("eq", 2, [P, GROUP], U32)
+        eq_sc = tiles("eq_sc", 2, [P, GROUP], U8)
+        planes = tiles("planes", 2, [P, PACK, T * GROUP], BF16)
+        (h_woven,) = tiles("h_woven", 1, [P, T * ROW], BF16)
+        hqs = tiles("hq", 2, [P, T * GROUP], U32)
+        hq_scs = tiles("hq_sc", 2, [P, T * GROUP], U8)
+        z = {(s, h): tiles(f"z{s}{h}_", 2, [P, BANK], F32) for s in range(T) for h in range(2)}
+        zw = tiles("zw", 2, [P, BANK], F32)
+        o_sb = tiles("o_sb", 4, [P, BANK], F32)
+        banks = {"V": [ps.tile([P, BANK], F32, name=f"vbank{n}") for n in range(4)],
+                 "S": [ps.tile([P, BANK], F32, name=f"sbank{n}") for n in range(4)]}
+        held = {}
+        used = {"V": [], "S": []}
+
+        def take(reader, key):
+            bank = banks[reader][len(used[reader]) % 4]
+            used[reader].append(key)
+            held[key] = bank
+            return bank
+
+        nc.sync.dma_start(out=raw[0][:], in_=e1_rows[0])
+        nc.sync.dma_start(out=scale_sb[:], in_=e1_scale.rearrange("o (p t) -> p (o t)", t=PACK))
+        nc.sync.dma_start(out=w_raw[1][:], in_=w[1].rearrange("(p j) c -> p (j c)", j=PACK))
+        nc.sync.dma_start(out=raw[1][:], in_=e1_rows[1])
+        nc.sync.dma_start(out=w_raw[0][:], in_=w[0].rearrange("(p j) c -> p (j c)", j=PACK))
         nc.sync.dma_start(out=v_sb[:], in_=v.rearrange("s (p t) -> p s t", t=PACK))
-        e2_sb = const.tile([P, 2, D], BF16, name="e2_sb", align_bytes=64)
-        nc.sync.dma_start(out=e2_sb[:], in_=e2.rearrange("(r p) k -> p r k", p=P))
-        b_sb = const.tile([P, T], BF16, name="b_sb", align_bytes=64)
+        nc.sync.dma_start(out=raw[2][:], in_=e1_rows[2])
+        for r in range(2):
+            nc.sync.dma_start(out=e2_sb[r][:], in_=e2[r * P : (r + 1) * P, :])
+        nc.sync.dma_start(out=raw[3][:], in_=e1_rows[3])
         nc.sync.dma_start(out=b_sb[:], in_=b.partition_broadcast(P))
-        u_sb = const.tile([P, T], BF16, name="u_sb", align_bytes=64)
         nc.sync.dma_start(out=u_sb[:], in_=u.partition_broadcast(P))
-        for g in range(1, GROUPS):
-            nc.sync.dma_start(out=bytes_sb[g][:], in_=e1_rows[g])
-
-        u_f32 = const.tile([P, T], F32, name="u_f32", align_bytes=64)
-        warm = const.tile([P, 1], F32, name="warm")
-        nc.vector.memset(warm[:], 0.0)
-        warm_out = const.tile([P, 1], F32, name="warm_out")
-        nc.scalar.activation(out=warm_out[:], in_=warm[:], func=ACT.Tanh)
-        ident = const.tile([P, P], F32, name="ident", align_bytes=64)
+        for g in range(4, GROUPS):
+            nc.sync.dma_start(out=raw[g][:], in_=e1_rows[g])
         make_identity(nc, ident[:])
-        ident_bf = const.tile([P, P], BF16, name="ident_bf", align_bytes=64)
-        make_identity(nc, ident_bf[:])
 
-        wq, wq_sc = [], []
-        for s in range(T):
-            wq_tile = const.tile([P, D], U32, name=f"wq{s}", align_bytes=64)
-            wq_sc_tile = const.tile([P, D], U8, name=f"wq_sc{s}", align_bytes=64)
-            wq.append(wq_tile)
-            wq_sc.append(wq_sc_tile)
-        e2q = const.tile([P, N2], U32, name="e2q", align_bytes=64)
-        e2q_sc = const.tile([P, N2], U8, name="e2q_sc", align_bytes=64)
-        w_grouped = {}
-        e2_grouped = const.tile([P, N2, PACK], BF16, name="e2_grouped", align_bytes=64)
+        widened = [0]
 
-        def w_interleave(s, engine_copy):
-            grouped = const.tile([P, D, PACK], BF16, name=f"w_grouped{s}", align_bytes=64)
-            w_grouped[s] = grouped
-            engine_copy(
-                out=grouped[:].rearrange("p (t m) j -> p t m j", t=PACK),
-                in_=w_raw[s][:].rearrange("p j (m t) -> p t m j", t=PACK),
-            )
+        def widen(copy, count):
+            start = widened[-1]
+            end = min(start + count, GROUPS * ROW)
+            while start < end:
+                g, c = divmod(start, ROW)
+                n = min(end - start, ROW - c)
+                copy(out=wide[g][:, c : c + n], in_=raw[g][:, c : c + n].bitcast(FP8))
+                start = start + n
+            widened.append(end)
 
-        def w_quantize(s):
-            nc.vector.quantize_mx(out=wq[s][:].bitcast(FP8X4), scales=wq_sc[s][:],
-                                  in_=w_grouped[s][:].rearrange("p c j -> p (c j)"))
+        def scalar_widen(out, in_):
+            nc.scalar.activation(out=out, in_=in_, func=ACT.Copy)
 
-        word_bank, xg = {}, {}
+        def weave_w(s, copy, part=slice(0, PACK)):
+            copy(out=w_woven[s][:].rearrange("p (t m j) -> p t m j", t=PACK, j=PACK)[:, part],
+                 in_=w_raw[s][:].rearrange("p (j m t) -> p t m j", t=PACK, j=PACK)[:, part])
 
-        def e2_turn():
-            bank = single.tile([P, 2, HALF], F32, name="words", tag="flex")
-            word_bank["e2", 0] = bank
-            for r in range(2):
-                words = e2_sb[:, r, :].bitcast(F32)
-                for h in range(2):
-                    nc.tensor.transpose(bank[:, h, r * P : (r + 1) * P], words[:, h : 2 * P : 2], ident[:])
+        def quantize(codes, scales, src):
+            nc.vector.quantize_mx(out=codes.bitcast(FP8X4), scales=scales, in_=src)
 
-        def e2_exit():
-            nc.scalar.copy(out=e2_grouped[:].rearrange("p n j -> p (n j)").bitcast(F32).rearrange("p (n h) -> p n h", h=2),
-                           in_=word_bank["e2", 0][:].rearrange("p h n -> p n h"))
-
-        def e2_quantize():
-            nc.vector.quantize_mx(out=e2q[:].bitcast(FP8X4), scales=e2q_sc[:], in_=e2_grouped[:].rearrange("p n j -> p (n j)"))
-
-        x, eq, eq_sc, banks_v, banks_s, hg, planes, hi, hq, hq_sc, sbank, z, zw, woven, o_sb = ({} for n in range(15))
-
-        def spread_scale():
-            nc.scalar.copy(out=scale_sb[:, 1, :], in_=scale_sb[:, 0, :])
-
-        def prod(g, h):
-            x_tile = work.tile([P, 2, D], BF16, name="x", tag="x", align_bytes=64)
-            x[g, h] = x_tile
-            flat = x_tile[:].rearrange("p j k -> p (j k)")
-            width = D if (g, h) == (0, 0) else 2 * D
-            for c in range(0, 2 * D, width):
-                col = h * 2 * D + c
-                nc.vector.tensor_tensor(out=flat[:, c : c + width], in0=bytes_sb[g][:, col : col + width].bitcast(FP8),
-                                        in1=scale_sb[:].rearrange("p j k -> p (j k)")[:, 0:width], op=MULT)
-
-        def turn(g, h):
-            bank = single.tile([P, 2, HALF], F32, name="words", tag="flex")
-            word_bank[g, h] = bank
+        def turn_words(bank, rows):
             for j in range(2):
-                words = x[g, h][:, j, :].bitcast(F32)
+                words = rows[j].bitcast(F32)
                 for e in range(2):
-                    nc.tensor.transpose(bank[:, e, j * P : (j + 1) * P], words[:, e : 2 * P : 2], ident[:])
+                    nc.tensor.transpose(bank[:, e * HALF + j * P : e * HALF + (j + 1) * P], words[:, e : 2 * P : 2], ident[:])
 
-        def word_exit(g, h):
-            if h == 0:
-                grouped = work.tile([P, GROUP, PACK], BF16, name="e_grouped", tag="e_grouped", align_bytes=64)
-                xg[g] = grouped
-            half = xg[g][:, h * HALF : (h + 1) * HALF, :]
-            nc.scalar.copy(out=half.rearrange("p n j -> p (n j)").bitcast(F32).rearrange("p (n e) -> p n e", e=2),
-                           in_=word_bank[g, h][:].rearrange("p e n -> p n e"))
+        def turn_e2():
+            turn_words(take("S", "e2"), [e2_sb[0][:], e2_sb[1][:]])
+
+        def exit_e2():
+            nc.scalar.copy(out=e2_woven[:].bitcast(F32).rearrange("p (n e) -> p n e", e=2),
+                           in_=held["e2"][:].rearrange("p (e n) -> p n e", e=2))
+
+        def turn_e(g, h):
+            assert widened[-1] >= g * ROW + (h + 1) * 2 * D
+            turn_words(take("V", ("e", g, h)), [wide[g][:, (2 * h + j) * D : (2 * h + j + 1) * D] for j in range(2)])
+
+        def exit_e(g, h):
+            nc.vector.tensor_tensor(
+                out=e_woven[g][:, h * 2 * D : (h + 1) * 2 * D].rearrange("p (n a e) -> p n a e", a=2, e=2),
+                in0=held["e", g, h][:].bitcast(BF16).rearrange("p (a n e) -> p n a e", a=2, e=2),
+                in1=scale_sb[:].rearrange("p (a e) -> p a e", e=2).unsqueeze(1).to_broadcast([P, HALF, 2, 2]), op=MULT)
 
         def quantize_e(g):
-            codes = work.tile([P, GROUP], U32, name="eq", tag="eq", align_bytes=64)
-            sc = work.tile([P, GROUP], U8, name="eq_sc", tag="eq_sc", align_bytes=64)
-            eq[g], eq_sc[g] = codes, sc
-            nc.vector.quantize_mx(out=codes[:].bitcast(FP8X4), scales=sc[:], in_=xg[g][:].rearrange("p n j -> p (n j)"))
+            quantize(eq[g % 2][:], eq_sc[g % 2][:], e_woven[g][:])
 
-        def left_v(g, j):
-            bank = psum.tile([P, PACK, P], F32, name="bank_v", tag="bank_v")
-            banks_v[g, j] = bank
-            cols = slice(j * P, (j + 1) * P)
-            for t in range(PACK):
-                rows = slice(t * P, (t + 1) * P)
-                nc.tensor.matmul_mx(out=bank[:, t, :], lhsT=wq[0][:, rows].bitcast(FP8X4), lhsT_scale=wq_sc[0][:, rows],
-                                    rhs=eq[g][:, cols].bitcast(FP8X4), rhs_scale=eq_sc[g][:, cols], start=True, stop=True)
-
-        def left_s(g, t):
-            bank = psum.tile([P, GROUP], F32, name="bank_s", tag="bank_s")
-            banks_s[g, t] = bank
+        def left(out, g, s, t, cols):
             rows = slice(t * P, (t + 1) * P)
-            nc.tensor.matmul_mx(out=bank[:], lhsT=wq[1][:, rows].bitcast(FP8X4), lhsT_scale=wq_sc[1][:, rows],
-                                rhs=eq[g][:].bitcast(FP8X4), rhs_scale=eq_sc[g][:], start=True, stop=True)
+            nc.tensor.matmul_mx(out=out, lhsT=wq[s][:, rows].bitcast(FP8X4), lhsT_scale=wq_sc[s][:, rows],
+                                rhs=eq[g % 2][:, cols].bitcast(FP8X4), rhs_scale=eq_sc[g % 2][:, cols], start=True, stop=True)
 
-        def exit_v(g, j):
-            if j == 0:
-                grouped = work.tile([P, GROUP, PACK], BF16, name="hg", tag="hg", align_bytes=64)
-                hg[g] = grouped
-            nc.vector.tensor_tensor(out=hg[g][:, j * P : (j + 1) * P, :], in0=banks_v[g, j][:].rearrange("p t n -> p n t"),
-                                    in1=v_sb[:, 0, :].unsqueeze(1).to_broadcast([P, P, PACK]), op=ADD)
+        def left_v(g, c):
+            s, j = divmod(c, PACK)
+            bank = take("V", ("hv", g, c))
+            for t in range(PACK):
+                left(bank[:, t * P : (t + 1) * P], g, s, t, slice(j * P, (j + 1) * P))
 
-        def exit_s(g, t):
-            if t == 0:
-                planes_tile = work.tile([P, PACK, GROUP], BF16, name="planes", tag="planes", align_bytes=64)
-                planes[g] = planes_tile
-            nc.scalar.activation(out=planes[g][:, t, :], in_=banks_s[g, t][:], func=ACT.Identity, bias=v_sb[:, 1, t : t + 1])
+        def exit_v(g, c):
+            nc.vector.tensor_tensor(out=h_woven[:, c * BANK : (c + 1) * BANK].rearrange("p (n t) -> p n t", t=PACK),
+                                    in0=held["hv", g, c][:].rearrange("p (t n) -> p n t", t=PACK),
+                                    in1=v_sb[:, c // PACK, :].unsqueeze(1).to_broadcast([P, P, PACK]), op=ADD)
 
-        def weave(g, h):
-            if h == 1 and g % 2 == 1:
-                return
-            bank = single.tile([P, HALF, PACK], BF16, name="woven", tag="flex")
-            woven[g, h] = bank
-            for j in range(2):
-                cols = slice((2 * h + j) * P, (2 * h + j + 1) * P)
-                nc.tensor.matmul(out=bank[:, j * P : (j + 1) * P, :].rearrange("p n t -> p t n"), lhsT=ident_bf[:],
-                                 rhs=planes[g][:, :, cols], start=True, stop=True)
+        def scalar_banks(g):
+            found = []
+            for s in (1, 0):
+                start = min(max(vector_blocks(g) * P - s * GROUP, 0), GROUP)
+                end = GROUP
+                while end > start:
+                    width = GROUP if end - start == GROUP else HALF if end - start >= HALF else P
+                    per_bank = BANK // width
+                    for first in range(0, PACK, per_bank):
+                        found.append([(s, end - width, width, t) for t in range(first, first + per_bank)])
+                    end = end - width
+            return found
 
-        def weave_exit(g, h):
-            if h == 0:
-                grouped = work.tile([P, GROUP, PACK], BF16, name="hi", tag="hi", align_bytes=64)
-                hi[g] = grouped
-            cols = slice(h * HALF, (h + 1) * HALF)
-            if (g, h) in woven:
-                nc.scalar.copy(out=hi[g][:, cols, :], in_=woven[g, h][:])
-            else:
-                nc.scalar.copy(out=hi[g][:, cols, :].rearrange("p (c i) t -> p c t i", i=4),
-                               in_=planes[g][:, :, cols].rearrange("p t (c i) -> p c t i", i=4))
+        def left_s(g, c):
+            bank = take("S", ("hs", g, c))
+            for n, (s, start, width, t) in enumerate(scalar_banks(g)[c]):
+                left(bank[:, n * width : (n + 1) * width], g, s, t, slice(start, start + width))
 
-        def quantize_h(g, s):
-            codes = work.tile([P, GROUP], U32, name=f"hq{s}", tag=f"hq{s}", align_bytes=64)
-            sc = work.tile([P, GROUP], U8, name=f"hq_sc{s}", tag=f"hq_sc{s}", align_bytes=64)
-            hq[g, s], hq_sc[g, s] = codes, sc
-            src = (hg, hi)[s][g]
-            nc.vector.quantize_mx(out=codes[:].bitcast(FP8X4), scales=sc[:], in_=src[:].rearrange("p n j -> p (n j)"))
+        def exit_s(g, c):
+            for n, (s, start, width, t) in enumerate(scalar_banks(g)[c]):
+                nc.scalar.activation(out=planes[g % 2][:, t, s * GROUP + start : s * GROUP + start + width],
+                                     in_=held["hs", g, c][:, n * width : (n + 1) * width], func=ACT.Identity,
+                                     bias=v_sb[:, s, t : t + 1])
+
+        def weave(copy, g, start, end):
+            if end > start:
+                copy(out=h_woven[:, start * PACK : end * PACK].rearrange("p (n t) -> p n t", t=PACK),
+                     in_=planes[g % 2][:, :, start:end].rearrange("p t n -> p n t"))
+
+        def weave_h(g):
+            weave(nc.gpsimd.tensor_copy, g, vector_blocks(g) * P + SW.get(g, 0), T * GROUP)
+
+        def weave_hs(g):
+            weave(nc.scalar.copy, g, vector_blocks(g) * P, vector_blocks(g) * P + SW.get(g, 0))
+
+        def quantize_h(g):
+            quantize(hqs[g % 2][:], hq_scs[g % 2][:], h_woven[:])
+
+        def turned(g, h):
+            return h >= SCALED_HALVES and g < TURNED_GROUPS
 
         def right(g, s, h):
-            bank = psum.tile([P, 2, N2], F32, name="sbank", tag="sbank")
-            sbank[g, s, h] = bank
+            bank = take("S", ("z", g, s, h))
+            hq, hq_sc = hqs[g % 2], hq_scs[g % 2]
             for j in range(2):
-                cols = slice((2 * h + j) * P, (2 * h + j + 1) * P)
-                nc.tensor.matmul_mx(out=bank[:, j, :], lhsT=hq[g, s][:, cols].bitcast(FP8X4), lhsT_scale=hq_sc[g, s][:, cols],
-                                    rhs=e2q[:].bitcast(FP8X4), rhs_scale=e2q_sc[:], start=True, stop=True)
+                if s == 0 and turned(g, h):
+                    fixed, fixed_sc, cols = e2q, e2q_sc, slice(j * P, (j + 1) * P)
+                    moving, moving_sc, rows = hq, hq_sc, slice(h * HALF, (h + 1) * HALF)
+                else:
+                    first = s * GROUP + (2 * h + j) * P
+                    fixed, fixed_sc, cols = hq, hq_sc, slice(first, first + P)
+                    moving, moving_sc, rows = e2q, e2q_sc, slice(0, N2)
+                nc.tensor.matmul_mx(out=bank[:, j * HALF : (j + 1) * HALF], lhsT=fixed[:, cols].bitcast(FP8X4), lhsT_scale=fixed_sc[:, cols],
+                                    rhs=moving[:, rows].bitcast(FP8X4), rhs_scale=moving_sc[:, rows], start=True, stop=True)
 
         def tanh(g, s, h):
-            z_tile = work.tile([P, 2 * N2], F32, name=f"z{s}{h}", tag=f"z{s}{h}", align_bytes=64)
-            z[g, s, h] = z_tile
-            nc.scalar.activation(out=z_tile[:], in_=sbank[g, s, h][:].rearrange("p j n -> p (j n)"), func=ACT.Tanh,
+            nc.scalar.activation(out=z[s, h][g % 2][:], in_=held["z", g, s, h][:], func=ACT.Tanh,
                                  bias=b_sb[:, s : s + 1], scale=D ** -0.5)
 
         def weigh(g, h):
-            zw_tile = const.tile([P, 2 * N2], F32, name=f"zw{h}", tag=f"zw{h}", align_bytes=64)
-            zw[g, h] = zw_tile
-            nc.gpsimd.tensor_scalar(out=zw_tile[:], in0=z[g, 0, h][:], scalar1=u_f32[:, 0:1], scalar2=0.0, op0=MULT, op1=ADD)
+            if turned(g, h):
+                nc.scalar.activation(out=zw[h][:], in_=z[1, h][g % 2][:], func=ACT.Copy, scale=u_f32[:, 1:2])
+
+        def lift(g, h):
+            bank = take("V", ("o", g, h))
+            src = z[0, h][g % 2]
+            if turned(g, h):
+                for j in range(2):
+                    for c in range(2):
+                        nc.tensor.transpose(bank[:, j * N2 + c * P : j * N2 + (c + 1) * P],
+                                            src[:, c * HALF + j * P : c * HALF + (j + 1) * P], ident[:])
+            else:
+                nc.tensor.matmul(out=bank[:], lhsT=diag[:], rhs=src[:], start=True, stop=True)
 
         def combine(g, h):
-            o = work.tile([P, 2 * N2], F32, name=f"o{h}", tag=f"o{h}", align_bytes=64)
-            nc.vector.scalar_tensor_tensor(out=o[:], in0=z[g, 1, h][:], scalar=u_f32[:, 1:2], in1=zw[g, h][:], op0=MULT, op1=ADD)
-            nc.sync.dma_start(out=out_rows[g][:, 2 * h : 2 * h + 2, :], in_=o[:].rearrange("p (j n) -> p j n", n=N2))
+            o = o_sb[(2 * g + h) % 4]
+            if turned(g, h):
+                nc.vector.scalar_tensor_tensor(out=o[:], in0=held["o", g, h][:], scalar=u_f32[:, 0:1], in1=zw[h][:], op0=MULT, op1=ADD)
+            else:
+                nc.vector.scalar_tensor_tensor(out=o[:], in0=z[1, h][g % 2][:], scalar=u_f32[:, 1:2], in1=held["o", g, h][:], op0=MULT, op1=ADD)
+            nc.sync.dma_start(out=out_rows[g][:, h * BANK : (h + 1) * BANK], in_=o[:])
 
         def run(f, g, *args):
             if 0 <= g < GROUPS:
                 f(g, *args)
 
-        for i in range(-3, GROUPS + 3):
-            run(weigh, i - 2, 1)
-            if i == -1:
-                e2_turn()
-            if i == -3:
-                spread_scale()
-            if i == 1:
-                e2_quantize()
-            run(word_exit, i + 1, 1)
-            run(quantize_e, i + 1)
-            run(left_v, i, 0)
-            run(tanh, i - 2, 0, 0)
-            run(left_s, i, 1)
-            run(exit_s, i, 2)
-            run(weave, i - 1, 1)
-            run(combine, i - 3, 0)
-            run(tanh, i - 2, 1, 1)
-            run(left_v, i, 1)
-            run(exit_s, i, 1)
-            if i == -2:
-                w_interleave(0, nc.vector.tensor_copy)
-            run(quantize_h, i - 1, 0)
-            run(turn, i + 2, 0)
-            if i == -1:
-                e2_exit()
-            run(weave_exit, i - 1, 1)
-            run(exit_v, i, 0)
-            run(right, i - 2, 1, 0)
-            run(left_s, i + 1, 0)
-            if i == -2:
-                w_interleave(1, nc.scalar.copy)
-            run(left_s, i + 1, 3)
-            run(exit_v, i, 1)
-            run(word_exit, i + 2, 0)
-            run(prod, i + 3, 1)
-            if i == -1:
-                w_quantize(0)
-            run(right, i - 1, 0, 1)
-            run(tanh, i - 2, 1, 0)
-            run(exit_s, i + 1, 0)
-            run(combine, i - 2, 1)
-            run(left_v, i, 3)
-            run(tanh, i - 1, 0, 1)
-            run(exit_s, i + 1, 3)
-            run(weave, i, 0)
-            run(weave_exit, i, 0)
-            run(turn, i + 2, 1)
-            run(quantize_h, i - 1, 1)
-            run(right, i - 1, 0, 0)
-            run(left_v, i, 2)
-            run(exit_v, i, 3)
+        widen(nc.vector.tensor_copy, 1024)
+        widen(scalar_widen, 512)
+        widen(nc.vector.tensor_copy, 512)
+        turn_e(0, 0)
+        turn_e(0, 1)
+        weave_w(1, nc.vector.tensor_copy, slice(0, 2))
+        weave_w(1, nc.scalar.copy, slice(2, 4))
+        widen(nc.gpsimd.tensor_copy, 1024)
+        widen(scalar_widen, 1024)
+        exit_e(0, 0)
+        exit_e(0, 1)
+        turn_e(1, 0)
+        turn_e(1, 1)
+        weave_w(0, nc.scalar.copy)
+        quantize(wq[1][:], wq_sc[1][:], w_woven[1][:])
+
+        for i in range(-1, GROUPS - 2):
             if i == 0:
-                nc.gpsimd.tensor_copy(out=u_f32[:], in_=u_sb[:])
-            run(prod, i + 3, 0)
-            run(left_s, i + 1, 2)
-            run(weigh, i - 2, 0)
-            if i == -2:
-                w_quantize(1)
-            run(exit_v, i, 2)
-            run(right, i - 1, 1, 1)
+                quantize(wq[0][:], wq_sc[0][:], w_woven[0][:])
+            if i == 1:
+                quantize(e2q[:], e2q_sc[:], e2_woven[:])
+            run(quantize_e, i + 1)
+            run(quantize_h, i - 1)
+            run(weave_h, i)
+            if i >= 0:
+                widen(scalar_widen, max((i + 4) * ROW - widened[-1], WS.get(i, 0)))
+            widen(nc.gpsimd.tensor_copy, WG.get(i, 0))
+            if i == 0:
+                nc.scalar.copy(out=u_f32[:], in_=u_sb[:])
+            for h in range(2):
+                run(weigh, i - 2, h)
+            n_s = len(scalar_banks(i + 1)) if 0 <= i + 1 < GROUPS else 0
+            n_v = vector_blocks(i) if 0 <= i < GROUPS else 0
+            fills = [(left_s, exit_s, (i + 1, c)) for c in range(min(n_s, 4))]
+            if 0 <= i - 1 < GROUPS:
+                fills += [(right, tanh, (i - 1, 0, h)) for h in range(2)]
+            fills += [(left_s, exit_s, (i + 1, c)) for c in range(4, n_s)]
+            if 0 <= i - 1 < GROUPS:
+                fills += [(right, tanh, (i - 1, 1, h)) for h in range(2)]
+            reads = [(exit_e, (i + 2, h)) for h in range(2) if 0 <= i + 2 < GROUPS]
+            reads += [(combine, (i - 2, 1))] if 0 <= i - 2 < GROUPS else []
+            for f, a in reads:
+                f(*a)
+            if 0 <= i - 2 < GROUPS:
+                for fill, drain, a in fills[:EARLY]:
+                    fill(*a)
+                    drain(*a)
+                fills = fills[EARLY:]
+                lift(i - 2, 0)
+                combine(i - 2, 0)
+                reads.append(None)
+            done_v = min(4 - len(reads), n_v)
+            for c in range(done_v):
+                left_v(i, c)
+                exit_v(i, c)
+            lead = LEAD.get(i, 3)
+            for n, (fill, drain, a) in enumerate(fills):
+                fill(*a)
+                drain(*a)
+                if n == 1:
+                    run(weave_hs, i)
+                if n >= lead and (n - lead) % SPACE.get(i, 1) == 0 and done_v < n_v:
+                    left_v(i, done_v)
+                    exit_v(i, done_v)
+                    done_v = done_v + 1
+            for c in range(done_v, n_v):
+                left_v(i, c)
+                exit_v(i, c)
+            if i == 0:
+                nc.scalar.activation(out=diag[:], in_=ident[:], func=ACT.Copy, scale=u_f32[:, 0:1])
+            for h in range(2):
+                run(turn_e, i + 3, h)
+            if i < GROUPS - 3:
+                run(lift, i - 1, 1)
+            if i == -1:
+                turn_e2()
+                exit_e2()
+
+        def both(fill, drain, *a):
+            fill(*a)
+            drain(*a)
+
+        last = GROUPS - 1
+        for g in (last - 1, last):
+            if g < last:
+                quantize_e(last)
+            quantize_h(g - 1)
+            weave_h(g)
+            fills = [(left_s, exit_s, last, c) for c in range(len(scalar_banks(last)))] if g < last else []
+            fills += [(right, tanh, g - 1, s, h) for s in range(T) for h in range(2)]
+            both(left_v, exit_v, g, 0)
+            both(left_v, exit_v, g, 1)
+            both(*fills.pop(0))
+            both(lift, combine, g - 2, 0)
+            both(*fills.pop(0))
+            weave_hs(g)
+            both(left_v, exit_v, g, 2)
+            both(*fills.pop(0))
+            both(lift, combine, g - 2, 1)
+            for c in range(3, vector_blocks(g)):
+                both(left_v, exit_v, g, c)
+            for f in fills:
+                both(*f)
+        for s in range(T):
+            cols = slice(s * GROUP, (s + 1) * GROUP)
+            quantize(hqs[last % 2][:, cols], hq_scs[last % 2][:, cols], h_woven[:, s * ROW : (s + 1) * ROW])
+        lift(last - 1, 0)
+        for h in range(2):
+            both(right, tanh, last, 0, h)
+        lift(last - 1, 1)
+        for h in range(2):
+            both(right, tanh, last, 1, h)
+        for h in range(2):
+            combine(last - 1, h)
+        for h in range(2):
+            nc.vector.tensor_scalar(out=zw[h][:], in0=z[0, h][last % 2][:], scalar1=u_f32[:, 0:1], scalar2=None, op0=MULT)
+        for h in range(2):
+            o = o_sb[(2 * last + h) % 4]
+            nc.vector.scalar_tensor_tensor(out=o[:], in0=z[1, h][last % 2][:], scalar=u_f32[:, 1:2], in1=zw[h][:], op0=MULT, op1=ADD)
+            nc.sync.dma_start(out=out_rows[last][:, h * BANK : (h + 1) * BANK], in_=o[:])

@@ -29,14 +29,14 @@ SCALED_HALVES = 1
 def vector_blocks(g):
     return VB[g]
 
-VB = [4, 3, 3, 2, 3, 3, 2, 3, 2, 2, 3, 3]
-WS = {2: 832, 3: 832, 4: 1280, 5: 832, 6: 832, 7: 832}
-WG = {-1: 2048, 0: 1280, 1: 512, 2: 1472, 3: 320, 4: 1472, 5: 1472, 6: 320, 7: 1472, 8: 1280}
+VB = [4, 3, 3, 2, 3, 3, 2, 3, 2, 2, 3, 4]
+WS = {-1: 1536, 0: 1536, 1: 1024, 2: 832, 3: 832, 4: 1280, 5: 832, 6: 832, 7: 832}
+WG = {-1: 1856, 0: 1280, 1: 320, 2: 1472, 3: 320, 4: 1472, 5: 1472, 6: 320, 7: 1472, 8: 1280}
 LEAD = {0: 1, 1: 3, **{n: 1 for n in range(2, 10)}}
 SPACE = {0: 2, 1: 2}
-TURNED_GROUPS = 8
+TURNED_GROUPS = 10
 EARLY = 2
-SW = {10: 128, 11: 128}
+SW = {10: 128}
 
 
 def tile_pairwiseneuraltensorscorer_t_kernel(tc, e1_bytes, e1_scale, e2, w, v, b, u, out):
@@ -54,7 +54,7 @@ def tile_pairwiseneuraltensorscorer_t_kernel(tc, e1_bytes, e1_scale, e2, w, v, b
 
         raw = tiles("raw", GROUPS, [P, ROW], U8)
         wide = tiles("wide", GROUPS, [P, ROW], BF16)
-        w_raw = tiles("w_raw", T, [P, ROW], BF16)
+        w_raw = [tiles(f"w_raw{s}_", 2, [P, PACK * HALF], BF16) for s in range(T)]
         w_woven = tiles("w_woven", T, [P, ROW], BF16)
         wq = tiles("wq", T, [P, D], U32)
         wq_sc = tiles("wq_sc", T, [P, D], U8)
@@ -69,7 +69,7 @@ def tile_pairwiseneuraltensorscorer_t_kernel(tc, e1_bytes, e1_scale, e2, w, v, b
         (e2q_sc,) = tiles("e2q_sc", 1, [P, N2], U8)
         (ident,) = tiles("ident", 1, [P, P], F32)
         (diag,) = tiles("diag", 1, [P, P], F32)
-        e_woven = [wide[2]] + tiles("e_woven", 1, [P, ROW], BF16) * (GROUPS - 1)
+        e_woven = [wide[3]] + tiles("e_woven", 1, [P, ROW], BF16) * (GROUPS - 1)
         eq = tiles("eq", 2, [P, GROUP], U32)
         eq_sc = tiles("eq_sc", 2, [P, GROUP], U8)
         planes = tiles("planes", 2, [P, PACK, T * GROUP], BF16)
@@ -78,7 +78,7 @@ def tile_pairwiseneuraltensorscorer_t_kernel(tc, e1_bytes, e1_scale, e2, w, v, b
         hq_scs = tiles("hq_sc", 2, [P, T * GROUP], U8)
         z = {(s, h): tiles(f"z{s}{h}_", 2, [P, BANK], F32) for s in range(T) for h in range(2)}
         zw = tiles("zw", 2, [P, BANK], F32)
-        o_sb = tiles("o_sb", 4, [P, BANK], F32)
+        o_sb = tiles("o_sb", 2 * GROUPS, [P, BANK], F32)
         banks = {"V": [ps.tile([P, BANK], F32, name=f"vbank{n}") for n in range(4)],
                  "S": [ps.tile([P, BANK], F32, name=f"sbank{n}") for n in range(4)]}
         held = {}
@@ -90,19 +90,26 @@ def tile_pairwiseneuraltensorscorer_t_kernel(tc, e1_bytes, e1_scale, e2, w, v, b
             held[key] = bank
             return bank
 
+        def load_w(s, h):
+            nc.sync.dma_start(out=w_raw[s][h][:].rearrange("p (j c) -> p j c", j=PACK),
+                              in_=w[s].rearrange("(p j) c -> p j c", j=PACK)[:, :, h * HALF : (h + 1) * HALF])
+
         nc.sync.dma_start(out=raw[0][:], in_=e1_rows[0])
-        nc.sync.dma_start(out=scale_sb[:], in_=e1_scale.rearrange("o (p t) -> p (o t)", t=PACK))
-        nc.sync.dma_start(out=w_raw[1][:], in_=w[1].rearrange("(p j) c -> p (j c)", j=PACK))
         nc.sync.dma_start(out=raw[1][:], in_=e1_rows[1])
-        nc.sync.dma_start(out=w_raw[0][:], in_=w[0].rearrange("(p j) c -> p (j c)", j=PACK))
-        nc.sync.dma_start(out=v_sb[:], in_=v.rearrange("s (p t) -> p s t", t=PACK))
+        load_w(1, 0)
+        nc.sync.dma_start(out=scale_sb[:], in_=e1_scale.rearrange("o (p t) -> p (o t)", t=PACK))
+        load_w(1, 1)
+        load_w(0, 0)
+        load_w(0, 1)
         nc.sync.dma_start(out=raw[2][:], in_=e1_rows[2])
         for r in range(2):
             nc.sync.dma_start(out=e2_sb[r][:], in_=e2[r * P : (r + 1) * P, :])
         nc.sync.dma_start(out=raw[3][:], in_=e1_rows[3])
+        nc.sync.dma_start(out=v_sb[:], in_=v.rearrange("s (p t) -> p s t", t=PACK))
+        nc.sync.dma_start(out=raw[4][:], in_=e1_rows[4])
         nc.sync.dma_start(out=b_sb[:], in_=b.partition_broadcast(P))
         nc.sync.dma_start(out=u_sb[:], in_=u.partition_broadcast(P))
-        for g in range(4, GROUPS):
+        for g in range(5, GROUPS):
             nc.sync.dma_start(out=raw[g][:], in_=e1_rows[g])
         make_identity(nc, ident[:])
 
@@ -121,9 +128,10 @@ def tile_pairwiseneuraltensorscorer_t_kernel(tc, e1_bytes, e1_scale, e2, w, v, b
         def scalar_widen(out, in_):
             nc.scalar.activation(out=out, in_=in_, func=ACT.Copy)
 
-        def weave_w(s, copy, part=slice(0, PACK)):
-            copy(out=w_woven[s][:].rearrange("p (t m j) -> p t m j", t=PACK, j=PACK)[:, part],
-                 in_=w_raw[s][:].rearrange("p (j m t) -> p t m j", t=PACK, j=PACK)[:, part])
+        def weave_w(s, h, copy):
+            part = slice(h * HALF // PACK, (h + 1) * HALF // PACK)
+            copy(out=w_woven[s][:].rearrange("p (t m j) -> p t m j", t=PACK, j=PACK)[:, :, part],
+                 in_=w_raw[s][h][:].rearrange("p (j m t) -> p t m j", t=PACK, j=PACK))
 
         def quantize(codes, scales, src):
             nc.vector.quantize_mx(out=codes.bitcast(FP8X4), scales=scales, in_=src)
@@ -245,7 +253,7 @@ def tile_pairwiseneuraltensorscorer_t_kernel(tc, e1_bytes, e1_scale, e2, w, v, b
                 nc.tensor.matmul(out=bank[:], lhsT=diag[:], rhs=src[:], start=True, stop=True)
 
         def combine(g, h):
-            o = o_sb[(2 * g + h) % 4]
+            o = o_sb[2 * g + h]
             if turned(g, h):
                 nc.vector.scalar_tensor_tensor(out=o[:], in0=held["o", g, h][:], scalar=u_f32[:, 0:1], in1=zw[h][:], op0=MULT, op1=ADD)
             else:
@@ -256,20 +264,23 @@ def tile_pairwiseneuraltensorscorer_t_kernel(tc, e1_bytes, e1_scale, e2, w, v, b
             if 0 <= g < GROUPS:
                 f(g, *args)
 
+        def both(fill, drain, *a):
+            fill(*a)
+            drain(*a)
+
         widen(nc.vector.tensor_copy, 1024)
-        widen(scalar_widen, 512)
-        widen(nc.vector.tensor_copy, 512)
+        widen(scalar_widen, 1024)
         turn_e(0, 0)
         turn_e(0, 1)
-        weave_w(1, nc.vector.tensor_copy, slice(0, 2))
-        weave_w(1, nc.scalar.copy, slice(2, 4))
-        widen(nc.gpsimd.tensor_copy, 1024)
-        widen(scalar_widen, 1024)
+        widen(nc.gpsimd.tensor_copy, ROW)
+        weave_w(1, 0, nc.scalar.copy)
+        weave_w(1, 1, nc.scalar.copy)
         exit_e(0, 0)
         exit_e(0, 1)
         turn_e(1, 0)
         turn_e(1, 1)
-        weave_w(0, nc.scalar.copy)
+        weave_w(0, 0, nc.scalar.copy)
+        weave_w(0, 1, nc.gpsimd.tensor_copy)
         quantize(wq[1][:], wq_sc[1][:], w_woven[1][:])
 
         for i in range(-1, GROUPS - 2):
@@ -280,9 +291,11 @@ def tile_pairwiseneuraltensorscorer_t_kernel(tc, e1_bytes, e1_scale, e2, w, v, b
             run(quantize_e, i + 1)
             run(quantize_h, i - 1)
             run(weave_h, i)
-            if i >= 0:
+            if i >= -1:
                 widen(scalar_widen, max((i + 4) * ROW - widened[-1], WS.get(i, 0)))
             widen(nc.gpsimd.tensor_copy, WG.get(i, 0))
+            if i == -1:
+                both(turn_e2, exit_e2)
             if i == 0:
                 nc.scalar.copy(out=u_f32[:], in_=u_sb[:])
             for h in range(2):
@@ -330,49 +343,63 @@ def tile_pairwiseneuraltensorscorer_t_kernel(tc, e1_bytes, e1_scale, e2, w, v, b
                 run(turn_e, i + 3, h)
             if i < GROUPS - 3:
                 run(lift, i - 1, 1)
-            if i == -1:
-                turn_e2()
-                exit_e2()
-
-        def both(fill, drain, *a):
-            fill(*a)
-            drain(*a)
 
         last = GROUPS - 1
-        for g in (last - 1, last):
-            if g < last:
-                quantize_e(last)
-            quantize_h(g - 1)
-            weave_h(g)
-            fills = [(left_s, exit_s, last, c) for c in range(len(scalar_banks(last)))] if g < last else []
-            fills += [(right, tanh, g - 1, s, h) for s in range(T) for h in range(2)]
-            both(left_v, exit_v, g, 0)
-            both(left_v, exit_v, g, 1)
-            both(*fills.pop(0))
-            both(lift, combine, g - 2, 0)
-            both(*fills.pop(0))
-            weave_hs(g)
-            both(left_v, exit_v, g, 2)
-            both(*fills.pop(0))
-            both(lift, combine, g - 2, 1)
-            for c in range(3, vector_blocks(g)):
-                both(left_v, exit_v, g, c)
-            for f in fills:
-                both(*f)
+        quantize_e(last)
+        quantize_h(last - 2)
+        weave_h(last - 1)
+        both(left_v, exit_v, last - 1, 0)
+        both(left_v, exit_v, last - 1, 1)
+        weigh(last - 3, 1)
+        both(lift, combine, last - 3, 1)
+        both(left_s, exit_s, last, 0)
+        both(left_s, exit_s, last, 1)
+        both(lift, combine, last - 3, 0)
+        weave_hs(last - 1)
+        for c in range(2, vector_blocks(last - 1)):
+            both(left_v, exit_v, last - 1, c)
+        for c in range(2, len(scalar_banks(last))):
+            both(left_s, exit_s, last, c)
+        quantize_h(last - 1)
+        weave_h(last)
+        both(right, tanh, last - 2, 0, 0)
+        both(left_v, exit_v, last, 0)
+        both(right, tanh, last - 2, 0, 1)
+        both(left_v, exit_v, last, 1)
+        both(right, tanh, last - 2, 1, 0)
+        both(left_v, exit_v, last, 2)
+        both(right, tanh, last - 2, 1, 1)
+        for c in range(3, vector_blocks(last)):
+            both(left_v, exit_v, last, c)
+        weave_hs(last)
+        both(lift, combine, last - 2, 0)
+        weigh(last - 2, 1)
+        for s in range(T):
+            for h in range(2):
+                both(right, tanh, last - 1, s, h)
         for s in range(T):
             cols = slice(s * GROUP, (s + 1) * GROUP)
             quantize(hqs[last % 2][:, cols], hq_scs[last % 2][:, cols], h_woven[:, s * ROW : (s + 1) * ROW])
-        lift(last - 1, 0)
+        both(lift, combine, last - 2, 1)
+        spare = h_woven[:, ROW : ROW + 2 * BANK].bitcast(F32)
+        nc.gpsimd.tensor_scalar(out=spare, in0=z[0, 1][(last - 1) % 2][:], scalar1=u_f32[:, 0:1], scalar2=0.0, op0=MULT, op1=ADD)
         for h in range(2):
             both(right, tanh, last, 0, h)
-        lift(last - 1, 1)
+        bank = take("V", ("o", last - 1, 0))
         for h in range(2):
+            cols = slice(h * HALF, (h + 1) * HALF)
+            nc.tensor.matmul(out=bank[:, cols], lhsT=diag[:], rhs=z[0, 0][(last - 1) % 2][:, cols], start=True, stop=True)
             both(right, tanh, last, 1, h)
-        for h in range(2):
-            combine(last - 1, h)
+
+        def add_in_sbuf(g, h, weighed):
+            o = o_sb[2 * g + h]
+            nc.vector.scalar_tensor_tensor(out=o[:], in0=z[1, h][g % 2][:], scalar=u_f32[:, 1:2], in1=weighed, op0=MULT, op1=ADD)
+            nc.sync.dma_start(out=out_rows[g][:, h * BANK : (h + 1) * BANK], in_=o[:])
+
+        add_in_sbuf(last - 1, 1, spare)
         for h in range(2):
             nc.vector.tensor_scalar(out=zw[h][:], in0=z[0, h][last % 2][:], scalar1=u_f32[:, 0:1], scalar2=None, op0=MULT)
+            if h == 0:
+                combine(last - 1, 0)
         for h in range(2):
-            o = o_sb[(2 * last + h) % 4]
-            nc.vector.scalar_tensor_tensor(out=o[:], in0=z[1, h][last % 2][:], scalar=u_f32[:, 1:2], in1=zw[h][:], op0=MULT, op1=ADD)
-            nc.sync.dma_start(out=out_rows[last][:, h * BANK : (h + 1) * BANK], in_=o[:])
+            add_in_sbuf(last, h, zw[h][:])

@@ -29,14 +29,14 @@ SCALED_HALVES = 1
 def vector_blocks(g):
     return VB[g]
 
-VB = [4, 3, 3, 2, 3, 3, 2, 3, 2, 2, 3, 4]
-WS = {-1: 1536, 0: 1536, 1: 1024, 2: 832, 3: 832, 4: 1280, 5: 832, 6: 832, 7: 832}
-WG = {-1: 1856, 0: 1280, 1: 320, 2: 1472, 3: 320, 4: 1472, 5: 1472, 6: 320, 7: 1472, 8: 1280}
+VB = [4, 3, 3, 3, 3, 3, 3, 3, 3, 2, 3, 4]
+WS = {}
+WG = {-1: 1664, 0: 960, 1: 0, **{n: 1024 for n in range(2, 8)}}
 LEAD = {0: 1, 1: 3, **{n: 1 for n in range(2, 10)}}
 SPACE = {0: 2, 1: 2}
 TURNED_GROUPS = 10
 EARLY = 2
-SW = {10: 128}
+SW = {9: 128, 10: 128}
 
 
 def tile_pairwiseneuraltensorscorer_t_kernel(tc, e1_bytes, e1_scale, e2, w, v, b, u, out):
@@ -69,7 +69,7 @@ def tile_pairwiseneuraltensorscorer_t_kernel(tc, e1_bytes, e1_scale, e2, w, v, b
         (e2q_sc,) = tiles("e2q_sc", 1, [P, N2], U8)
         (ident,) = tiles("ident", 1, [P, P], F32)
         (diag,) = tiles("diag", 1, [P, P], F32)
-        e_woven = [wide[3]] + tiles("e_woven", 1, [P, ROW], BF16) * (GROUPS - 1)
+        e_woven = [wide[(g + 3) % GROUPS] for g in range(GROUPS)]
         eq = tiles("eq", 2, [P, GROUP], U32)
         eq_sc = tiles("eq_sc", 2, [P, GROUP], U8)
         planes = tiles("planes", 2, [P, PACK, T * GROUP], BF16)
@@ -290,10 +290,9 @@ def tile_pairwiseneuraltensorscorer_t_kernel(tc, e1_bytes, e1_scale, e2, w, v, b
                 quantize(e2q[:], e2q_sc[:], e2_woven[:])
             run(quantize_e, i + 1)
             run(quantize_h, i - 1)
-            run(weave_h, i)
-            if i >= -1:
-                widen(scalar_widen, max((i + 4) * ROW - widened[-1], WS.get(i, 0)))
+            widen(scalar_widen, max((i + 4) * ROW - widened[-1], 0))
             widen(nc.gpsimd.tensor_copy, WG.get(i, 0))
+            run(weave_h, i)
             if i == -1:
                 both(turn_e2, exit_e2)
             if i == 0:

@@ -29,12 +29,13 @@ SCALED_HALVES = 1
 def vector_blocks(g):
     return VB[g]
 
-VB = [4, 3, 3, 3, 3, 3, 3, 3, 3, 2, 3, 4]
+VB = [4, 4, 3, 3, 3, 3, 3, 3, 3, 2, 3, 4]
 WS = {}
-WG = {-1: 1664, 0: 960, 1: 0, **{n: 1024 for n in range(2, 8)}}
+WG = {-1: 1664, 0: 960, 1: 1088, **{n: 1088 for n in range(2, 8)}}
 LEAD = {0: 1, 1: 3, **{n: 1 for n in range(2, 10)}}
 SPACE = {0: 2, 1: 2}
 TURNED_GROUPS = 10
+FULL_END = 9
 EARLY = 2
 SW = {9: 128, 10: 128}
 
@@ -82,12 +83,15 @@ def tile_pairwiseneuraltensorscorer_t_kernel(tc, e1_bytes, e1_scale, e2, w, v, b
         banks = {"V": [ps.tile([P, BANK], F32, name=f"vbank{n}") for n in range(4)],
                  "S": [ps.tile([P, BANK], F32, name=f"sbank{n}") for n in range(4)]}
         held = {}
-        used = {"V": [], "S": []}
 
         def take(reader, key):
-            bank = banks[reader][len(used[reader]) % 4]
-            used[reader].append(key)
-            held[key] = bank
+            bank = banks[reader].pop(0)
+            held[key] = (reader, bank)
+            return bank
+
+        def give(key):
+            reader, bank = held.pop(key)
+            banks[reader].append(bank)
             return bank
 
         def load_w(s, h):
@@ -147,7 +151,7 @@ def tile_pairwiseneuraltensorscorer_t_kernel(tc, e1_bytes, e1_scale, e2, w, v, b
 
         def exit_e2():
             nc.scalar.copy(out=e2_woven[:].bitcast(F32).rearrange("p (n e) -> p n e", e=2),
-                           in_=held["e2"][:].rearrange("p (e n) -> p n e", e=2))
+                           in_=give("e2")[:].rearrange("p (e n) -> p n e", e=2))
 
         def turn_e(g, h):
             assert widened[-1] >= g * ROW + (h + 1) * 2 * D
@@ -156,7 +160,7 @@ def tile_pairwiseneuraltensorscorer_t_kernel(tc, e1_bytes, e1_scale, e2, w, v, b
         def exit_e(g, h):
             nc.vector.tensor_tensor(
                 out=e_woven[g][:, h * 2 * D : (h + 1) * 2 * D].rearrange("p (n a e) -> p n a e", a=2, e=2),
-                in0=held["e", g, h][:].bitcast(BF16).rearrange("p (a n e) -> p n a e", a=2, e=2),
+                in0=give(("e", g, h))[:].bitcast(BF16).rearrange("p (a n e) -> p n a e", a=2, e=2),
                 in1=scale_sb[:].rearrange("p (a e) -> p a e", e=2).unsqueeze(1).to_broadcast([P, HALF, 2, 2]), op=MULT)
 
         def quantize_e(g):
@@ -175,7 +179,7 @@ def tile_pairwiseneuraltensorscorer_t_kernel(tc, e1_bytes, e1_scale, e2, w, v, b
 
         def exit_v(g, c):
             nc.vector.tensor_tensor(out=h_woven[:, c * BANK : (c + 1) * BANK].rearrange("p (n t) -> p n t", t=PACK),
-                                    in0=held["hv", g, c][:].rearrange("p (t n) -> p n t", t=PACK),
+                                    in0=give(("hv", g, c))[:].rearrange("p (t n) -> p n t", t=PACK),
                                     in1=v_sb[:, c // PACK, :].unsqueeze(1).to_broadcast([P, P, PACK]), op=ADD)
 
         def scalar_banks(g):
@@ -197,9 +201,10 @@ def tile_pairwiseneuraltensorscorer_t_kernel(tc, e1_bytes, e1_scale, e2, w, v, b
                 left(bank[:, n * width : (n + 1) * width], g, s, t, slice(start, start + width))
 
         def exit_s(g, c):
+            bank = give(("hs", g, c))
             for n, (s, start, width, t) in enumerate(scalar_banks(g)[c]):
                 nc.scalar.activation(out=planes[g % 2][:, t, s * GROUP + start : s * GROUP + start + width],
-                                     in_=held["hs", g, c][:, n * width : (n + 1) * width], func=ACT.Identity,
+                                     in_=bank[:, n * width : (n + 1) * width], func=ACT.Identity,
                                      bias=v_sb[:, s, t : t + 1])
 
         def weave(copy, g, start, end):
@@ -234,7 +239,7 @@ def tile_pairwiseneuraltensorscorer_t_kernel(tc, e1_bytes, e1_scale, e2, w, v, b
                                     rhs=moving[:, rows].bitcast(FP8X4), rhs_scale=moving_sc[:, rows], start=True, stop=True)
 
         def tanh(g, s, h):
-            nc.scalar.activation(out=z[s, h][g % 2][:], in_=held["z", g, s, h][:], func=ACT.Tanh,
+            nc.scalar.activation(out=z[s, h][g % 2][:], in_=give(("z", g, s, h))[:], func=ACT.Tanh,
                                  bias=b_sb[:, s : s + 1], scale=D ** -0.5)
 
         def weigh(g, h):
@@ -255,9 +260,9 @@ def tile_pairwiseneuraltensorscorer_t_kernel(tc, e1_bytes, e1_scale, e2, w, v, b
         def combine(g, h):
             o = o_sb[2 * g + h]
             if turned(g, h):
-                nc.vector.scalar_tensor_tensor(out=o[:], in0=held["o", g, h][:], scalar=u_f32[:, 0:1], in1=zw[h][:], op0=MULT, op1=ADD)
+                nc.vector.scalar_tensor_tensor(out=o[:], in0=give(("o", g, h))[:], scalar=u_f32[:, 0:1], in1=zw[h][:], op0=MULT, op1=ADD)
             else:
-                nc.vector.scalar_tensor_tensor(out=o[:], in0=z[1, h][g % 2][:], scalar=u_f32[:, 1:2], in1=held["o", g, h][:], op0=MULT, op1=ADD)
+                nc.vector.scalar_tensor_tensor(out=o[:], in0=z[1, h][g % 2][:], scalar=u_f32[:, 1:2], in1=give(("o", g, h))[:], op0=MULT, op1=ADD)
             nc.sync.dma_start(out=out_rows[g][:, h * BANK : (h + 1) * BANK], in_=o[:])
 
         def run(f, g, *args):
@@ -299,6 +304,30 @@ def tile_pairwiseneuraltensorscorer_t_kernel(tc, e1_bytes, e1_scale, e2, w, v, b
                 nc.scalar.copy(out=u_f32[:], in_=u_sb[:])
             for h in range(2):
                 run(weigh, i - 2, h)
+            if 2 <= i < FULL_END:
+                exit_e(i + 2, 1)
+                exit_e(i + 2, 0)
+                for c in range(4):
+                    both(left_s, exit_s, i + 1, c)
+                both(right, tanh, i - 1, 0, 0)
+                both(left_v, exit_v, i, 0)
+                both(right, tanh, i - 1, 0, 1)
+                left_v(i, 1)
+                combine(i - 2, 1)
+                combine(i - 2, 0)
+                both(left_s, exit_s, i + 1, 4)
+                both(left_v, exit_v, i, 2)
+                exit_v(i, 1)
+                for c in range(5, len(scalar_banks(i + 1))):
+                    both(left_s, exit_s, i + 1, c)
+                for h in range(2):
+                    both(right, tanh, i - 1, 1, h)
+                for h in range(2):
+                    turn_e(i + 3, h)
+                if i + 1 < FULL_END:
+                    lift(i - 1, 0)
+                lift(i - 1, 1)
+                continue
             n_s = len(scalar_banks(i + 1)) if 0 <= i + 1 < GROUPS else 0
             n_v = vector_blocks(i) if 0 <= i < GROUPS else 0
             fills = [(left_s, exit_s, (i + 1, c)) for c in range(min(n_s, 4))]
@@ -340,6 +369,8 @@ def tile_pairwiseneuraltensorscorer_t_kernel(tc, e1_bytes, e1_scale, e2, w, v, b
                 nc.scalar.activation(out=diag[:], in_=ident[:], func=ACT.Copy, scale=u_f32[:, 0:1])
             for h in range(2):
                 run(turn_e, i + 3, h)
+            if i == 1:
+                lift(0, 0)
             if i < GROUPS - 3:
                 run(lift, i - 1, 1)
 

@@ -29,15 +29,17 @@ SCALED_HALVES = 1
 def vector_blocks(g):
     return VB[g]
 
-VB = [4, 4, 3, 3, 3, 3, 3, 3, 3, 2, 3, 4]
+VB = [4,4,3,3,3,3,3,3,3,2,3,4]
 WS = {}
-WG = {-1: 1664, 0: 960, 1: 1088, **{n: 1088 for n in range(2, 8)}}
+WG = {-1: 1664, 0: 960, 1: 1088, **{n: 1344 for n in range(2, 8)}}
 LEAD = {0: 1, 1: 3, **{n: 1 for n in range(2, 10)}}
 SPACE = {0: 2, 1: 2}
-TURNED_GROUPS = 10
+TURNED_GROUPS = 11
 FULL_END = 9
+AT = (5, 6, 7)
+HEAD_G = 1536
 EARLY = 2
-SW = {9: 128, 10: 128}
+SW = {}
 
 
 def tile_pairwiseneuraltensorscorer_t_kernel(tc, e1_bytes, e1_scale, e2, w, v, b, u, out):
@@ -55,7 +57,7 @@ def tile_pairwiseneuraltensorscorer_t_kernel(tc, e1_bytes, e1_scale, e2, w, v, b
 
         raw = tiles("raw", GROUPS, [P, ROW], U8)
         wide = tiles("wide", GROUPS, [P, ROW], BF16)
-        w_raw = [tiles(f"w_raw{s}_", 2, [P, PACK * HALF], BF16) for s in range(T)]
+        w_raw = tiles("w_raw", T, [P, ROW], BF16)
         w_woven = tiles("w_woven", T, [P, ROW], BF16)
         wq = tiles("wq", T, [P, D], U32)
         wq_sc = tiles("wq_sc", T, [P, D], U8)
@@ -78,7 +80,7 @@ def tile_pairwiseneuraltensorscorer_t_kernel(tc, e1_bytes, e1_scale, e2, w, v, b
         hqs = tiles("hq", 2, [P, T * GROUP], U32)
         hq_scs = tiles("hq_sc", 2, [P, T * GROUP], U8)
         z = {(s, h): tiles(f"z{s}{h}_", 2, [P, BANK], F32) for s in range(T) for h in range(2)}
-        zw = tiles("zw", 2, [P, BANK], F32)
+        zw = tiles("zw", 4, [P, BANK], F32)
         o_sb = tiles("o_sb", 2 * GROUPS, [P, BANK], F32)
         banks = {"V": [ps.tile([P, BANK], F32, name=f"vbank{n}") for n in range(4)],
                  "S": [ps.tile([P, BANK], F32, name=f"sbank{n}") for n in range(4)]}
@@ -94,17 +96,11 @@ def tile_pairwiseneuraltensorscorer_t_kernel(tc, e1_bytes, e1_scale, e2, w, v, b
             banks[reader].append(bank)
             return bank
 
-        def load_w(s, h):
-            nc.sync.dma_start(out=w_raw[s][h][:].rearrange("p (j c) -> p j c", j=PACK),
-                              in_=w[s].rearrange("(p j) c -> p j c", j=PACK)[:, :, h * HALF : (h + 1) * HALF])
-
         nc.sync.dma_start(out=raw[0][:], in_=e1_rows[0])
         nc.sync.dma_start(out=raw[1][:], in_=e1_rows[1])
-        load_w(1, 0)
+        nc.sync.dma_start(out=w_raw[1][:], in_=w[1].rearrange("(p j) c -> p (j c)", j=PACK))
         nc.sync.dma_start(out=scale_sb[:], in_=e1_scale.rearrange("o (p t) -> p (o t)", t=PACK))
-        load_w(1, 1)
-        load_w(0, 0)
-        load_w(0, 1)
+        nc.sync.dma_start(out=w_raw[0][:], in_=w[0].rearrange("(p j) c -> p (j c)", j=PACK))
         nc.sync.dma_start(out=raw[2][:], in_=e1_rows[2])
         for r in range(2):
             nc.sync.dma_start(out=e2_sb[r][:], in_=e2[r * P : (r + 1) * P, :])
@@ -135,7 +131,7 @@ def tile_pairwiseneuraltensorscorer_t_kernel(tc, e1_bytes, e1_scale, e2, w, v, b
         def weave_w(s, h, copy):
             part = slice(h * HALF // PACK, (h + 1) * HALF // PACK)
             copy(out=w_woven[s][:].rearrange("p (t m j) -> p t m j", t=PACK, j=PACK)[:, :, part],
-                 in_=w_raw[s][h][:].rearrange("p (j m t) -> p t m j", t=PACK, j=PACK))
+                 in_=w_raw[s][:].rearrange("p (j m t) -> p t m j", t=PACK, j=PACK)[:, :, part])
 
         def quantize(codes, scales, src):
             nc.vector.quantize_mx(out=codes.bitcast(FP8X4), scales=scales, in_=src)
@@ -244,7 +240,7 @@ def tile_pairwiseneuraltensorscorer_t_kernel(tc, e1_bytes, e1_scale, e2, w, v, b
 
         def weigh(g, h):
             if turned(g, h):
-                nc.scalar.activation(out=zw[h][:], in_=z[1, h][g % 2][:], func=ACT.Copy, scale=u_f32[:, 1:2])
+                nc.scalar.activation(out=zw[g % 2][:], in_=z[1, h][g % 2][:], func=ACT.Copy, scale=u_f32[:, 1:2])
 
         def lift(g, h):
             bank = take("V", ("o", g, h))
@@ -260,7 +256,7 @@ def tile_pairwiseneuraltensorscorer_t_kernel(tc, e1_bytes, e1_scale, e2, w, v, b
         def combine(g, h):
             o = o_sb[2 * g + h]
             if turned(g, h):
-                nc.vector.scalar_tensor_tensor(out=o[:], in0=give(("o", g, h))[:], scalar=u_f32[:, 0:1], in1=zw[h][:], op0=MULT, op1=ADD)
+                nc.vector.scalar_tensor_tensor(out=o[:], in0=give(("o", g, h))[:], scalar=u_f32[:, 0:1], in1=zw[g % 2][:], op0=MULT, op1=ADD)
             else:
                 nc.vector.scalar_tensor_tensor(out=o[:], in0=z[1, h][g % 2][:], scalar=u_f32[:, 1:2], in1=give(("o", g, h))[:], op0=MULT, op1=ADD)
             nc.sync.dma_start(out=out_rows[g][:, h * BANK : (h + 1) * BANK], in_=o[:])
@@ -277,15 +273,16 @@ def tile_pairwiseneuraltensorscorer_t_kernel(tc, e1_bytes, e1_scale, e2, w, v, b
         widen(scalar_widen, 1024)
         turn_e(0, 0)
         turn_e(0, 1)
-        widen(nc.gpsimd.tensor_copy, ROW)
+        widen(nc.gpsimd.tensor_copy, HEAD_G)
+        widen(scalar_widen, ROW - HEAD_G)
         weave_w(1, 0, nc.scalar.copy)
         weave_w(1, 1, nc.scalar.copy)
         exit_e(0, 0)
         exit_e(0, 1)
         turn_e(1, 0)
         turn_e(1, 1)
-        weave_w(0, 0, nc.scalar.copy)
         weave_w(0, 1, nc.gpsimd.tensor_copy)
+        weave_w(0, 0, nc.scalar.copy)
         quantize(wq[1][:], wq_sc[1][:], w_woven[1][:])
 
         for i in range(-1, GROUPS - 2):
@@ -295,11 +292,20 @@ def tile_pairwiseneuraltensorscorer_t_kernel(tc, e1_bytes, e1_scale, e2, w, v, b
                 quantize(e2q[:], e2q_sc[:], e2_woven[:])
             run(quantize_e, i + 1)
             run(quantize_h, i - 1)
-            widen(scalar_widen, max((i + 4) * ROW - widened[-1], 0))
+            widen(scalar_widen, max((i + 4) * ROW - widened[-1], WS.get(i, 0)))
             widen(nc.gpsimd.tensor_copy, WG.get(i, 0))
             run(weave_h, i)
             if i == -1:
+                for h in range(2):
+                    exit_e(1, h)
+                for c in range(3):
+                    both(left_s, exit_s, 0, c)
+                for h in range(2):
+                    turn_e(2, h)
                 both(turn_e2, exit_e2)
+                for c in range(3, len(scalar_banks(0))):
+                    both(left_s, exit_s, 0, c)
+                continue
             if i == 0:
                 nc.scalar.copy(out=u_f32[:], in_=u_sb[:])
             for h in range(2):
@@ -307,21 +313,21 @@ def tile_pairwiseneuraltensorscorer_t_kernel(tc, e1_bytes, e1_scale, e2, w, v, b
             if 2 <= i < FULL_END:
                 exit_e(i + 2, 1)
                 exit_e(i + 2, 0)
-                for c in range(4):
-                    both(left_s, exit_s, i + 1, c)
-                both(right, tanh, i - 1, 0, 0)
-                both(left_v, exit_v, i, 0)
-                both(right, tanh, i - 1, 0, 1)
-                left_v(i, 1)
-                combine(i - 2, 1)
-                combine(i - 2, 0)
-                both(left_s, exit_s, i + 1, 4)
-                both(left_v, exit_v, i, 2)
-                exit_v(i, 1)
-                for c in range(5, len(scalar_banks(i + 1))):
-                    both(left_s, exit_s, i + 1, c)
-                for h in range(2):
-                    both(right, tanh, i - 1, 1, h)
+                fills = [(left_s, exit_s, i + 1, c) for c in range(len(scalar_banks(i + 1)))]
+                fills[4:4] = [(right, tanh, i - 1, 0, h) for h in range(2)]
+                fills += [(right, tanh, i - 1, 1, h) for h in range(2)]
+                for n, f in enumerate(fills):
+                    if n == AT[0]:
+                        both(left_v, exit_v, i, 0)
+                    if n == AT[1]:
+                        left_v(i, 1)
+                        combine(i - 2, 1)
+                        combine(i - 2, 0)
+                    if n == AT[2]:
+                        for c in range(2, vector_blocks(i)):
+                            both(left_v, exit_v, i, c)
+                        exit_v(i, 1)
+                    both(*f)
                 for h in range(2):
                     turn_e(i + 3, h)
                 if i + 1 < FULL_END:
@@ -392,44 +398,32 @@ def tile_pairwiseneuraltensorscorer_t_kernel(tc, e1_bytes, e1_scale, e2, w, v, b
             both(left_s, exit_s, last, c)
         quantize_h(last - 1)
         weave_h(last)
-        both(right, tanh, last - 2, 0, 0)
-        both(left_v, exit_v, last, 0)
-        both(right, tanh, last - 2, 0, 1)
-        both(left_v, exit_v, last, 1)
-        both(right, tanh, last - 2, 1, 0)
-        both(left_v, exit_v, last, 2)
-        both(right, tanh, last - 2, 1, 1)
-        for c in range(3, vector_blocks(last)):
-            both(left_v, exit_v, last, c)
+        for c, (s, h) in enumerate(((0, 0), (0, 1), (1, 0), (1, 1))):
+            both(right, tanh, last - 2, s, h)
+            if c < vector_blocks(last):
+                both(left_v, exit_v, last, c)
         weave_hs(last)
-        both(lift, combine, last - 2, 0)
         weigh(last - 2, 1)
-        for s in range(T):
-            for h in range(2):
-                both(right, tanh, last - 1, s, h)
+        for h in range(2):
+            both(right, tanh, last - 1, 0, h)
+        both(lift, combine, last - 2, 0)
+        for h in range(2):
+            both(right, tanh, last - 1, 1, h)
         for s in range(T):
             cols = slice(s * GROUP, (s + 1) * GROUP)
             quantize(hqs[last % 2][:, cols], hq_scs[last % 2][:, cols], h_woven[:, s * ROW : (s + 1) * ROW])
+        lift(last - 1, 0)
         both(lift, combine, last - 2, 1)
-        spare = h_woven[:, ROW : ROW + 2 * BANK].bitcast(F32)
-        nc.gpsimd.tensor_scalar(out=spare, in0=z[0, 1][(last - 1) % 2][:], scalar1=u_f32[:, 0:1], scalar2=0.0, op0=MULT, op1=ADD)
+        combine(last - 1, 0)
+        weigh(last - 1, 1)
         for h in range(2):
             both(right, tanh, last, 0, h)
-        bank = take("V", ("o", last - 1, 0))
+        both(lift, combine, last - 1, 1)
         for h in range(2):
-            cols = slice(h * HALF, (h + 1) * HALF)
-            nc.tensor.matmul(out=bank[:, cols], lhsT=diag[:], rhs=z[0, 0][(last - 1) % 2][:, cols], start=True, stop=True)
             both(right, tanh, last, 1, h)
-
-        def add_in_sbuf(g, h, weighed):
-            o = o_sb[2 * g + h]
-            nc.vector.scalar_tensor_tensor(out=o[:], in0=z[1, h][g % 2][:], scalar=u_f32[:, 1:2], in1=weighed, op0=MULT, op1=ADD)
-            nc.sync.dma_start(out=out_rows[g][:, h * BANK : (h + 1) * BANK], in_=o[:])
-
-        add_in_sbuf(last - 1, 1, spare)
+        nc.gpsimd.tensor_scalar(out=zw[2][:], in0=z[0, 0][last % 2][:], scalar1=u_f32[:, 0:1], scalar2=0.0, op0=MULT, op1=ADD)
+        nc.vector.tensor_scalar(out=zw[3][:], in0=z[0, 1][last % 2][:], scalar1=u_f32[:, 0:1], scalar2=None, op0=MULT)
         for h in range(2):
-            nc.vector.tensor_scalar(out=zw[h][:], in0=z[0, h][last % 2][:], scalar1=u_f32[:, 0:1], scalar2=None, op0=MULT)
-            if h == 0:
-                combine(last - 1, 0)
-        for h in range(2):
-            add_in_sbuf(last, h, zw[h][:])
+            o = o_sb[2 * last + h]
+            nc.vector.scalar_tensor_tensor(out=o[:], in0=z[1, h][last % 2][:], scalar=u_f32[:, 1:2], in1=zw[2 + h][:], op0=MULT, op1=ADD)
+            nc.sync.dma_start(out=out_rows[last][:, h * BANK : (h + 1) * BANK], in_=o[:])

@@ -29,16 +29,18 @@ SCALED_HALVES = 1
 def vector_blocks(g):
     return VB[g]
 
-VB = [4,4,3,3,3,3,3,3,3,2,3,4]
+VB = [4,3,3,3,3,3,3,3,2,2,3,4]
 WS = {}
-WG = {-1: 1664, 0: 960, 1: 1088, **{n: 1344 for n in range(2, 8)}}
+WG = {-1: 1664, 0: 1280, 1: 256, **{n: 1088 for n in range(2, 8)}}
 LEAD = {0: 1, 1: 3, **{n: 1 for n in range(2, 10)}}
 SPACE = {0: 2, 1: 2}
 TURNED_GROUPS = 11
+TURNED_FROM = 8
 FULL_END = 9
-AT = (5, 6, 7)
-HEAD_G = 1536
-EARLY = 2
+AT = (4,6,7)
+EARLY_E = 0
+HEAD_G = 1024
+EARLY = 3
 SW = {}
 
 
@@ -97,9 +99,9 @@ def tile_pairwiseneuraltensorscorer_t_kernel(tc, e1_bytes, e1_scale, e2, w, v, b
             return bank
 
         nc.sync.dma_start(out=raw[0][:], in_=e1_rows[0])
-        nc.sync.dma_start(out=raw[1][:], in_=e1_rows[1])
         nc.sync.dma_start(out=w_raw[1][:], in_=w[1].rearrange("(p j) c -> p (j c)", j=PACK))
         nc.sync.dma_start(out=scale_sb[:], in_=e1_scale.rearrange("o (p t) -> p (o t)", t=PACK))
+        nc.sync.dma_start(out=raw[1][:], in_=e1_rows[1])
         nc.sync.dma_start(out=w_raw[0][:], in_=w[0].rearrange("(p j) c -> p (j c)", j=PACK))
         nc.sync.dma_start(out=raw[2][:], in_=e1_rows[2])
         for r in range(2):
@@ -218,7 +220,7 @@ def tile_pairwiseneuraltensorscorer_t_kernel(tc, e1_bytes, e1_scale, e2, w, v, b
             quantize(hqs[g % 2][:], hq_scs[g % 2][:], h_woven[:])
 
         def turned(g, h):
-            return h >= SCALED_HALVES and g < TURNED_GROUPS
+            return h >= SCALED_HALVES and TURNED_FROM <= g < TURNED_GROUPS
 
         def right(g, s, h):
             bank = take("S", ("z", g, s, h))
@@ -273,16 +275,18 @@ def tile_pairwiseneuraltensorscorer_t_kernel(tc, e1_bytes, e1_scale, e2, w, v, b
         widen(scalar_widen, 1024)
         turn_e(0, 0)
         turn_e(0, 1)
+        weave_w(1, 0, nc.vector.tensor_copy)
+        weave_w(1, 1, nc.scalar.copy)
         widen(nc.gpsimd.tensor_copy, HEAD_G)
         widen(scalar_widen, ROW - HEAD_G)
-        weave_w(1, 0, nc.scalar.copy)
-        weave_w(1, 1, nc.scalar.copy)
         exit_e(0, 0)
         exit_e(0, 1)
         turn_e(1, 0)
         turn_e(1, 1)
         weave_w(0, 1, nc.gpsimd.tensor_copy)
         weave_w(0, 0, nc.scalar.copy)
+        if EARLY_E:
+            exit_e(1, 0)
         quantize(wq[1][:], wq_sc[1][:], w_woven[1][:])
 
         for i in range(-1, GROUPS - 2):
@@ -296,7 +300,7 @@ def tile_pairwiseneuraltensorscorer_t_kernel(tc, e1_bytes, e1_scale, e2, w, v, b
             widen(nc.gpsimd.tensor_copy, WG.get(i, 0))
             run(weave_h, i)
             if i == -1:
-                for h in range(2):
+                for h in range(EARLY_E, 2):
                     exit_e(1, h)
                 for c in range(3):
                     both(left_s, exit_s, 0, c)
@@ -317,6 +321,8 @@ def tile_pairwiseneuraltensorscorer_t_kernel(tc, e1_bytes, e1_scale, e2, w, v, b
                 fills[4:4] = [(right, tanh, i - 1, 0, h) for h in range(2)]
                 fills += [(right, tanh, i - 1, 1, h) for h in range(2)]
                 for n, f in enumerate(fills):
+                    if n == EARLY and not turned(i - 2, 1):
+                        lift(i - 2, 1)
                     if n == AT[0]:
                         both(left_v, exit_v, i, 0)
                     if n == AT[1]:
@@ -332,7 +338,8 @@ def tile_pairwiseneuraltensorscorer_t_kernel(tc, e1_bytes, e1_scale, e2, w, v, b
                     turn_e(i + 3, h)
                 if i + 1 < FULL_END:
                     lift(i - 1, 0)
-                lift(i - 1, 1)
+                if turned(i - 1, 1) or i + 1 == FULL_END:
+                    lift(i - 1, 1)
                 continue
             n_s = len(scalar_banks(i + 1)) if 0 <= i + 1 < GROUPS else 0
             n_v = vector_blocks(i) if 0 <= i < GROUPS else 0
@@ -377,7 +384,7 @@ def tile_pairwiseneuraltensorscorer_t_kernel(tc, e1_bytes, e1_scale, e2, w, v, b
                 run(turn_e, i + 3, h)
             if i == 1:
                 lift(0, 0)
-            if i < GROUPS - 3:
+            if i < GROUPS - 3 and (i != 1 or turned(0, 1)):
                 run(lift, i - 1, 1)
 
         last = GROUPS - 1

@@ -18,30 +18,39 @@ ACT = mybir.ActivationFunctionType
 
 P = 128
 PACK = 4
-GROUP = 512
+GROUP = P * PACK
 GROUPS = N1 // GROUP
-HALF = 256
+LAST = GROUPS - 1
 ROW = PACK * D
 BANK = 512
-SCALED_HALVES = 1
+HALF = BANK // 2
+AHEAD = 3
+
+LONG = 1408
+SHORT = 256
 
 
 def vector_blocks(g):
-    return VB[g]
+    if g in (0, LAST):
+        return PACK
+    widening_over = g + AHEAD >= LAST
+    if g < LAST - 1 and (g % 3 == 0 or widening_over):
+        return 2
+    return 3
 
-VB = [4,3,3,3,3,3,3,3,2,2,3,4]
-WS = {}
-WG = {-1: 1664, 0: 1280, 1: 256, **{n: 1088 for n in range(2, 8)}}
-LEAD = {0: 1, 1: 3, **{n: 1 for n in range(2, 10)}}
-SPACE = {0: 2, 1: 2}
-TURNED_GROUPS = 11
-TURNED_FROM = 8
-FULL_END = 9
-AT = (4,6,7)
-EARLY_E = 0
-HEAD_G = 1024
-EARLY = 3
-SW = {}
+
+def gpsimd_columns(i):
+    return SHORT if i == 1 or vector_blocks(i) == 2 else LONG
+
+
+def scalar_banks(g):
+    found = []
+    for s, first in ((1, 0), (0, vector_blocks(g) * P)):
+        width = GROUP - first
+        if width > 0:
+            per_bank = BANK // width
+            found.extend([(s, first, width, t) for t in range(t0, t0 + per_bank)] for t0 in range(0, PACK, per_bank))
+    return found
 
 
 def tile_pairwiseneuraltensorscorer_t_kernel(tc, e1_bytes, e1_scale, e2, w, v, b, u, out):
@@ -73,46 +82,52 @@ def tile_pairwiseneuraltensorscorer_t_kernel(tc, e1_bytes, e1_scale, e2, w, v, b
         (e2q,) = tiles("e2q", 1, [P, N2], U32)
         (e2q_sc,) = tiles("e2q_sc", 1, [P, N2], U8)
         (ident,) = tiles("ident", 1, [P, P], F32)
-        (diag,) = tiles("diag", 1, [P, P], F32)
-        e_woven = [wide[(g + 3) % GROUPS] for g in range(GROUPS)]
+        (u0_ident,) = tiles("u0_ident", 1, [P, P], F32)
+        e_woven = [wide[(g + AHEAD) % GROUPS] for g in range(GROUPS)]
         eq = tiles("eq", 2, [P, GROUP], U32)
         eq_sc = tiles("eq_sc", 2, [P, GROUP], U8)
         planes = tiles("planes", 2, [P, PACK, T * GROUP], BF16)
         (h_woven,) = tiles("h_woven", 1, [P, T * ROW], BF16)
-        hqs = tiles("hq", 2, [P, T * GROUP], U32)
-        hq_scs = tiles("hq_sc", 2, [P, T * GROUP], U8)
+        hq = tiles("hq", 2, [P, T * GROUP], U32)
+        hq_sc = tiles("hq_sc", 2, [P, T * GROUP], U8)
         z = {(s, h): tiles(f"z{s}{h}_", 2, [P, BANK], F32) for s in range(T) for h in range(2)}
-        zw = tiles("zw", 4, [P, BANK], F32)
+        u0_z = tiles("u0_z", 3, [P, BANK], F32)
         o_sb = tiles("o_sb", 2 * GROUPS, [P, BANK], F32)
-        banks = {"V": [ps.tile([P, BANK], F32, name=f"vbank{n}") for n in range(4)],
-                 "S": [ps.tile([P, BANK], F32, name=f"sbank{n}") for n in range(4)]}
+
+        free = {"vector": [ps.tile([P, BANK], F32, name=f"vbank{n}") for n in range(4)],
+                "scalar": [ps.tile([P, BANK], F32, name=f"sbank{n}") for n in range(4)]}
         held = {}
 
         def take(reader, key):
-            bank = banks[reader].pop(0)
-            held[key] = (reader, bank)
-            return bank
+            held[key] = (reader, free[reader].pop(0))
+            return held[key][1]
 
         def give(key):
             reader, bank = held.pop(key)
-            banks[reader].append(bank)
+            free[reader].append(bank)
             return bank
 
-        nc.sync.dma_start(out=raw[0][:], in_=e1_rows[0])
-        nc.sync.dma_start(out=w_raw[1][:], in_=w[1].rearrange("(p j) c -> p (j c)", j=PACK))
+        def load_e1(g):
+            nc.sync.dma_start(out=raw[g][:], in_=e1_rows[g])
+
+        def load_w(s):
+            nc.sync.dma_start(out=w_raw[s][:], in_=w[s].rearrange("(p j) c -> p (j c)", j=PACK))
+
+        load_e1(0)
+        load_w(1)
         nc.sync.dma_start(out=scale_sb[:], in_=e1_scale.rearrange("o (p t) -> p (o t)", t=PACK))
-        nc.sync.dma_start(out=raw[1][:], in_=e1_rows[1])
-        nc.sync.dma_start(out=w_raw[0][:], in_=w[0].rearrange("(p j) c -> p (j c)", j=PACK))
-        nc.sync.dma_start(out=raw[2][:], in_=e1_rows[2])
+        load_e1(1)
+        load_w(0)
+        load_e1(2)
         for r in range(2):
             nc.sync.dma_start(out=e2_sb[r][:], in_=e2[r * P : (r + 1) * P, :])
-        nc.sync.dma_start(out=raw[3][:], in_=e1_rows[3])
+        load_e1(3)
         nc.sync.dma_start(out=v_sb[:], in_=v.rearrange("s (p t) -> p s t", t=PACK))
-        nc.sync.dma_start(out=raw[4][:], in_=e1_rows[4])
+        load_e1(4)
         nc.sync.dma_start(out=b_sb[:], in_=b.partition_broadcast(P))
         nc.sync.dma_start(out=u_sb[:], in_=u.partition_broadcast(P))
         for g in range(5, GROUPS):
-            nc.sync.dma_start(out=raw[g][:], in_=e1_rows[g])
+            load_e1(g)
         make_identity(nc, ident[:])
 
         widened = [0]
@@ -127,13 +142,13 @@ def tile_pairwiseneuraltensorscorer_t_kernel(tc, e1_bytes, e1_scale, e2, w, v, b
                 start = start + n
             widened.append(end)
 
-        def scalar_widen(out, in_):
+        def scalar_cast(out, in_):
             nc.scalar.activation(out=out, in_=in_, func=ACT.Copy)
 
-        def weave_w(s, h, copy):
-            part = slice(h * HALF // PACK, (h + 1) * HALF // PACK)
-            copy(out=w_woven[s][:].rearrange("p (t m j) -> p t m j", t=PACK, j=PACK)[:, :, part],
-                 in_=w_raw[s][:].rearrange("p (j m t) -> p t m j", t=PACK, j=PACK)[:, :, part])
+        def weave_w(s, h, copy, walk):
+            part = slice(h * P // 2, (h + 1) * P // 2)
+            copy(out=w_woven[s][:].rearrange("p (t m j) -> p m t j", t=PACK, j=PACK)[:, part].rearrange("p m t j -> " + walk),
+                 in_=w_raw[s][:].rearrange("p (j m t) -> p m t j", t=PACK, j=PACK)[:, part].rearrange("p m t j -> " + walk))
 
         def quantize(codes, scales, src):
             nc.vector.quantize_mx(out=codes.bitcast(FP8X4), scales=scales, in_=src)
@@ -141,296 +156,223 @@ def tile_pairwiseneuraltensorscorer_t_kernel(tc, e1_bytes, e1_scale, e2, w, v, b
         def turn_words(bank, rows):
             for j in range(2):
                 words = rows[j].bitcast(F32)
-                for e in range(2):
-                    nc.tensor.transpose(bank[:, e * HALF + j * P : e * HALF + (j + 1) * P], words[:, e : 2 * P : 2], ident[:])
+                for a in range(2):
+                    nc.tensor.transpose(bank[:, a * HALF + j * P : a * HALF + (j + 1) * P], words[:, a : 2 * P : 2], ident[:])
 
         def turn_e2():
-            turn_words(take("S", "e2"), [e2_sb[0][:], e2_sb[1][:]])
+            turn_words(take("scalar", "e2"), [e2_sb[0][:], e2_sb[1][:]])
 
-        def exit_e2():
-            nc.scalar.copy(out=e2_woven[:].bitcast(F32).rearrange("p (n e) -> p n e", e=2),
-                           in_=give("e2")[:].rearrange("p (e n) -> p n e", e=2))
+        def read_e2():
+            nc.scalar.copy(out=e2_woven[:].bitcast(F32).rearrange("p (n a) -> p n a", a=2),
+                           in_=give("e2")[:].rearrange("p (a n) -> p n a", a=2))
 
         def turn_e(g, h):
             assert widened[-1] >= g * ROW + (h + 1) * 2 * D
-            turn_words(take("V", ("e", g, h)), [wide[g][:, (2 * h + j) * D : (2 * h + j + 1) * D] for j in range(2)])
+            turn_words(take("vector", ("e", g, h)), [wide[g][:, (2 * h + j) * D : (2 * h + j + 1) * D] for j in range(2)])
 
-        def exit_e(g, h):
+        def read_e(g, h):
             nc.vector.tensor_tensor(
-                out=e_woven[g][:, h * 2 * D : (h + 1) * 2 * D].rearrange("p (n a e) -> p n a e", a=2, e=2),
-                in0=give(("e", g, h))[:].bitcast(BF16).rearrange("p (a n e) -> p n a e", a=2, e=2),
-                in1=scale_sb[:].rearrange("p (a e) -> p a e", e=2).unsqueeze(1).to_broadcast([P, HALF, 2, 2]), op=MULT)
+                out=e_woven[g][:, h * 2 * D : (h + 1) * 2 * D].rearrange("p (n a i) -> p n a i", a=2, i=2),
+                in0=give(("e", g, h))[:].bitcast(BF16).rearrange("p (a n i) -> p n a i", a=2, i=2),
+                in1=scale_sb[:].rearrange("p (a i) -> p a i", i=2).unsqueeze(1).to_broadcast([P, HALF, 2, 2]), op=MULT)
 
         def quantize_e(g):
             quantize(eq[g % 2][:], eq_sc[g % 2][:], e_woven[g][:])
 
-        def left(out, g, s, t, cols):
-            rows = slice(t * P, (t + 1) * P)
-            nc.tensor.matmul_mx(out=out, lhsT=wq[s][:, rows].bitcast(FP8X4), lhsT_scale=wq_sc[s][:, rows],
+        def plane(dst, g, s, t, cols):
+            fixed = slice(t * P, (t + 1) * P)
+            nc.tensor.matmul_mx(out=dst, lhsT=wq[s][:, fixed].bitcast(FP8X4), lhsT_scale=wq_sc[s][:, fixed],
                                 rhs=eq[g % 2][:, cols].bitcast(FP8X4), rhs_scale=eq_sc[g % 2][:, cols], start=True, stop=True)
 
-        def left_v(g, c):
-            s, j = divmod(c, PACK)
-            bank = take("V", ("hv", g, c))
+        def fill_block(g, c):
+            bank = take("vector", ("block", g, c))
             for t in range(PACK):
-                left(bank[:, t * P : (t + 1) * P], g, s, t, slice(j * P, (j + 1) * P))
+                plane(bank[:, t * P : (t + 1) * P], g, 0, t, slice(c * P, (c + 1) * P))
 
-        def exit_v(g, c):
+        def read_block(g, c):
             nc.vector.tensor_tensor(out=h_woven[:, c * BANK : (c + 1) * BANK].rearrange("p (n t) -> p n t", t=PACK),
-                                    in0=give(("hv", g, c))[:].rearrange("p (t n) -> p n t", t=PACK),
-                                    in1=v_sb[:, c // PACK, :].unsqueeze(1).to_broadcast([P, P, PACK]), op=ADD)
+                                    in0=give(("block", g, c))[:].rearrange("p (t n) -> p n t", t=PACK),
+                                    in1=v_sb[:, 0, :].unsqueeze(1).to_broadcast([P, P, PACK]), op=ADD)
 
-        def scalar_banks(g):
-            found = []
-            for s in (1, 0):
-                start = min(max(vector_blocks(g) * P - s * GROUP, 0), GROUP)
-                end = GROUP
-                while end > start:
-                    width = GROUP if end - start == GROUP else HALF if end - start >= HALF else P
-                    per_bank = BANK // width
-                    for first in range(0, PACK, per_bank):
-                        found.append([(s, end - width, width, t) for t in range(first, first + per_bank)])
-                    end = end - width
-            return found
+        def fill_planes(g, c):
+            bank = take("scalar", ("planes", g, c))
+            for n, (s, first, width, t) in enumerate(scalar_banks(g)[c]):
+                plane(bank[:, n * width : (n + 1) * width], g, s, t, slice(first, first + width))
 
-        def left_s(g, c):
-            bank = take("S", ("hs", g, c))
-            for n, (s, start, width, t) in enumerate(scalar_banks(g)[c]):
-                left(bank[:, n * width : (n + 1) * width], g, s, t, slice(start, start + width))
+        def read_planes(g, c):
+            bank = give(("planes", g, c))
+            for n, (s, first, width, t) in enumerate(scalar_banks(g)[c]):
+                nc.scalar.activation(out=planes[g % 2][:, t, s * GROUP + first : s * GROUP + first + width],
+                                     in_=bank[:, n * width : (n + 1) * width], func=ACT.Identity, bias=v_sb[:, s, t : t + 1])
 
-        def exit_s(g, c):
-            bank = give(("hs", g, c))
-            for n, (s, start, width, t) in enumerate(scalar_banks(g)[c]):
-                nc.scalar.activation(out=planes[g % 2][:, t, s * GROUP + start : s * GROUP + start + width],
-                                     in_=bank[:, n * width : (n + 1) * width], func=ACT.Identity,
-                                     bias=v_sb[:, s, t : t + 1])
-
-        def weave(copy, g, start, end):
-            if end > start:
-                copy(out=h_woven[:, start * PACK : end * PACK].rearrange("p (n t) -> p n t", t=PACK),
-                     in_=planes[g % 2][:, :, start:end].rearrange("p t n -> p n t"))
-
-        def weave_h(g):
-            weave(nc.gpsimd.tensor_copy, g, vector_blocks(g) * P + SW.get(g, 0), T * GROUP)
-
-        def weave_hs(g):
-            weave(nc.scalar.copy, g, vector_blocks(g) * P, vector_blocks(g) * P + SW.get(g, 0))
+        def weave_h(g, copy, first, end):
+            copy(out=h_woven[:, first * PACK : end * PACK].rearrange("p (n t) -> p n t", t=PACK),
+                 in_=planes[g % 2][:, :, first:end].rearrange("p t n -> p n t"))
 
         def quantize_h(g):
-            quantize(hqs[g % 2][:], hq_scs[g % 2][:], h_woven[:])
+            quantize(hq[g % 2][:], hq_sc[g % 2][:], h_woven[:])
 
-        def turned(g, h):
-            return h >= SCALED_HALVES and TURNED_FROM <= g < TURNED_GROUPS
-
-        def right(g, s, h):
-            bank = take("S", ("z", g, s, h))
-            hq, hq_sc = hqs[g % 2], hq_scs[g % 2]
+        def fill_scores(g, s, h):
+            bank = take("scalar", ("scores", g, s, h))
             for j in range(2):
-                if s == 0 and turned(g, h):
-                    fixed, fixed_sc, cols = e2q, e2q_sc, slice(j * P, (j + 1) * P)
-                    moving, moving_sc, rows = hq, hq_sc, slice(h * HALF, (h + 1) * HALF)
-                else:
-                    first = s * GROUP + (2 * h + j) * P
-                    fixed, fixed_sc, cols = hq, hq_sc, slice(first, first + P)
-                    moving, moving_sc, rows = e2q, e2q_sc, slice(0, N2)
-                nc.tensor.matmul_mx(out=bank[:, j * HALF : (j + 1) * HALF], lhsT=fixed[:, cols].bitcast(FP8X4), lhsT_scale=fixed_sc[:, cols],
-                                    rhs=moving[:, rows].bitcast(FP8X4), rhs_scale=moving_sc[:, rows], start=True, stop=True)
+                fixed = slice(s * GROUP + (2 * h + j) * P, s * GROUP + (2 * h + j + 1) * P)
+                nc.tensor.matmul_mx(out=bank[:, j * N2 : (j + 1) * N2], lhsT=hq[g % 2][:, fixed].bitcast(FP8X4),
+                                    lhsT_scale=hq_sc[g % 2][:, fixed], rhs=e2q[:].bitcast(FP8X4), rhs_scale=e2q_sc[:],
+                                    start=True, stop=True)
 
-        def tanh(g, s, h):
-            nc.scalar.activation(out=z[s, h][g % 2][:], in_=give(("z", g, s, h))[:], func=ACT.Tanh,
+        def read_scores(g, s, h):
+            nc.scalar.activation(out=z[s, h][g % 2][:], in_=give(("scores", g, s, h))[:], func=ACT.Tanh,
                                  bias=b_sb[:, s : s + 1], scale=D ** -0.5)
 
-        def weigh(g, h):
-            if turned(g, h):
-                nc.scalar.activation(out=zw[g % 2][:], in_=z[1, h][g % 2][:], func=ACT.Copy, scale=u_f32[:, 1:2])
+        def fill_sum(g, h):
+            nc.tensor.matmul(out=take("vector", ("sum", g, h))[:], lhsT=u0_ident[:], rhs=z[0, h][g % 2][:], start=True, stop=True)
 
-        def lift(g, h):
-            bank = take("V", ("o", g, h))
-            src = z[0, h][g % 2]
-            if turned(g, h):
-                for j in range(2):
-                    for c in range(2):
-                        nc.tensor.transpose(bank[:, j * N2 + c * P : j * N2 + (c + 1) * P],
-                                            src[:, c * HALF + j * P : c * HALF + (j + 1) * P], ident[:])
-            else:
-                nc.tensor.matmul(out=bank[:], lhsT=diag[:], rhs=src[:], start=True, stop=True)
-
-        def combine(g, h):
+        def add_slices(g, h, weighed):
             o = o_sb[2 * g + h]
-            if turned(g, h):
-                nc.vector.scalar_tensor_tensor(out=o[:], in0=give(("o", g, h))[:], scalar=u_f32[:, 0:1], in1=zw[g % 2][:], op0=MULT, op1=ADD)
-            else:
-                nc.vector.scalar_tensor_tensor(out=o[:], in0=z[1, h][g % 2][:], scalar=u_f32[:, 1:2], in1=give(("o", g, h))[:], op0=MULT, op1=ADD)
+            nc.vector.scalar_tensor_tensor(out=o[:], in0=z[1, h][g % 2][:], scalar=u_f32[:, 1:2], in1=weighed[:], op0=MULT, op1=ADD)
             nc.sync.dma_start(out=out_rows[g][:, h * BANK : (h + 1) * BANK], in_=o[:])
 
-        def run(f, g, *args):
-            if 0 <= g < GROUPS:
-                f(g, *args)
+        def read_sum(g, h):
+            add_slices(g, h, give(("sum", g, h)))
 
-        def both(fill, drain, *a):
-            fill(*a)
-            drain(*a)
+        def block(g, c):
+            fill_block(g, c)
+            read_block(g, c)
 
-        widen(nc.vector.tensor_copy, 1024)
-        widen(scalar_widen, 1024)
-        turn_e(0, 0)
-        turn_e(0, 1)
-        weave_w(1, 0, nc.vector.tensor_copy)
-        weave_w(1, 1, nc.scalar.copy)
-        widen(nc.gpsimd.tensor_copy, HEAD_G)
-        widen(scalar_widen, ROW - HEAD_G)
-        exit_e(0, 0)
-        exit_e(0, 1)
-        turn_e(1, 0)
-        turn_e(1, 1)
-        weave_w(0, 1, nc.gpsimd.tensor_copy)
-        weave_w(0, 0, nc.scalar.copy)
-        if EARLY_E:
-            exit_e(1, 0)
+        def planes_bank(g, c):
+            fill_planes(g, c)
+            read_planes(g, c)
+
+        def scores(g, s, h):
+            fill_scores(g, s, h)
+            read_scores(g, s, h)
+
+        widen(nc.vector.tensor_copy, ROW // 2)
+        widen(scalar_cast, ROW // 2)
+        for h in range(2):
+            turn_e(0, h)
+        weave_w(1, 0, nc.vector.tensor_copy, "p t m j")
+        weave_w(1, 1, nc.scalar.copy, "p m j t")
+        widen(nc.gpsimd.tensor_copy, LONG)
+        widen(scalar_cast, ROW - LONG)
+        for h in range(2):
+            read_e(0, h)
+        for h in range(2):
+            turn_e(1, h)
+        weave_w(0, 0, nc.gpsimd.tensor_copy, "p t m j")
+        weave_w(0, 1, nc.scalar.copy, "p m j t")
         quantize(wq[1][:], wq_sc[1][:], w_woven[1][:])
+        quantize_e(0)
+        widen(scalar_cast, ROW)
+        widen(nc.gpsimd.tensor_copy, LONG)
+        for h in range(2):
+            read_e(1, h)
+        for c in range(PACK - 1):
+            planes_bank(0, c)
+        for h in range(2):
+            turn_e(2, h)
+        turn_e2()
+        read_e2()
+        planes_bank(0, PACK - 1)
+        quantize(wq[0][:], wq_sc[0][:], w_woven[0][:])
 
-        for i in range(-1, GROUPS - 2):
-            if i == 0:
-                quantize(wq[0][:], wq_sc[0][:], w_woven[0][:])
+        for i in range(LAST - 1):
             if i == 1:
                 quantize(e2q[:], e2q_sc[:], e2_woven[:])
-            run(quantize_e, i + 1)
-            run(quantize_h, i - 1)
-            widen(scalar_widen, max((i + 4) * ROW - widened[-1], WS.get(i, 0)))
-            widen(nc.gpsimd.tensor_copy, WG.get(i, 0))
-            run(weave_h, i)
-            if i == -1:
-                for h in range(EARLY_E, 2):
-                    exit_e(1, h)
-                for c in range(3):
-                    both(left_s, exit_s, 0, c)
-                for h in range(2):
-                    turn_e(2, h)
-                both(turn_e2, exit_e2)
-                for c in range(3, len(scalar_banks(0))):
-                    both(left_s, exit_s, 0, c)
-                continue
+            quantize_e(i + 1)
+            if i >= 1:
+                quantize_h(i - 1)
+            widen(scalar_cast, max((i + AHEAD + 1) * ROW - widened[-1], ROW // 2 if i >= 1 else 0))
+            widen(nc.gpsimd.tensor_copy, gpsimd_columns(i))
+            weave_h(i, nc.gpsimd.tensor_copy, vector_blocks(i) * P, T * GROUP)
             if i == 0:
                 nc.scalar.copy(out=u_f32[:], in_=u_sb[:])
-            for h in range(2):
-                run(weigh, i - 2, h)
-            if 2 <= i < FULL_END:
-                exit_e(i + 2, 1)
-                exit_e(i + 2, 0)
-                fills = [(left_s, exit_s, i + 1, c) for c in range(len(scalar_banks(i + 1)))]
-                fills[4:4] = [(right, tanh, i - 1, 0, h) for h in range(2)]
-                fills += [(right, tanh, i - 1, 1, h) for h in range(2)]
-                for n, f in enumerate(fills):
-                    if n == EARLY and not turned(i - 2, 1):
-                        lift(i - 2, 1)
-                    if n == AT[0]:
-                        both(left_v, exit_v, i, 0)
-                    if n == AT[1]:
-                        left_v(i, 1)
-                        combine(i - 2, 1)
-                        combine(i - 2, 0)
-                    if n == AT[2]:
-                        for c in range(2, vector_blocks(i)):
-                            both(left_v, exit_v, i, c)
-                        exit_v(i, 1)
-                    both(*f)
-                for h in range(2):
-                    turn_e(i + 3, h)
-                if i + 1 < FULL_END:
-                    lift(i - 1, 0)
-                if turned(i - 1, 1) or i + 1 == FULL_END:
-                    lift(i - 1, 1)
-                continue
-            n_s = len(scalar_banks(i + 1)) if 0 <= i + 1 < GROUPS else 0
-            n_v = vector_blocks(i) if 0 <= i < GROUPS else 0
-            fills = [(left_s, exit_s, (i + 1, c)) for c in range(min(n_s, 4))]
-            if 0 <= i - 1 < GROUPS:
-                fills += [(right, tanh, (i - 1, 0, h)) for h in range(2)]
-            fills += [(left_s, exit_s, (i + 1, c)) for c in range(4, n_s)]
-            if 0 <= i - 1 < GROUPS:
-                fills += [(right, tanh, (i - 1, 1, h)) for h in range(2)]
-            reads = [(exit_e, (i + 2, h)) for h in range(2) if 0 <= i + 2 < GROUPS]
-            reads += [(combine, (i - 2, 1))] if 0 <= i - 2 < GROUPS else []
-            for f, a in reads:
-                f(*a)
-            if 0 <= i - 2 < GROUPS:
-                for fill, drain, a in fills[:EARLY]:
-                    fill(*a)
-                    drain(*a)
-                fills = fills[EARLY:]
-                lift(i - 2, 0)
-                combine(i - 2, 0)
-                reads.append(None)
-            done_v = min(4 - len(reads), n_v)
-            for c in range(done_v):
-                left_v(i, c)
-                exit_v(i, c)
-            lead = LEAD.get(i, 3)
-            for n, (fill, drain, a) in enumerate(fills):
-                fill(*a)
-                drain(*a)
-                if n == 1:
-                    run(weave_hs, i)
-                if n >= lead and (n - lead) % SPACE.get(i, 1) == 0 and done_v < n_v:
-                    left_v(i, done_v)
-                    exit_v(i, done_v)
-                    done_v = done_v + 1
-            for c in range(done_v, n_v):
-                left_v(i, c)
-                exit_v(i, c)
+            for h in (0, 1) if i == 0 else (1, 0):
+                read_e(i + 2, h)
+            slice0_banks = list(range(PACK, len(scalar_banks(i + 1))))
             if i == 0:
-                nc.scalar.activation(out=diag[:], in_=ident[:], func=ACT.Copy, scale=u_f32[:, 0:1])
-            for h in range(2):
-                run(turn_e, i + 3, h)
-            if i == 1:
-                lift(0, 0)
-            if i < GROUPS - 3 and (i != 1 or turned(0, 1)):
-                run(lift, i - 1, 1)
+                for c in range(2):
+                    block(i, c)
+                for c in range(PACK):
+                    planes_bank(i + 1, c)
+                    if c >= 2:
+                        block(i, c)
+            elif i == 1:
+                for c in range(2):
+                    block(i, c)
+                for c in range(PACK):
+                    planes_bank(i + 1, c)
+                scores(i - 1, 0, 0)
+                block(i, 2)
+                scores(i - 1, 0, 1)
+            else:
+                for c in range(PACK):
+                    if c == PACK - 1:
+                        fill_sum(i - 2, 1)
+                    planes_bank(i + 1, c)
+                block(i, 0)
+                for h in range(2):
+                    scores(i - 1, 0, h)
+                fill_block(i, 1)
+                for h in (1, 0):
+                    read_sum(i - 2, h)
+                planes_bank(i + 1, slice0_banks.pop(0))
+                for c in range(2, vector_blocks(i)):
+                    block(i, c)
+                read_block(i, 1)
+            for c in slice0_banks:
+                planes_bank(i + 1, c)
+            if i == 0:
+                nc.scalar.activation(out=u0_ident[:], in_=ident[:], func=ACT.Copy, scale=u_f32[:, 0:1])
+            else:
+                for h in range(2):
+                    scores(i - 1, 1, h)
+            for n in range(2):
+                if i + AHEAD <= LAST:
+                    turn_e(i + AHEAD, n)
+                else:
+                    fill_block(i + 1, n)
+            if i >= 1:
+                fill_sum(i - 1, 0)
 
-        last = GROUPS - 1
-        quantize_e(last)
-        quantize_h(last - 2)
-        weave_h(last - 1)
-        both(left_v, exit_v, last - 1, 0)
-        both(left_v, exit_v, last - 1, 1)
-        weigh(last - 3, 1)
-        both(lift, combine, last - 3, 1)
-        both(left_s, exit_s, last, 0)
-        both(left_s, exit_s, last, 1)
-        both(lift, combine, last - 3, 0)
-        weave_hs(last - 1)
-        for c in range(2, vector_blocks(last - 1)):
-            both(left_v, exit_v, last - 1, c)
-        for c in range(2, len(scalar_banks(last))):
-            both(left_s, exit_s, last, c)
-        quantize_h(last - 1)
-        weave_h(last)
-        for c, (s, h) in enumerate(((0, 0), (0, 1), (1, 0), (1, 1))):
-            both(right, tanh, last - 2, s, h)
-            if c < vector_blocks(last):
-                both(left_v, exit_v, last, c)
-        weave_hs(last)
-        weigh(last - 2, 1)
-        for h in range(2):
-            both(right, tanh, last - 1, 0, h)
-        both(lift, combine, last - 2, 0)
-        for h in range(2):
-            both(right, tanh, last - 1, 1, h)
+        quantize_e(LAST)
+        quantize_h(LAST - 2)
+        weave_h(LAST - 1, nc.gpsimd.tensor_copy, GROUP, T * GROUP)
+        for c in range(2):
+            read_block(LAST - 1, c)
+            planes_bank(LAST, c)
+        weave_h(LAST - 1, nc.scalar.copy, vector_blocks(LAST - 1) * P, GROUP)
+        read_sum(LAST - 3, 0)
+        fill_sum(LAST - 3, 1)
+        read_sum(LAST - 3, 1)
+        block(LAST - 1, 2)
+        for c in range(2, PACK):
+            planes_bank(LAST, c)
+
+        quantize_h(LAST - 1)
+        weave_h(LAST, nc.gpsimd.tensor_copy, GROUP, T * GROUP)
+        for c in range(PACK):
+            scores(LAST - 2, *divmod(c, 2))
+            block(LAST, c)
+        for s in range(T):
+            for h in range(2):
+                scores(LAST - 1, s, h)
+            fill_sum(LAST - 2, s)
+            if s == 0:
+                read_sum(LAST - 2, 0)
         for s in range(T):
             cols = slice(s * GROUP, (s + 1) * GROUP)
-            quantize(hqs[last % 2][:, cols], hq_scs[last % 2][:, cols], h_woven[:, s * ROW : (s + 1) * ROW])
-        lift(last - 1, 0)
-        both(lift, combine, last - 2, 1)
-        combine(last - 1, 0)
-        weigh(last - 1, 1)
+            quantize(hq[LAST % 2][:, cols], hq_sc[LAST % 2][:, cols], h_woven[:, s * ROW : (s + 1) * ROW])
+        nc.scalar.activation(out=u0_z[2][:], in_=z[0, 1][(LAST - 1) % 2][:], func=ACT.Copy, scale=u_f32[:, 0:1])
+        add_slices(LAST - 1, 1, u0_z[2])
+        read_sum(LAST - 2, 1)
         for h in range(2):
-            both(right, tanh, last, 0, h)
-        both(lift, combine, last - 1, 1)
+            scores(LAST, 0, h)
+        fill_sum(LAST - 1, 0)
+        read_sum(LAST - 1, 0)
         for h in range(2):
-            both(right, tanh, last, 1, h)
-        nc.gpsimd.tensor_scalar(out=zw[2][:], in0=z[0, 0][last % 2][:], scalar1=u_f32[:, 0:1], scalar2=0.0, op0=MULT, op1=ADD)
-        nc.vector.tensor_scalar(out=zw[3][:], in0=z[0, 1][last % 2][:], scalar1=u_f32[:, 0:1], scalar2=None, op0=MULT)
+            scores(LAST, 1, h)
+        nc.gpsimd.tensor_scalar(out=u0_z[0][:], in0=z[0, 0][LAST % 2][:], scalar1=u_f32[:, 0:1], scalar2=0.0, op0=MULT, op1=ADD)
+        nc.vector.tensor_scalar(out=u0_z[1][:], in0=z[0, 1][LAST % 2][:], scalar1=u_f32[:, 0:1], scalar2=None, op0=MULT)
         for h in range(2):
-            o = o_sb[2 * last + h]
-            nc.vector.scalar_tensor_tensor(out=o[:], in0=z[1, h][last % 2][:], scalar=u_f32[:, 1:2], in1=zw[2 + h][:], op0=MULT, op1=ADD)
-            nc.sync.dma_start(out=out_rows[last][:, h * BANK : (h + 1) * BANK], in_=o[:])
+            add_slices(LAST, h, u0_z[h])

@@ -26,17 +26,18 @@ BANK = 512
 HALF = BANK // 2
 AHEAD = 3
 
-LONG = 1408
+LONG = 1344
 SHORT = 256
+HEAD = 1664
+SCALAR_LEAST = 896
+MIDDLE = 5
+NO_WIDENING = LAST - AHEAD
 
 
 def vector_blocks(g):
     if g in (0, LAST):
         return PACK
-    widening_over = g + AHEAD >= LAST
-    if g < LAST - 1 and (g % 3 == 0 or widening_over):
-        return 2
-    return 3
+    return 2 if g == MIDDLE or NO_WIDENING <= g < LAST - 1 else 3
 
 
 def gpsimd_columns(i):
@@ -91,7 +92,7 @@ def tile_pairwiseneuraltensorscorer_t_kernel(tc, e1_bytes, e1_scale, e2, w, v, b
         hq = tiles("hq", 2, [P, T * GROUP], U32)
         hq_sc = tiles("hq_sc", 2, [P, T * GROUP], U8)
         z = {(s, h): tiles(f"z{s}{h}_", 2, [P, BANK], F32) for s in range(T) for h in range(2)}
-        u0_z = tiles("u0_z", 3, [P, BANK], F32)
+        u0_z = tiles("u0_z", 4, [P, BANK], F32)
         o_sb = tiles("o_sb", 2 * GROUPS, [P, BANK], F32)
 
         free = {"vector": [ps.tile([P, BANK], F32, name=f"vbank{n}") for n in range(4)],
@@ -145,10 +146,9 @@ def tile_pairwiseneuraltensorscorer_t_kernel(tc, e1_bytes, e1_scale, e2, w, v, b
         def scalar_cast(out, in_):
             nc.scalar.activation(out=out, in_=in_, func=ACT.Copy)
 
-        def weave_w(s, h, copy, walk):
-            part = slice(h * P // 2, (h + 1) * P // 2)
-            copy(out=w_woven[s][:].rearrange("p (t m j) -> p m t j", t=PACK, j=PACK)[:, part].rearrange("p m t j -> " + walk),
-                 in_=w_raw[s][:].rearrange("p (j m t) -> p m t j", t=PACK, j=PACK)[:, part].rearrange("p m t j -> " + walk))
+        def weave_w(s, copy, part):
+            copy(out=w_woven[s][:].rearrange("p (t m j) -> p t m j", t=PACK, j=PACK)[:, :, part],
+                 in_=w_raw[s][:].rearrange("p (j m t) -> p t m j", t=PACK, j=PACK)[:, :, part])
 
         def quantize(codes, scales, src):
             nc.vector.quantize_mx(out=codes.bitcast(FP8X4), scales=scales, in_=src)
@@ -235,6 +235,9 @@ def tile_pairwiseneuraltensorscorer_t_kernel(tc, e1_bytes, e1_scale, e2, w, v, b
         def read_sum(g, h):
             add_slices(g, h, give(("sum", g, h)))
 
+        def weigh(g):
+            nc.scalar.activation(out=u0_z[g % 2][:], in_=z[0, 1][g % 2][:], func=ACT.Copy, scale=u_f32[:, 0:1])
+
         def block(g, c):
             fill_block(g, c)
             read_block(g, c)
@@ -251,20 +254,19 @@ def tile_pairwiseneuraltensorscorer_t_kernel(tc, e1_bytes, e1_scale, e2, w, v, b
         widen(scalar_cast, ROW // 2)
         for h in range(2):
             turn_e(0, h)
-        weave_w(1, 0, nc.vector.tensor_copy, "p t m j")
-        weave_w(1, 1, nc.scalar.copy, "p m j t")
-        widen(nc.gpsimd.tensor_copy, LONG)
-        widen(scalar_cast, ROW - LONG)
+        weave_w(1, nc.vector.tensor_copy, slice(0, P))
+        widen(nc.gpsimd.tensor_copy, ROW // 4)
+        widen(scalar_cast, ROW - ROW // 4)
         for h in range(2):
             read_e(0, h)
         for h in range(2):
             turn_e(1, h)
-        weave_w(0, 0, nc.gpsimd.tensor_copy, "p t m j")
-        weave_w(0, 1, nc.scalar.copy, "p m j t")
+        weave_w(0, nc.gpsimd.tensor_copy, slice(0, P // 2))
+        weave_w(0, nc.scalar.copy, slice(P // 2, P))
         quantize(wq[1][:], wq_sc[1][:], w_woven[1][:])
         quantize_e(0)
         widen(scalar_cast, ROW)
-        widen(nc.gpsimd.tensor_copy, LONG)
+        widen(nc.gpsimd.tensor_copy, HEAD)
         for h in range(2):
             read_e(1, h)
         for c in range(PACK - 1):
@@ -282,9 +284,12 @@ def tile_pairwiseneuraltensorscorer_t_kernel(tc, e1_bytes, e1_scale, e2, w, v, b
             quantize_e(i + 1)
             if i >= 1:
                 quantize_h(i - 1)
-            widen(scalar_cast, max((i + AHEAD + 1) * ROW - widened[-1], ROW // 2 if i >= 1 else 0))
+            widen(scalar_cast, max((i + AHEAD + 1) * ROW - widened[-1], SCALAR_LEAST if i >= 1 else 0))
             widen(nc.gpsimd.tensor_copy, gpsimd_columns(i))
+            assert widened[-1] <= (i + AHEAD + 2) * ROW
             weave_h(i, nc.gpsimd.tensor_copy, vector_blocks(i) * P, T * GROUP)
+            if i >= NO_WIDENING:
+                weigh(i - 2)
             if i == 0:
                 nc.scalar.copy(out=u_f32[:], in_=u_sb[:])
             for h in (0, 1) if i == 0 else (1, 0):
@@ -307,19 +312,21 @@ def tile_pairwiseneuraltensorscorer_t_kernel(tc, e1_bytes, e1_scale, e2, w, v, b
                 scores(i - 1, 0, 1)
             else:
                 for c in range(PACK):
-                    if c == PACK - 1:
+                    if c == PACK - 1 and i < NO_WIDENING:
                         fill_sum(i - 2, 1)
                     planes_bank(i + 1, c)
                 block(i, 0)
                 for h in range(2):
                     scores(i - 1, 0, h)
                 fill_block(i, 1)
-                for h in (1, 0):
+                for h in (1, 0) if i < NO_WIDENING else (0,):
                     read_sum(i - 2, h)
                 planes_bank(i + 1, slice0_banks.pop(0))
                 for c in range(2, vector_blocks(i)):
                     block(i, c)
                 read_block(i, 1)
+                if i >= NO_WIDENING:
+                    add_slices(i - 2, 1, u0_z[i % 2])
             for c in slice0_banks:
                 planes_bank(i + 1, c)
             if i == 0:
@@ -337,15 +344,15 @@ def tile_pairwiseneuraltensorscorer_t_kernel(tc, e1_bytes, e1_scale, e2, w, v, b
 
         quantize_e(LAST)
         quantize_h(LAST - 2)
+        weigh(LAST - 3)
         weave_h(LAST - 1, nc.gpsimd.tensor_copy, GROUP, T * GROUP)
         for c in range(2):
             read_block(LAST - 1, c)
             planes_bank(LAST, c)
         weave_h(LAST - 1, nc.scalar.copy, vector_blocks(LAST - 1) * P, GROUP)
-        read_sum(LAST - 3, 0)
-        fill_sum(LAST - 3, 1)
-        read_sum(LAST - 3, 1)
         block(LAST - 1, 2)
+        read_sum(LAST - 3, 0)
+        add_slices(LAST - 3, 1, u0_z[(LAST - 3) % 2])
         for c in range(2, PACK):
             planes_bank(LAST, c)
 
@@ -354,25 +361,24 @@ def tile_pairwiseneuraltensorscorer_t_kernel(tc, e1_bytes, e1_scale, e2, w, v, b
         for c in range(PACK):
             scores(LAST - 2, *divmod(c, 2))
             block(LAST, c)
-        for s in range(T):
-            for h in range(2):
-                scores(LAST - 1, s, h)
-            fill_sum(LAST - 2, s)
-            if s == 0:
-                read_sum(LAST - 2, 0)
+        weigh(LAST - 2)
+        for h in range(2):
+            scores(LAST - 1, 0, h)
+        fill_sum(LAST - 2, 0)
+        read_sum(LAST - 2, 0)
+        for h in range(2):
+            scores(LAST - 1, 1, h)
+        fill_sum(LAST - 1, 0)
         for s in range(T):
             cols = slice(s * GROUP, (s + 1) * GROUP)
             quantize(hq[LAST % 2][:, cols], hq_sc[LAST % 2][:, cols], h_woven[:, s * ROW : (s + 1) * ROW])
-        nc.scalar.activation(out=u0_z[2][:], in_=z[0, 1][(LAST - 1) % 2][:], func=ACT.Copy, scale=u_f32[:, 0:1])
-        add_slices(LAST - 1, 1, u0_z[2])
-        read_sum(LAST - 2, 1)
-        for h in range(2):
-            scores(LAST, 0, h)
-        fill_sum(LAST - 1, 0)
+        weigh(LAST - 1)
+        for g in (LAST - 2, LAST - 1):
+            add_slices(g, 1, u0_z[g % 2])
         read_sum(LAST - 1, 0)
+        for c in range(PACK):
+            scores(LAST, *divmod(c, 2))
+        nc.gpsimd.tensor_scalar(out=u0_z[2][:], in0=z[0, 0][LAST % 2][:], scalar1=u_f32[:, 0:1], scalar2=0.0, op0=MULT, op1=ADD)
+        nc.vector.tensor_scalar(out=u0_z[3][:], in0=z[0, 1][LAST % 2][:], scalar1=u_f32[:, 0:1], scalar2=None, op0=MULT)
         for h in range(2):
-            scores(LAST, 1, h)
-        nc.gpsimd.tensor_scalar(out=u0_z[0][:], in0=z[0, 0][LAST % 2][:], scalar1=u_f32[:, 0:1], scalar2=0.0, op0=MULT, op1=ADD)
-        nc.vector.tensor_scalar(out=u0_z[1][:], in0=z[0, 1][LAST % 2][:], scalar1=u_f32[:, 0:1], scalar2=None, op0=MULT)
-        for h in range(2):
-            add_slices(LAST, h, u0_z[h])
+            add_slices(LAST, h, u0_z[2 + h])

@@ -146,9 +146,9 @@ def tile_pairwiseneuraltensorscorer_t_kernel(tc, e1_bytes, e1_scale, e2, w, v, b
         def scalar_cast(out, in_):
             nc.scalar.activation(out=out, in_=in_, func=ACT.Copy)
 
-        def weave_w(s, copy, part):
-            copy(out=w_woven[s][:].rearrange("p (t m j) -> p t m j", t=PACK, j=PACK)[:, :, part],
-                 in_=w_raw[s][:].rearrange("p (j m t) -> p t m j", t=PACK, j=PACK)[:, :, part])
+        def weave_w(s, copy, part, walk):
+            copy(out=w_woven[s][:].rearrange("p (t m j) -> p m t j", t=PACK, j=PACK)[:, part].rearrange("p m t j -> " + walk),
+                 in_=w_raw[s][:].rearrange("p (j m t) -> p m t j", t=PACK, j=PACK)[:, part].rearrange("p m t j -> " + walk))
 
         def quantize(codes, scales, src):
             nc.vector.quantize_mx(out=codes.bitcast(FP8X4), scales=scales, in_=src)
@@ -254,15 +254,15 @@ def tile_pairwiseneuraltensorscorer_t_kernel(tc, e1_bytes, e1_scale, e2, w, v, b
         widen(scalar_cast, ROW // 2)
         for h in range(2):
             turn_e(0, h)
-        weave_w(1, nc.vector.tensor_copy, slice(0, P))
+        weave_w(1, nc.vector.tensor_copy, slice(0, P), "p m j t")
         widen(nc.gpsimd.tensor_copy, ROW // 4)
         widen(scalar_cast, ROW - ROW // 4)
         for h in range(2):
             read_e(0, h)
         for h in range(2):
             turn_e(1, h)
-        weave_w(0, nc.gpsimd.tensor_copy, slice(0, P // 2))
-        weave_w(0, nc.scalar.copy, slice(P // 2, P))
+        weave_w(0, nc.gpsimd.tensor_copy, slice(0, P // 2), "p t m j")
+        weave_w(0, nc.scalar.copy, slice(P // 2, P), "p m j t")
         quantize(wq[1][:], wq_sc[1][:], w_woven[1][:])
         quantize_e(0)
         widen(scalar_cast, ROW)

@@ -31,6 +31,7 @@ SHORT = 256
 HEAD = 1664
 SCALAR_LEAST = 896
 MIDDLE = 5
+QUARTER = P // 4
 NO_WIDENING = LAST - AHEAD
 
 
@@ -205,9 +206,9 @@ def tile_pairwiseneuraltensorscorer_t_kernel(tc, e1_bytes, e1_scale, e2, w, v, b
                 nc.scalar.activation(out=planes[g % 2][:, t, s * GROUP + first : s * GROUP + first + width],
                                      in_=bank[:, n * width : (n + 1) * width], func=ACT.Identity, bias=v_sb[:, s, t : t + 1])
 
-        def weave_h(g, copy, first, end):
-            copy(out=h_woven[:, first * PACK : end * PACK].rearrange("p (n t) -> p n t", t=PACK),
-                 in_=planes[g % 2][:, :, first:end].rearrange("p t n -> p n t"))
+        def weave_h(g, copy, first, end, walk):
+            copy(out=h_woven[:, first * PACK : end * PACK].rearrange("p (c i t) -> " + walk, i=PACK, t=PACK),
+                 in_=planes[g % 2][:, :, first:end].rearrange("p t (c i) -> " + walk, i=PACK))
 
         def quantize_h(g):
             quantize(hq[g % 2][:], hq_sc[g % 2][:], h_woven[:])
@@ -254,15 +255,16 @@ def tile_pairwiseneuraltensorscorer_t_kernel(tc, e1_bytes, e1_scale, e2, w, v, b
         widen(scalar_cast, ROW // 2)
         for h in range(2):
             turn_e(0, h)
-        weave_w(1, nc.vector.tensor_copy, slice(0, P), "p m j t")
-        widen(nc.gpsimd.tensor_copy, ROW // 4)
-        widen(scalar_cast, ROW - ROW // 4)
+        weave_w(1, nc.vector.tensor_copy, slice(0, P - QUARTER), "p m j t")
+        weave_w(1, nc.scalar.copy, slice(P - QUARTER, P), "p m j t")
+        widen(nc.gpsimd.tensor_copy, ROW // 2)
+        widen(scalar_cast, ROW // 2)
         for h in range(2):
             read_e(0, h)
         for h in range(2):
             turn_e(1, h)
-        weave_w(0, nc.gpsimd.tensor_copy, slice(0, P // 2), "p t m j")
-        weave_w(0, nc.scalar.copy, slice(P // 2, P), "p m j t")
+        weave_w(0, nc.gpsimd.tensor_copy, slice(0, QUARTER), "p t m j")
+        weave_w(0, nc.scalar.copy, slice(QUARTER, P), "p m j t")
         quantize(wq[1][:], wq_sc[1][:], w_woven[1][:])
         quantize_e(0)
         widen(scalar_cast, ROW)
@@ -287,7 +289,7 @@ def tile_pairwiseneuraltensorscorer_t_kernel(tc, e1_bytes, e1_scale, e2, w, v, b
             widen(scalar_cast, max((i + AHEAD + 1) * ROW - widened[-1], SCALAR_LEAST if i >= 1 else 0))
             widen(nc.gpsimd.tensor_copy, gpsimd_columns(i))
             assert widened[-1] <= (i + AHEAD + 2) * ROW
-            weave_h(i, nc.gpsimd.tensor_copy, vector_blocks(i) * P, T * GROUP)
+            weave_h(i, nc.gpsimd.tensor_copy, vector_blocks(i) * P, T * GROUP, "p (c i) t")
             if i >= NO_WIDENING:
                 weigh(i - 2)
             if i == 0:
@@ -345,11 +347,11 @@ def tile_pairwiseneuraltensorscorer_t_kernel(tc, e1_bytes, e1_scale, e2, w, v, b
         quantize_e(LAST)
         quantize_h(LAST - 2)
         weigh(LAST - 3)
-        weave_h(LAST - 1, nc.gpsimd.tensor_copy, GROUP, T * GROUP)
+        weave_h(LAST - 1, nc.gpsimd.tensor_copy, GROUP, T * GROUP, "p (c i) t")
         for c in range(2):
             read_block(LAST - 1, c)
             planes_bank(LAST, c)
-        weave_h(LAST - 1, nc.scalar.copy, vector_blocks(LAST - 1) * P, GROUP)
+        weave_h(LAST - 1, nc.scalar.copy, vector_blocks(LAST - 1) * P, GROUP, "p c t i")
         block(LAST - 1, 2)
         read_sum(LAST - 3, 0)
         add_slices(LAST - 3, 1, u0_z[(LAST - 3) % 2])
@@ -357,7 +359,7 @@ def tile_pairwiseneuraltensorscorer_t_kernel(tc, e1_bytes, e1_scale, e2, w, v, b
             planes_bank(LAST, c)
 
         quantize_h(LAST - 1)
-        weave_h(LAST, nc.gpsimd.tensor_copy, GROUP, T * GROUP)
+        weave_h(LAST, nc.gpsimd.tensor_copy, GROUP, T * GROUP, "p (c i) t")
         for c in range(PACK):
             scores(LAST - 2, *divmod(c, 2))
             block(LAST, c)

@@ -26,9 +26,8 @@ BANK = 512
 HALF = BANK // 2
 AHEAD = 3
 
-LONG = 1344
+LONG = 1408
 SHORT = 256
-HEAD = 1664
 SCALAR_LEAST = 896
 MIDDLE = 5
 QUARTER = P // 4
@@ -268,7 +267,7 @@ def tile_pairwiseneuraltensorscorer_t_kernel(tc, e1_bytes, e1_scale, e2, w, v, b
         quantize(wq[1][:], wq_sc[1][:], w_woven[1][:])
         quantize_e(0)
         widen(scalar_cast, ROW)
-        widen(nc.gpsimd.tensor_copy, HEAD)
+        widen(nc.gpsimd.tensor_copy, LONG)
         for h in range(2):
             read_e(1, h)
         for c in range(PACK - 1):
@@ -347,11 +346,11 @@ def tile_pairwiseneuraltensorscorer_t_kernel(tc, e1_bytes, e1_scale, e2, w, v, b
         quantize_e(LAST)
         quantize_h(LAST - 2)
         weigh(LAST - 3)
-        weave_h(LAST - 1, nc.gpsimd.tensor_copy, GROUP, T * GROUP, "p (c i) t")
+        weave_h(LAST - 1, nc.gpsimd.tensor_copy, GROUP + P, T * GROUP, "p (c i) t")
         for c in range(2):
             read_block(LAST - 1, c)
             planes_bank(LAST, c)
-        weave_h(LAST - 1, nc.scalar.copy, vector_blocks(LAST - 1) * P, GROUP, "p c t i")
+        weave_h(LAST - 1, nc.scalar.copy, vector_blocks(LAST - 1) * P, GROUP + P, "p c t i")
         block(LAST - 1, 2)
         read_sum(LAST - 3, 0)
         add_slices(LAST - 3, 1, u0_z[(LAST - 3) % 2])

@@ -25,23 +25,34 @@ ROW = PACK * D
 BANK = 512
 HALF = BANK // 2
 AHEAD = 3
+H_TILES = 3
 
-LONG = 1408
-SHORT = 256
-SCALAR_LEAST = 896
-MIDDLE = 5
+GPSIMD_COLUMNS = 1792
+SCALAR_SHORT = 1280
+SCALAR_LONG = 768
+HEAD_COLUMNS = 1408
 QUARTER = P // 4
+SPLIT = GROUP + HALF
+Z_TILES = 4
 NO_WIDENING = LAST - AHEAD
 
 
+def long_period(i):
+    return i == 0 or (i % 2 == 1 and i < NO_WIDENING)
+
+
 def vector_blocks(g):
-    if g in (0, LAST):
-        return PACK
-    return 2 if g == MIDDLE or NO_WIDENING <= g < LAST - 1 else 3
+    if g >= LAST - 1:
+        return 2 if g < LAST else PACK
+    return PACK if long_period(g) else 2
 
 
-def gpsimd_columns(i):
-    return SHORT if i == 1 or vector_blocks(i) == 2 else LONG
+def weighed(g):
+    return g % 2 == 1 or g >= NO_WIDENING - 2
+
+
+def scalar_columns(i):
+    return SCALAR_LONG if long_period(i) else SCALAR_SHORT
 
 
 def scalar_banks(g):
@@ -67,8 +78,8 @@ def tile_pairwiseneuraltensorscorer_t_kernel(tc, e1_bytes, e1_scale, e2, w, v, b
         e1_rows = e1_bytes.rearrange("(g p j) k -> g p (j k)", p=P, j=PACK)
         out_rows = out.rearrange("(g p j) n -> g p (j n)", p=P, j=PACK)
 
-        raw = tiles("raw", GROUPS, [P, ROW], U8)
-        wide = tiles("wide", GROUPS, [P, ROW], BF16)
+        (raw,) = tiles("raw", 1, [P, GROUPS * ROW], U8)
+        (wide,) = tiles("wide", 1, [P, GROUPS * ROW], BF16)
         w_raw = tiles("w_raw", T, [P, ROW], BF16)
         w_woven = tiles("w_woven", T, [P, ROW], BF16)
         wq = tiles("wq", T, [P, D], U32)
@@ -84,16 +95,21 @@ def tile_pairwiseneuraltensorscorer_t_kernel(tc, e1_bytes, e1_scale, e2, w, v, b
         (e2q_sc,) = tiles("e2q_sc", 1, [P, N2], U8)
         (ident,) = tiles("ident", 1, [P, P], F32)
         (u0_ident,) = tiles("u0_ident", 1, [P, P], F32)
-        e_woven = [wide[(g + AHEAD) % GROUPS] for g in range(GROUPS)]
+        h_tiles = tiles("h_woven", H_TILES, [P, T * ROW], BF16)
+        h_woven = [h_tiles[g % H_TILES] for g in range(GROUPS)]
+        e_woven = [h_tiles[(g - 1) % H_TILES][:, ROW : 2 * ROW] if g >= 2 else wide[:, (g + AHEAD) * ROW : (g + AHEAD + 1) * ROW] for g in range(GROUPS)]
         eq = tiles("eq", 2, [P, GROUP], U32)
         eq_sc = tiles("eq_sc", 2, [P, GROUP], U8)
         planes = tiles("planes", 2, [P, PACK, T * GROUP], BF16)
-        (h_woven,) = tiles("h_woven", 1, [P, T * ROW], BF16)
         hq = tiles("hq", 2, [P, T * GROUP], U32)
         hq_sc = tiles("hq_sc", 2, [P, T * GROUP], U8)
-        z = {(s, h): tiles(f"z{s}{h}_", 2, [P, BANK], F32) for s in range(T) for h in range(2)}
-        u0_z = tiles("u0_z", 4, [P, BANK], F32)
-        o_sb = tiles("o_sb", 2 * GROUPS, [P, BANK], F32)
+        z0 = tiles("z0_", 2 * Z_TILES, [P, BANK], F32)
+        z1 = tiles("z1_", 2 * GROUPS, [P, BANK], F32)
+
+        def z(g, s, h):
+            return z1[2 * g + h] if s else z0[2 * (g % Z_TILES) + h]
+
+        u0_z = tiles("u0_z", 3, [P, BANK], F32)
 
         free = {"vector": [ps.tile([P, BANK], F32, name=f"vbank{n}") for n in range(4)],
                 "scalar": [ps.tile([P, BANK], F32, name=f"sbank{n}") for n in range(4)]}
@@ -109,7 +125,7 @@ def tile_pairwiseneuraltensorscorer_t_kernel(tc, e1_bytes, e1_scale, e2, w, v, b
             return bank
 
         def load_e1(g):
-            nc.sync.dma_start(out=raw[g][:], in_=e1_rows[g])
+            nc.sync.dma_start(out=raw[:, g * ROW : (g + 1) * ROW], in_=e1_rows[g])
 
         def load_w(s):
             nc.sync.dma_start(out=w_raw[s][:], in_=w[s].rearrange("(p j) c -> p (j c)", j=PACK))
@@ -136,11 +152,8 @@ def tile_pairwiseneuraltensorscorer_t_kernel(tc, e1_bytes, e1_scale, e2, w, v, b
         def widen(copy, count):
             start = widened[-1]
             end = min(start + count, GROUPS * ROW)
-            while start < end:
-                g, c = divmod(start, ROW)
-                n = min(end - start, ROW - c)
-                copy(out=wide[g][:, c : c + n], in_=raw[g][:, c : c + n].bitcast(FP8))
-                start = start + n
+            if start < end:
+                copy(out=wide[:, start:end], in_=raw[:, start:end].bitcast(FP8))
             widened.append(end)
 
         def scalar_cast(out, in_):
@@ -168,7 +181,7 @@ def tile_pairwiseneuraltensorscorer_t_kernel(tc, e1_bytes, e1_scale, e2, w, v, b
 
         def turn_e(g, h):
             assert widened[-1] >= g * ROW + (h + 1) * 2 * D
-            turn_words(take("vector", ("e", g, h)), [wide[g][:, (2 * h + j) * D : (2 * h + j + 1) * D] for j in range(2)])
+            turn_words(take("vector", ("e", g, h)), [wide[:, (PACK * g + 2 * h + j) * D : (PACK * g + 2 * h + j + 1) * D] for j in range(2)])
 
         def read_e(g, h):
             nc.vector.tensor_tensor(
@@ -177,7 +190,7 @@ def tile_pairwiseneuraltensorscorer_t_kernel(tc, e1_bytes, e1_scale, e2, w, v, b
                 in1=scale_sb[:].rearrange("p (a i) -> p a i", i=2).unsqueeze(1).to_broadcast([P, HALF, 2, 2]), op=MULT)
 
         def quantize_e(g):
-            quantize(eq[g % 2][:], eq_sc[g % 2][:], e_woven[g][:])
+            quantize(eq[g % 2][:], eq_sc[g % 2][:], e_woven[g])
 
         def plane(dst, g, s, t, cols):
             fixed = slice(t * P, (t + 1) * P)
@@ -190,7 +203,7 @@ def tile_pairwiseneuraltensorscorer_t_kernel(tc, e1_bytes, e1_scale, e2, w, v, b
                 plane(bank[:, t * P : (t + 1) * P], g, 0, t, slice(c * P, (c + 1) * P))
 
         def read_block(g, c):
-            nc.vector.tensor_tensor(out=h_woven[:, c * BANK : (c + 1) * BANK].rearrange("p (n t) -> p n t", t=PACK),
+            nc.vector.tensor_tensor(out=h_woven[g][:, c * BANK : (c + 1) * BANK].rearrange("p (n t) -> p n t", t=PACK),
                                     in0=give(("block", g, c))[:].rearrange("p (t n) -> p n t", t=PACK),
                                     in1=v_sb[:, 0, :].unsqueeze(1).to_broadcast([P, P, PACK]), op=ADD)
 
@@ -205,12 +218,16 @@ def tile_pairwiseneuraltensorscorer_t_kernel(tc, e1_bytes, e1_scale, e2, w, v, b
                 nc.scalar.activation(out=planes[g % 2][:, t, s * GROUP + first : s * GROUP + first + width],
                                      in_=bank[:, n * width : (n + 1) * width], func=ACT.Identity, bias=v_sb[:, s, t : t + 1])
 
+        def woven(g, first, end):
+            shift = SPLIT if g == LAST and first >= SPLIT else 0
+            return h_woven[g][:, (first - shift) * PACK : (end - shift) * PACK]
+
         def weave_h(g, copy, first, end, walk):
-            copy(out=h_woven[:, first * PACK : end * PACK].rearrange("p (c i t) -> " + walk, i=PACK, t=PACK),
+            copy(out=woven(g, first, end).rearrange("p (c i t) -> " + walk, i=PACK, t=PACK),
                  in_=planes[g % 2][:, :, first:end].rearrange("p t (c i) -> " + walk, i=PACK))
 
-        def quantize_h(g):
-            quantize(hq[g % 2][:], hq_sc[g % 2][:], h_woven[:])
+        def quantize_h(g, first=0, end=T * GROUP):
+            quantize(hq[g % 2][:, first:end], hq_sc[g % 2][:, first:end], woven(g, first, end))
 
         def fill_scores(g, s, h):
             bank = take("scalar", ("scores", g, s, h))
@@ -221,22 +238,25 @@ def tile_pairwiseneuraltensorscorer_t_kernel(tc, e1_bytes, e1_scale, e2, w, v, b
                                     start=True, stop=True)
 
         def read_scores(g, s, h):
-            nc.scalar.activation(out=z[s, h][g % 2][:], in_=give(("scores", g, s, h))[:], func=ACT.Tanh,
+            nc.scalar.activation(out=z(g, s, h)[:], in_=give(("scores", g, s, h))[:], func=ACT.Tanh,
                                  bias=b_sb[:, s : s + 1], scale=D ** -0.5)
 
         def fill_sum(g, h):
-            nc.tensor.matmul(out=take("vector", ("sum", g, h))[:], lhsT=u0_ident[:], rhs=z[0, h][g % 2][:], start=True, stop=True)
+            nc.tensor.matmul(out=take("vector", ("sum", g, h))[:], lhsT=u0_ident[:], rhs=z(g, 0, h)[:], start=True, stop=True)
 
         def add_slices(g, h, weighed):
-            o = o_sb[2 * g + h]
-            nc.vector.scalar_tensor_tensor(out=o[:], in0=z[1, h][g % 2][:], scalar=u_f32[:, 1:2], in1=weighed[:], op0=MULT, op1=ADD)
+            o = z(g, 1, h)
+            nc.vector.scalar_tensor_tensor(out=o[:], in0=o[:], scalar=u_f32[:, 1:2], in1=weighed[:], op0=MULT, op1=ADD)
             nc.sync.dma_start(out=out_rows[g][:, h * BANK : (h + 1) * BANK], in_=o[:])
 
         def read_sum(g, h):
             add_slices(g, h, give(("sum", g, h)))
 
-        def weigh(g):
-            nc.scalar.activation(out=u0_z[g % 2][:], in_=z[0, 1][g % 2][:], func=ACT.Copy, scale=u_f32[:, 0:1])
+        def weigh(g, h, dst):
+            nc.scalar.activation(out=dst[:], in_=z(g, 0, h)[:], func=ACT.Copy, scale=u_f32[:, 0:1])
+
+        def gpsimd_weigh(g, dst):
+            nc.gpsimd.tensor_scalar(out=dst, in0=z(g, 0, 1)[:], scalar1=u_f32[:, 0:1], scalar2=0.0, op0=MULT, op1=ADD)
 
         def block(g, c):
             fill_block(g, c)
@@ -267,17 +287,19 @@ def tile_pairwiseneuraltensorscorer_t_kernel(tc, e1_bytes, e1_scale, e2, w, v, b
         quantize(wq[1][:], wq_sc[1][:], w_woven[1][:])
         quantize_e(0)
         widen(scalar_cast, ROW)
-        widen(nc.gpsimd.tensor_copy, LONG)
+        widen(nc.gpsimd.tensor_copy, HEAD_COLUMNS)
         for h in range(2):
             read_e(1, h)
         for c in range(PACK - 1):
             planes_bank(0, c)
         for h in range(2):
             turn_e(2, h)
+        widen(scalar_cast, ROW - HEAD_COLUMNS)
+        planes_bank(0, PACK - 1)
         turn_e2()
         read_e2()
-        planes_bank(0, PACK - 1)
         quantize(wq[0][:], wq_sc[0][:], w_woven[0][:])
+
 
         for i in range(LAST - 1):
             if i == 1:
@@ -285,17 +307,19 @@ def tile_pairwiseneuraltensorscorer_t_kernel(tc, e1_bytes, e1_scale, e2, w, v, b
             quantize_e(i + 1)
             if i >= 1:
                 quantize_h(i - 1)
-            widen(scalar_cast, max((i + AHEAD + 1) * ROW - widened[-1], SCALAR_LEAST if i >= 1 else 0))
-            widen(nc.gpsimd.tensor_copy, gpsimd_columns(i))
-            assert widened[-1] <= (i + AHEAD + 2) * ROW
-            weave_h(i, nc.gpsimd.tensor_copy, vector_blocks(i) * P, T * GROUP, "p (c i) t")
+            widen(scalar_cast, max((i + AHEAD + 1) * ROW - widened[-1], scalar_columns(i)))
             if i >= NO_WIDENING:
-                weigh(i - 2)
+                weigh(i - 2, 1, u0_z[(i - 2) % 3])
+            if i == 0:
+                widen(nc.gpsimd.tensor_copy, HEAD_COLUMNS)
+            weave_h(i, nc.gpsimd.tensor_copy, vector_blocks(i) * P, T * GROUP, "p (c i) t")
+            if long_period(i) and i >= 1:
+                widen(nc.gpsimd.tensor_copy, GPSIMD_COLUMNS if i >= 2 else HEAD_COLUMNS)
             if i == 0:
                 nc.scalar.copy(out=u_f32[:], in_=u_sb[:])
-            for h in (0, 1) if i == 0 else (1, 0):
+            for h in range(2):
                 read_e(i + 2, h)
-            slice0_banks = list(range(PACK, len(scalar_banks(i + 1))))
+            rest = list(range(PACK, len(scalar_banks(i + 1))))
             if i == 0:
                 for c in range(2):
                     block(i, c)
@@ -303,83 +327,90 @@ def tile_pairwiseneuraltensorscorer_t_kernel(tc, e1_bytes, e1_scale, e2, w, v, b
                     planes_bank(i + 1, c)
                     if c >= 2:
                         block(i, c)
-            elif i == 1:
-                for c in range(2):
-                    block(i, c)
+                nc.scalar.activation(out=u0_ident[:], in_=ident[:], func=ACT.Copy, scale=u_f32[:, 0:1])
+            elif long_period(i):
                 for c in range(PACK):
-                    planes_bank(i + 1, c)
-                scores(i - 1, 0, 0)
-                block(i, 2)
-                scores(i - 1, 0, 1)
-            else:
-                for c in range(PACK):
-                    if c == PACK - 1 and i < NO_WIDENING:
-                        fill_sum(i - 2, 1)
                     planes_bank(i + 1, c)
                 block(i, 0)
+                if i >= 2:
+                    read_sum(i - 2, 0)
                 for h in range(2):
                     scores(i - 1, 0, h)
-                fill_block(i, 1)
-                for h in (1, 0) if i < NO_WIDENING else (0,):
-                    read_sum(i - 2, h)
-                planes_bank(i + 1, slice0_banks.pop(0))
-                for c in range(2, vector_blocks(i)):
-                    block(i, c)
-                read_block(i, 1)
-                if i >= NO_WIDENING:
-                    add_slices(i - 2, 1, u0_z[i % 2])
-            for c in slice0_banks:
-                planes_bank(i + 1, c)
-            if i == 0:
-                nc.scalar.activation(out=u0_ident[:], in_=ident[:], func=ACT.Copy, scale=u_f32[:, 0:1])
-            else:
+                block(i, 1)
+                for c in range(2):
+                    planes_bank(i + 1, rest[c])
+                    block(i, 2 + c)
                 for h in range(2):
                     scores(i - 1, 1, h)
+            else:
+                for c in range(PACK):
+                    if c == PACK - 1 and not weighed(i - 2):
+                        fill_sum(i - 2, 1)
+                    planes_bank(i + 1, c)
+                if i >= NO_WIDENING:
+                    fill_sum(i - 2, 0)
+                fill_block(i, 0)
+                for h in range(1 if weighed(i - 2) else 2):
+                    read_sum(i - 2, h)
+                read_block(i, 0)
+                scores(i - 1, 0, 0)
+                block(i, 1)
+                scores(i - 1, 0, 1)
+                for n, c in enumerate(rest):
+                    planes_bank(i + 1, c)
+                    if i + AHEAD > LAST:
+                        fill_block(i + 1, n)
+                for h in range(2):
+                    scores(i - 1, 1, h)
+            if i >= 2 and weighed(i - 2):
+                add_slices(i - 2, 1, u0_z[(i - 2) % 3])
+            if 1 <= i < NO_WIDENING - 1 and weighed(i - 1):
+                weigh(i - 1, 1, u0_z[(i - 1) % 3])
             for n in range(2):
                 if i + AHEAD <= LAST:
                     turn_e(i + AHEAD, n)
-                else:
-                    fill_block(i + 1, n)
-            if i >= 1:
+            if 1 <= i < NO_WIDENING - 1 or i == LAST - 2:
                 fill_sum(i - 1, 0)
 
-        quantize_e(LAST)
-        quantize_h(LAST - 2)
-        weigh(LAST - 3)
-        weave_h(LAST - 1, nc.gpsimd.tensor_copy, GROUP + P, T * GROUP, "p (c i) t")
+        g8, g9, g10, g11 = range(LAST - 3, LAST + 1)
+        quantize_e(g11)
+        quantize_h(g9)
+        weave_h(g10, nc.gpsimd.tensor_copy, vector_blocks(g10) * P, T * GROUP, "p (c i) t")
+        for c in range(PACK):
+            planes_bank(g11, c)
+        fill_block(g11, 0)
         for c in range(2):
-            read_block(LAST - 1, c)
-            planes_bank(LAST, c)
-        weave_h(LAST - 1, nc.scalar.copy, vector_blocks(LAST - 1) * P, GROUP + P, "p c t i")
-        block(LAST - 1, 2)
-        read_sum(LAST - 3, 0)
-        add_slices(LAST - 3, 1, u0_z[(LAST - 3) % 2])
-        for c in range(2, PACK):
-            planes_bank(LAST, c)
-
-        quantize_h(LAST - 1)
-        weave_h(LAST, nc.gpsimd.tensor_copy, GROUP, T * GROUP, "p (c i) t")
+            read_block(g10, c)
+        read_sum(g8, 0)
+        for c in range(1, PACK):
+            fill_block(g11, c)
+            scores(g9, *divmod(c - 1, 2))
+            read_block(g11, c - 1)
+        scores(g9, 1, 1)
+        read_block(g11, PACK - 1)
+        fill_sum(g8, 1)
+        fill_sum(g9, 0)
+        weave_h(g11, nc.scalar.copy, GROUP, SPLIT, "p c t i")
+        quantize_h(g10)
+        quantize_h(g11, 0, GROUP)
+        weave_h(g11, nc.gpsimd.tensor_copy, SPLIT, T * GROUP, "p (c i) t")
         for c in range(PACK):
-            scores(LAST - 2, *divmod(c, 2))
-            block(LAST, c)
-        weigh(LAST - 2)
+            scores(g10, *divmod(c, 2))
+        fill_sum(g10, 0)
+        read_sum(g8, 1)
+        read_sum(g9, 0)
         for h in range(2):
-            scores(LAST - 1, 0, h)
-        fill_sum(LAST - 2, 0)
-        read_sum(LAST - 2, 0)
+            scores(g11, 0, h)
+        quantize_h(g11, GROUP, SPLIT)
+        quantize_h(g11, SPLIT, T * GROUP)
         for h in range(2):
-            scores(LAST - 1, 1, h)
-        fill_sum(LAST - 1, 0)
-        for s in range(T):
-            cols = slice(s * GROUP, (s + 1) * GROUP)
-            quantize(hq[LAST % 2][:, cols], hq_sc[LAST % 2][:, cols], h_woven[:, s * ROW : (s + 1) * ROW])
-        weigh(LAST - 1)
-        for g in (LAST - 2, LAST - 1):
-            add_slices(g, 1, u0_z[g % 2])
-        read_sum(LAST - 1, 0)
-        for c in range(PACK):
-            scores(LAST, *divmod(c, 2))
-        nc.gpsimd.tensor_scalar(out=u0_z[2][:], in0=z[0, 0][LAST % 2][:], scalar1=u_f32[:, 0:1], scalar2=0.0, op0=MULT, op1=ADD)
-        nc.vector.tensor_scalar(out=u0_z[3][:], in0=z[0, 1][LAST % 2][:], scalar1=u_f32[:, 0:1], scalar2=None, op0=MULT)
-        for h in range(2):
-            add_slices(LAST, h, u0_z[2 + h])
+            scores(g11, 1, h)
+        nc.vector.tensor_scalar(out=u0_z[0][:], in0=z(g9, 0, 1)[:], scalar1=u_f32[:, 0:1], scalar2=None, op0=MULT)
+        nc.vector.tensor_scalar(out=u0_z[1][:], in0=z(g10, 0, 1)[:], scalar1=u_f32[:, 0:1], scalar2=None, op0=MULT)
+        add_slices(g9, 1, u0_z[0])
+        fill_sum(g11, 0)
+        read_sum(g10, 0)
+        add_slices(g10, 1, u0_z[1])
+        nc.vector.tensor_scalar(out=u0_z[2][:], in0=z(g11, 0, 1)[:], scalar1=u_f32[:, 0:1], scalar2=None, op0=MULT)
+        read_sum(g11, 0)
+        add_slices(g11, 1, u0_z[2])

@@ -27,9 +27,9 @@ HALF = BANK // 2
 AHEAD = 3
 H_TILES = 3
 
-GPSIMD_COLUMNS = 1792
+GPSIMD_COLUMNS = 2048
 SCALAR_SHORT = 1280
-SCALAR_LONG = 768
+SCALAR_LONG = 1024
 HEAD_COLUMNS = 1408
 QUARTER = P // 4
 SPLIT = GROUP + HALF
@@ -38,7 +38,7 @@ NO_WIDENING = LAST - AHEAD
 
 
 def long_period(i):
-    return i == 0 or (i % 2 == 1 and i < NO_WIDENING)
+    return i < NO_WIDENING and (i == 1 or i % 3 == 0)
 
 
 def vector_blocks(g):
@@ -48,7 +48,7 @@ def vector_blocks(g):
 
 
 def weighed(g):
-    return g % 2 == 1 or g >= NO_WIDENING - 2
+    return long_period(g + 2) or g >= NO_WIDENING - 2
 
 
 def scalar_columns(i):
@@ -282,8 +282,8 @@ def tile_pairwiseneuraltensorscorer_t_kernel(tc, e1_bytes, e1_scale, e2, w, v, b
             read_e(0, h)
         for h in range(2):
             turn_e(1, h)
-        weave_w(0, nc.gpsimd.tensor_copy, slice(0, QUARTER), "p t m j")
-        weave_w(0, nc.scalar.copy, slice(QUARTER, P), "p m j t")
+        weave_w(0, nc.gpsimd.tensor_copy, slice(0, 16), "p t m j")
+        weave_w(0, nc.scalar.copy, slice(16, P), "p m j t")
         quantize(wq[1][:], wq_sc[1][:], w_woven[1][:])
         quantize_e(0)
         widen(scalar_cast, ROW)
@@ -317,7 +317,7 @@ def tile_pairwiseneuraltensorscorer_t_kernel(tc, e1_bytes, e1_scale, e2, w, v, b
                 widen(nc.gpsimd.tensor_copy, GPSIMD_COLUMNS if i >= 2 else HEAD_COLUMNS)
             if i == 0:
                 nc.scalar.copy(out=u_f32[:], in_=u_sb[:])
-            for h in range(2):
+            for h in (0, 1) if i == 0 else (1, 0):
                 read_e(i + 2, h)
             rest = list(range(PACK, len(scalar_banks(i + 1))))
             if i == 0:
@@ -329,28 +329,39 @@ def tile_pairwiseneuraltensorscorer_t_kernel(tc, e1_bytes, e1_scale, e2, w, v, b
                         block(i, c)
                 nc.scalar.activation(out=u0_ident[:], in_=ident[:], func=ACT.Copy, scale=u_f32[:, 0:1])
             elif long_period(i):
+                both = i >= 2 and not weighed(i - 2)
                 for c in range(PACK):
+                    if c == PACK - 1 and both:
+                        fill_sum(i - 2, 1)
                     planes_bank(i + 1, c)
-                block(i, 0)
-                if i >= 2:
+                fill_block(i, 0)
+                if both:
+                    for h in range(2):
+                        read_sum(i - 2, h)
+                read_block(i, 0)
+                if i >= 2 and not both:
                     read_sum(i - 2, 0)
-                for h in range(2):
-                    scores(i - 1, 0, h)
-                block(i, 1)
+                scores(i - 1, 0, 0)
+                if both:
+                    block(i, 1)
+                scores(i - 1, 0, 1)
+                if not both:
+                    block(i, 1)
                 for c in range(2):
-                    planes_bank(i + 1, rest[c])
+                    if rest:
+                        planes_bank(i + 1, rest[c])
                     block(i, 2 + c)
                 for h in range(2):
                     scores(i - 1, 1, h)
             else:
                 for c in range(PACK):
-                    if c == PACK - 1 and not weighed(i - 2):
+                    if c == PACK - 1 and i >= 2 and not weighed(i - 2):
                         fill_sum(i - 2, 1)
                     planes_bank(i + 1, c)
                 if i >= NO_WIDENING:
                     fill_sum(i - 2, 0)
                 fill_block(i, 0)
-                for h in range(1 if weighed(i - 2) else 2):
+                for h in range(0 if i < 2 else 1 if weighed(i - 2) else 2):
                     read_sum(i - 2, h)
                 read_block(i, 0)
                 scores(i - 1, 0, 0)

@@ -28,8 +28,9 @@ AHEAD = 3
 H_TILES = 3
 
 GPSIMD_COLUMNS = 2048
-SCALAR_SHORT = 1280
-SCALAR_LONG = 1024
+GPSIMD_SHORT = 256
+SCALAR_SHORT = 1152
+SCALAR_LONG = 896
 HEAD_COLUMNS = 1408
 QUARTER = P // 4
 SPLIT = GROUP + HALF
@@ -53,6 +54,12 @@ def weighed(g):
 
 def scalar_columns(i):
     return SCALAR_LONG if long_period(i) else SCALAR_SHORT
+
+
+def gpsimd_columns(i):
+    if i == 1:
+        return HEAD_COLUMNS
+    return GPSIMD_COLUMNS if long_period(i) else GPSIMD_SHORT
 
 
 def scalar_banks(g):
@@ -134,8 +141,8 @@ def tile_pairwiseneuraltensorscorer_t_kernel(tc, e1_bytes, e1_scale, e2, w, v, b
         load_w(1)
         nc.sync.dma_start(out=scale_sb[:], in_=e1_scale.rearrange("o (p t) -> p (o t)", t=PACK))
         load_e1(1)
-        load_w(0)
         load_e1(2)
+        load_w(0)
         for r in range(2):
             nc.sync.dma_start(out=e2_sb[r][:], in_=e2[r * P : (r + 1) * P, :])
         load_e1(3)
@@ -237,17 +244,19 @@ def tile_pairwiseneuraltensorscorer_t_kernel(tc, e1_bytes, e1_scale, e2, w, v, b
                                     lhsT_scale=hq_sc[g % 2][:, fixed], rhs=e2q[:].bitcast(FP8X4), rhs_scale=e2q_sc[:],
                                     start=True, stop=True)
 
+        def tanh(dst, src, s):
+            nc.scalar.activation(out=dst, in_=src, func=ACT.Tanh, bias=b_sb[:, s : s + 1], scale=D ** -0.5)
+
         def read_scores(g, s, h):
-            nc.scalar.activation(out=z(g, s, h)[:], in_=give(("scores", g, s, h))[:], func=ACT.Tanh,
-                                 bias=b_sb[:, s : s + 1], scale=D ** -0.5)
+            tanh(z(g, s, h)[:], give(("scores", g, s, h))[:], s)
 
         def fill_sum(g, h):
             nc.tensor.matmul(out=take("vector", ("sum", g, h))[:], lhsT=u0_ident[:], rhs=z(g, 0, h)[:], start=True, stop=True)
 
-        def add_slices(g, h, weighed):
+        def add_slices(g, h, weighed, cols=slice(0, BANK)):
             o = z(g, 1, h)
-            nc.vector.scalar_tensor_tensor(out=o[:], in0=o[:], scalar=u_f32[:, 1:2], in1=weighed[:], op0=MULT, op1=ADD)
-            nc.sync.dma_start(out=out_rows[g][:, h * BANK : (h + 1) * BANK], in_=o[:])
+            nc.vector.scalar_tensor_tensor(out=o[:, cols], in0=o[:, cols], scalar=u_f32[:, 1:2], in1=weighed[:, cols], op0=MULT, op1=ADD)
+            nc.sync.dma_start(out=out_rows[g][:, h * BANK + cols.start : h * BANK + cols.stop], in_=o[:, cols])
 
         def read_sum(g, h):
             add_slices(g, h, give(("sum", g, h)))
@@ -274,28 +283,27 @@ def tile_pairwiseneuraltensorscorer_t_kernel(tc, e1_bytes, e1_scale, e2, w, v, b
         widen(scalar_cast, ROW // 2)
         for h in range(2):
             turn_e(0, h)
-        weave_w(1, nc.vector.tensor_copy, slice(0, P - QUARTER), "p m j t")
-        weave_w(1, nc.scalar.copy, slice(P - QUARTER, P), "p m j t")
+        weave_w(1, nc.vector.tensor_copy, slice(0, 96), "p m j t")
+        weave_w(1, nc.scalar.copy, slice(96, P), "p m j t")
         widen(nc.gpsimd.tensor_copy, ROW // 2)
         widen(scalar_cast, ROW // 2)
         for h in range(2):
             read_e(0, h)
         for h in range(2):
             turn_e(1, h)
+        widen(scalar_cast, ROW)
         weave_w(0, nc.gpsimd.tensor_copy, slice(0, 16), "p t m j")
         weave_w(0, nc.scalar.copy, slice(16, P), "p m j t")
         quantize(wq[1][:], wq_sc[1][:], w_woven[1][:])
         quantize_e(0)
-        widen(scalar_cast, ROW)
         widen(nc.gpsimd.tensor_copy, HEAD_COLUMNS)
-        for h in range(2):
-            read_e(1, h)
-        for c in range(PACK - 1):
-            planes_bank(0, c)
+        widen(scalar_cast, ROW - HEAD_COLUMNS)
         for h in range(2):
             turn_e(2, h)
-        widen(scalar_cast, ROW - HEAD_COLUMNS)
-        planes_bank(0, PACK - 1)
+        for h in range(2):
+            read_e(1, h)
+        for c in range(PACK):
+            planes_bank(0, c)
         turn_e2()
         read_e2()
         quantize(wq[0][:], wq_sc[0][:], w_woven[0][:])
@@ -313,8 +321,8 @@ def tile_pairwiseneuraltensorscorer_t_kernel(tc, e1_bytes, e1_scale, e2, w, v, b
             if i == 0:
                 widen(nc.gpsimd.tensor_copy, HEAD_COLUMNS)
             weave_h(i, nc.gpsimd.tensor_copy, vector_blocks(i) * P, T * GROUP, "p (c i) t")
-            if long_period(i) and i >= 1:
-                widen(nc.gpsimd.tensor_copy, GPSIMD_COLUMNS if i >= 2 else HEAD_COLUMNS)
+            if i >= 1:
+                widen(nc.gpsimd.tensor_copy, gpsimd_columns(i))
             if i == 0:
                 nc.scalar.copy(out=u_f32[:], in_=u_sb[:])
             for h in (0, 1) if i == 0 else (1, 0):
@@ -325,8 +333,8 @@ def tile_pairwiseneuraltensorscorer_t_kernel(tc, e1_bytes, e1_scale, e2, w, v, b
                     block(i, c)
                 for c in range(PACK):
                     planes_bank(i + 1, c)
-                    if c >= 2:
-                        block(i, c)
+                    if c in (1, 2):
+                        block(i, c + 1)
                 nc.scalar.activation(out=u0_ident[:], in_=ident[:], func=ACT.Copy, scale=u_f32[:, 0:1])
             elif long_period(i):
                 both = i >= 2 and not weighed(i - 2)

@@ -31,8 +31,9 @@ GPSIMD_COLUMNS = 2048
 GPSIMD_SHORT = 256
 SCALAR_SHORT = 1152
 SCALAR_LONG = 896
-HEAD_COLUMNS = 1408
+HEAD_COLUMNS = 1280
 QUARTER = P // 4
+EARLY_COLUMNS = 768
 SPLIT = GROUP + HALF
 Z_TILES = 4
 NO_WIDENING = LAST - AHEAD
@@ -53,6 +54,8 @@ def weighed(g):
 
 
 def scalar_columns(i):
+    if i == 1:
+        return HEAD_COLUMNS
     return SCALAR_LONG if long_period(i) else SCALAR_SHORT
 
 
@@ -104,7 +107,7 @@ def tile_pairwiseneuraltensorscorer_t_kernel(tc, e1_bytes, e1_scale, e2, w, v, b
         (u0_ident,) = tiles("u0_ident", 1, [P, P], F32)
         h_tiles = tiles("h_woven", H_TILES, [P, T * ROW], BF16)
         h_woven = [h_tiles[g % H_TILES] for g in range(GROUPS)]
-        e_woven = [h_tiles[(g - 1) % H_TILES][:, ROW : 2 * ROW] if g >= 2 else wide[:, (g + AHEAD) * ROW : (g + AHEAD + 1) * ROW] for g in range(GROUPS)]
+        e_woven = [h_tiles[(g - 1) % H_TILES][:, ROW : 2 * ROW] if g >= 2 else wide[:, (g + AHEAD) * ROW + EARLY_COLUMNS : (g + AHEAD + 1) * ROW + EARLY_COLUMNS] for g in range(GROUPS)]
         eq = tiles("eq", 2, [P, GROUP], U32)
         eq_sc = tiles("eq_sc", 2, [P, GROUP], U8)
         planes = tiles("planes", 2, [P, PACK, T * GROUP], BF16)
@@ -138,14 +141,14 @@ def tile_pairwiseneuraltensorscorer_t_kernel(tc, e1_bytes, e1_scale, e2, w, v, b
             nc.sync.dma_start(out=w_raw[s][:], in_=w[s].rearrange("(p j) c -> p (j c)", j=PACK))
 
         load_e1(0)
-        load_w(1)
-        nc.sync.dma_start(out=scale_sb[:], in_=e1_scale.rearrange("o (p t) -> p (o t)", t=PACK))
         load_e1(1)
+        nc.sync.dma_start(out=scale_sb[:], in_=e1_scale.rearrange("o (p t) -> p (o t)", t=PACK))
         load_e1(2)
+        load_w(1)
+        load_e1(3)
         load_w(0)
         for r in range(2):
             nc.sync.dma_start(out=e2_sb[r][:], in_=e2[r * P : (r + 1) * P, :])
-        load_e1(3)
         nc.sync.dma_start(out=v_sb[:], in_=v.rearrange("s (p t) -> p s t", t=PACK))
         load_e1(4)
         nc.sync.dma_start(out=b_sb[:], in_=b.partition_broadcast(P))
@@ -283,49 +286,50 @@ def tile_pairwiseneuraltensorscorer_t_kernel(tc, e1_bytes, e1_scale, e2, w, v, b
         widen(scalar_cast, ROW // 2)
         for h in range(2):
             turn_e(0, h)
-        weave_w(1, nc.vector.tensor_copy, slice(0, 96), "p m j t")
-        weave_w(1, nc.scalar.copy, slice(96, P), "p m j t")
-        widen(nc.gpsimd.tensor_copy, ROW // 2)
-        widen(scalar_cast, ROW // 2)
-        for h in range(2):
-            read_e(0, h)
+        widen(nc.vector.tensor_copy, ROW)
         for h in range(2):
             turn_e(1, h)
-        widen(scalar_cast, ROW)
-        weave_w(0, nc.gpsimd.tensor_copy, slice(0, 16), "p t m j")
-        weave_w(0, nc.scalar.copy, slice(16, P), "p m j t")
-        quantize(wq[1][:], wq_sc[1][:], w_woven[1][:])
-        quantize_e(0)
-        widen(nc.gpsimd.tensor_copy, HEAD_COLUMNS)
-        widen(scalar_cast, ROW - HEAD_COLUMNS)
+        widen(scalar_cast, ROW // 2)
+        widen(nc.gpsimd.tensor_copy, ROW // 2)
+        weave_w(1, nc.gpsimd.tensor_copy, slice(0, 16), "p t m j")
+        weave_w(1, nc.scalar.copy, slice(16, P), "p m j t")
+        widen(nc.gpsimd.tensor_copy, EARLY_COLUMNS)
         for h in range(2):
+            read_e(0, h)
             turn_e(2, h)
-        for h in range(2):
-            read_e(1, h)
+        weave_w(0, nc.scalar.copy, slice(0, P), "p m j t")
+        read_e(1, 0)
+        quantize_e(0)
+        quantize(wq[1][:], wq_sc[1][:], w_woven[1][:])
+        widen(nc.gpsimd.tensor_copy, 3 * D)
+        widen(scalar_cast, D)
+        read_e(1, 1)
         for c in range(PACK):
             planes_bank(0, c)
         turn_e2()
         read_e2()
-        quantize(wq[0][:], wq_sc[0][:], w_woven[0][:])
+        read_e(2, 0)
 
 
         for i in range(LAST - 1):
             if i == 1:
                 quantize(e2q[:], e2q_sc[:], e2_woven[:])
             quantize_e(i + 1)
-            if i >= 1:
+            if i == 0:
+                quantize(wq[0][:], wq_sc[0][:], w_woven[0][:])
+            else:
                 quantize_h(i - 1)
             widen(scalar_cast, max((i + AHEAD + 1) * ROW - widened[-1], scalar_columns(i)))
             if i >= NO_WIDENING:
                 weigh(i - 2, 1, u0_z[(i - 2) % 3])
             if i == 0:
-                widen(nc.gpsimd.tensor_copy, HEAD_COLUMNS)
+                widen(nc.gpsimd.tensor_copy, D)
             weave_h(i, nc.gpsimd.tensor_copy, vector_blocks(i) * P, T * GROUP, "p (c i) t")
             if i >= 1:
                 widen(nc.gpsimd.tensor_copy, gpsimd_columns(i))
             if i == 0:
                 nc.scalar.copy(out=u_f32[:], in_=u_sb[:])
-            for h in (0, 1) if i == 0 else (1, 0):
+            for h in (1,) if i == 0 else (1, 0):
                 read_e(i + 2, h)
             rest = list(range(PACK, len(scalar_banks(i + 1))))
             if i == 0:

from contextlib import ExitStack

import concourse.mybir as mybir
from concourse.masks import make_identity

N1, N2, D, T = 6144, 256, 512, 2
FLOPS = 2 * N1 * D * D * T + 2 * N1 * D * N2 * T

F32 = mybir.dt.float32
BF16 = mybir.dt.bfloat16
U32 = mybir.dt.uint32
U8 = mybir.dt.uint8
FP8 = mybir.dt.float8_e4m3fn
FP8X4 = mybir.dt.float8_e4m3fn_x4
ADD = mybir.AluOpType.add
MULT = mybir.AluOpType.mult
ACT = mybir.ActivationFunctionType

P = 128
PACK = 4
GROUP = P * PACK
GROUPS = N1 // GROUP
LAST = GROUPS - 1
ROW = PACK * D
BANK = 512
HALF = BANK // 2
AHEAD = 3
H_TILES = 3

GPSIMD_COLUMNS = 2048
GPSIMD_SHORT = 256
SCALAR_SHORT = 1152
SCALAR_LONG = 896
HEAD_COLUMNS = 1280
QUARTER = P // 4
EARLY_COLUMNS = 768
SPLIT = GROUP + HALF
Z_TILES = 4
NO_WIDENING = LAST - AHEAD


def long_period(i):
    return i < NO_WIDENING and (i == 1 or i % 3 == 0)


def vector_blocks(g):
    if g >= LAST - 1:
        return 2 if g < LAST else PACK
    return PACK if long_period(g) else 2


def weighed(g):
    return long_period(g + 2) or g >= NO_WIDENING - 2


def scalar_columns(i):
    if i == 1:
        return HEAD_COLUMNS
    return SCALAR_LONG if long_period(i) else SCALAR_SHORT


def gpsimd_columns(i):
    if i == 1:
        return HEAD_COLUMNS
    return GPSIMD_COLUMNS if long_period(i) else GPSIMD_SHORT


def scalar_banks(g):
    found = []
    for s, first in ((1, 0), (0, vector_blocks(g) * P)):
        width = GROUP - first
        if width > 0:
            per_bank = BANK // width
            found.extend([(s, first, width, t) for t in range(t0, t0 + per_bank)] for t0 in range(0, PACK, per_bank))
    return found


def tile_pairwiseneuraltensorscorer_t_kernel(tc, e1_bytes, e1_scale, e2, w, v, b, u, out):
    nc = tc.nc
    with ExitStack() as ctx:
        sb = ctx.enter_context(tc.tile_pool(name="sb", bufs=1))
        ps = ctx.enter_context(tc.psum_pool(name="ps", bufs=1))
        ctx.enter_context(tc.manual_schedule())

        def tiles(name, count, shape, dtype):
            return [sb.tile(shape, dtype, name=f"{name}{n}", align_bytes=64) for n in range(count)]

        e1_rows = e1_bytes.rearrange("(g p j) k -> g p (j k)", p=P, j=PACK)
        out_rows = out.rearrange("(g p j) n -> g p (j n)", p=P, j=PACK)

        (raw,) = tiles("raw", 1, [P, GROUPS * ROW], U8)
        (wide,) = tiles("wide", 1, [P, GROUPS * ROW], BF16)
        w_raw = tiles("w_raw", T, [P, ROW], BF16)
        w_woven = tiles("w_woven", T, [P, ROW], BF16)
        wq = tiles("wq", T, [P, D], U32)
        wq_sc = tiles("wq_sc", T, [P, D], U8)
        (scale_sb,) = tiles("scale_sb", 1, [P, PACK], F32)
        (v_sb,) = tiles("v_sb", 1, [P, T, PACK], BF16)
        (b_sb,) = tiles("b_sb", 1, [P, T], BF16)
        (u_sb,) = tiles("u_sb", 1, [P, T], BF16)
        (u_f32,) = tiles("u_f32", 1, [P, T], F32)
        e2_sb = tiles("e2_sb", 2, [P, D], BF16)
        (e2_woven,) = tiles("e2_woven", 1, [P, N2 * PACK], BF16)
        (e2q,) = tiles("e2q", 1, [P, N2], U32)
        (e2q_sc,) = tiles("e2q_sc", 1, [P, N2], U8)
        (ident,) = tiles("ident", 1, [P, P], F32)
        (u0_ident,) = tiles("u0_ident", 1, [P, P], F32)
        h_tiles = tiles("h_woven", H_TILES, [P, T * ROW], BF16)
        h_woven = [h_tiles[g % H_TILES] for g in range(GROUPS)]
        e_woven = [h_tiles[(g - 1) % H_TILES][:, ROW : 2 * ROW] if g >= 2 else wide[:, (g + AHEAD) * ROW + EARLY_COLUMNS : (g + AHEAD + 1) * ROW + EARLY_COLUMNS] for g in range(GROUPS)]
        eq = tiles("eq", 2, [P, GROUP], U32)
        eq_sc = tiles("eq_sc", 2, [P, GROUP], U8)
        planes = tiles("planes", 2, [P, PACK, T * GROUP], BF16)
        hq = tiles("hq", 2, [P, T * GROUP], U32)
        hq_sc = tiles("hq_sc", 2, [P, T * GROUP], U8)
        z0 = tiles("z0_", 2 * Z_TILES, [P, BANK], F32)
        z1 = tiles("z1_", 2 * GROUPS, [P, BANK], F32)

        def z(g, s, h):
            return z1[2 * g + h] if s else z0[2 * (g % Z_TILES) + h]

        u0_z = tiles("u0_z", 3, [P, BANK], F32)

        free = {"vector": [ps.tile([P, BANK], F32, name=f"vbank{n}") for n in range(4)],
                "scalar": [ps.tile([P, BANK], F32, name=f"sbank{n}") for n in range(4)]}
        held = {}

        def take(reader, key):
            held[key] = (reader, free[reader].pop(0))
            return held[key][1]

        def give(key):
            reader, bank = held.pop(key)
            free[reader].append(bank)
            return bank

        def load_e1(g):
            nc.sync.dma_start(out=raw[:, g * ROW : (g + 1) * ROW], in_=e1_rows[g])

        def load_w(s):
            nc.sync.dma_start(out=w_raw[s][:], in_=w[s].rearrange("(p j) c -> p (j c)", j=PACK))

        load_e1(0)
        load_e1(1)
        nc.sync.dma_start(out=scale_sb[:], in_=e1_scale.rearrange("o (p t) -> p (o t)", t=PACK))
        load_e1(2)
        load_w(1)
        load_e1(3)
        load_w(0)
        for r in range(2):
            nc.sync.dma_start(out=e2_sb[r][:], in_=e2[r * P : (r + 1) * P, :])
        nc.sync.dma_start(out=v_sb[:], in_=v.rearrange("s (p t) -> p s t", t=PACK))
        load_e1(4)
        nc.sync.dma_start(out=b_sb[:], in_=b.partition_broadcast(P))
        nc.sync.dma_start(out=u_sb[:], in_=u.partition_broadcast(P))
        for g in range(5, GROUPS):
            load_e1(g)
        make_identity(nc, ident[:])

        widened = [0]

        def widen(copy, count):
            start = widened[-1]
            end = min(start + count, GROUPS * ROW)
            if start < end:
                copy(out=wide[:, start:end], in_=raw[:, start:end].bitcast(FP8))
            widened.append(end)

        def scalar_cast(out, in_):
            nc.scalar.activation(out=out, in_=in_, func=ACT.Copy)

        def weave_w(s, copy, part, walk):
            copy(out=w_woven[s][:].rearrange("p (t m j) -> p m t j", t=PACK, j=PACK)[:, part].rearrange("p m t j -> " + walk),
                 in_=w_raw[s][:].rearrange("p (j m t) -> p m t j", t=PACK, j=PACK)[:, part].rearrange("p m t j -> " + walk))

        def quantize(codes, scales, src):
            nc.vector.quantize_mx(out=codes.bitcast(FP8X4), scales=scales, in_=src)

        def turn_words(bank, rows):
            for j in range(2):
                words = rows[j].bitcast(F32)
                for a in range(2):
                    nc.tensor.transpose(bank[:, a * HALF + j * P : a * HALF + (j + 1) * P], words[:, a : 2 * P : 2], ident[:])

        def turn_e2():
            turn_words(take("scalar", "e2"), [e2_sb[0][:], e2_sb[1][:]])

        def read_e2():
            nc.scalar.copy(out=e2_woven[:].bitcast(F32).rearrange("p (n a) -> p n a", a=2),
                           in_=give("e2")[:].rearrange("p (a n) -> p n a", a=2))

        def turn_e(g, h):
            assert widened[-1] >= g * ROW + (h + 1) * 2 * D
            turn_words(take("vector", ("e", g, h)), [wide[:, (PACK * g + 2 * h + j) * D : (PACK * g + 2 * h + j + 1) * D] for j in range(2)])

        def read_e(g, h):
            nc.vector.tensor_tensor(
                out=e_woven[g][:, h * 2 * D : (h + 1) * 2 * D].rearrange("p (n a i) -> p n a i", a=2, i=2),
                in0=give(("e", g, h))[:].bitcast(BF16).rearrange("p (a n i) -> p n a i", a=2, i=2),
                in1=scale_sb[:].rearrange("p (a i) -> p a i", i=2).unsqueeze(1).to_broadcast([P, HALF, 2, 2]), op=MULT)

        def quantize_e(g):
            quantize(eq[g % 2][:], eq_sc[g % 2][:], e_woven[g])

        def plane(dst, g, s, t, cols):
            fixed = slice(t * P, (t + 1) * P)
            nc.tensor.matmul_mx(out=dst, lhsT=wq[s][:, fixed].bitcast(FP8X4), lhsT_scale=wq_sc[s][:, fixed],
                                rhs=eq[g % 2][:, cols].bitcast(FP8X4), rhs_scale=eq_sc[g % 2][:, cols], start=True, stop=True)

        def fill_block(g, c):
            bank = take("vector", ("block", g, c))
            for t in range(PACK):
                plane(bank[:, t * P : (t + 1) * P], g, 0, t, slice(c * P, (c + 1) * P))

        def read_block(g, c):
            nc.vector.tensor_tensor(out=h_woven[g][:, c * BANK : (c + 1) * BANK].rearrange("p (n t) -> p n t", t=PACK),
                                    in0=give(("block", g, c))[:].rearrange("p (t n) -> p n t", t=PACK),
                                    in1=v_sb[:, 0, :].unsqueeze(1).to_broadcast([P, P, PACK]), op=ADD)

        def fill_planes(g, c):
            bank = take("scalar", ("planes", g, c))
            for n, (s, first, width, t) in enumerate(scalar_banks(g)[c]):
                plane(bank[:, n * width : (n + 1) * width], g, s, t, slice(first, first + width))

        def read_planes(g, c):
            bank = give(("planes", g, c))
            for n, (s, first, width, t) in enumerate(scalar_banks(g)[c]):
                nc.scalar.activation(out=planes[g % 2][:, t, s * GROUP + first : s * GROUP + first + width],
                                     in_=bank[:, n * width : (n + 1) * width], func=ACT.Identity, bias=v_sb[:, s, t : t + 1])

        def woven(g, first, end):
            shift = SPLIT if g == LAST and first >= SPLIT else 0
            return h_woven[g][:, (first - shift) * PACK : (end - shift) * PACK]

        def weave_h(g, copy, first, end, walk):
            copy(out=woven(g, first, end).rearrange("p (c i t) -> " + walk, i=PACK, t=PACK),
                 in_=planes[g % 2][:, :, first:end].rearrange("p t (c i) -> " + walk, i=PACK))

        def quantize_h(g, first=0, end=T * GROUP):
            quantize(hq[g % 2][:, first:end], hq_sc[g % 2][:, first:end], woven(g, first, end))

        def fill_scores(g, s, h):
            bank = take("scalar", ("scores", g, s, h))
            for j in range(2):
                fixed = slice(s * GROUP + (2 * h + j) * P, s * GROUP + (2 * h + j + 1) * P)
                nc.tensor.matmul_mx(out=bank[:, j * N2 : (j + 1) * N2], lhsT=hq[g % 2][:, fixed].bitcast(FP8X4),
                                    lhsT_scale=hq_sc[g % 2][:, fixed], rhs=e2q[:].bitcast(FP8X4), rhs_scale=e2q_sc[:],
                                    start=True, stop=True)

        def tanh(dst, src, s):
            nc.scalar.activation(out=dst, in_=src, func=ACT.Tanh, bias=b_sb[:, s : s + 1], scale=D ** -0.5)

        def read_scores(g, s, h):
            tanh(z(g, s, h)[:], give(("scores", g, s, h))[:], s)

        def fill_sum(g, h):
            nc.tensor.matmul(out=take("vector", ("sum", g, h))[:], lhsT=u0_ident[:], rhs=z(g, 0, h)[:], start=True, stop=True)

        def add_slices(g, h, weighed, cols=slice(0, BANK)):
            o = z(g, 1, h)
            nc.vector.scalar_tensor_tensor(out=o[:, cols], in0=o[:, cols], scalar=u_f32[:, 1:2], in1=weighed[:, cols], op0=MULT, op1=ADD)
            nc.sync.dma_start(out=out_rows[g][:, h * BANK + cols.start : h * BANK + cols.stop], in_=o[:, cols])

        def read_sum(g, h):
            add_slices(g, h, give(("sum", g, h)))

        def weigh(g, h, dst):
            nc.scalar.activation(out=dst[:], in_=z(g, 0, h)[:], func=ACT.Copy, scale=u_f32[:, 0:1])

        def gpsimd_weigh(g, dst):
            nc.gpsimd.tensor_scalar(out=dst, in0=z(g, 0, 1)[:], scalar1=u_f32[:, 0:1], scalar2=0.0, op0=MULT, op1=ADD)

        def block(g, c):
            fill_block(g, c)
            read_block(g, c)

        def planes_bank(g, c):
            fill_planes(g, c)
            read_planes(g, c)

        def scores(g, s, h):
            fill_scores(g, s, h)
            read_scores(g, s, h)

        widen(nc.vector.tensor_copy, ROW // 2)
        widen(scalar_cast, ROW // 2)
        for h in range(2):
            turn_e(0, h)
        widen(nc.vector.tensor_copy, ROW)
        for h in range(2):
            turn_e(1, h)
        widen(scalar_cast, ROW // 2)
        widen(nc.gpsimd.tensor_copy, ROW // 2)
        weave_w(1, nc.gpsimd.tensor_copy, slice(0, 16), "p t m j")
        weave_w(1, nc.scalar.copy, slice(16, P), "p m j t")
        widen(nc.gpsimd.tensor_copy, EARLY_COLUMNS)
        for h in range(2):
            read_e(0, h)
            turn_e(2, h)
        weave_w(0, nc.scalar.copy, slice(0, P), "p m j t")
        read_e(1, 0)
        quantize_e(0)
        quantize(wq[1][:], wq_sc[1][:], w_woven[1][:])
        widen(nc.gpsimd.tensor_copy, 3 * D)
        widen(scalar_cast, D)
        read_e(1, 1)
        for c in range(PACK):
            planes_bank(0, c)
        turn_e2()
        read_e2()
        read_e(2, 0)


        for i in range(LAST - 1):
            if i == 1:
                quantize(e2q[:], e2q_sc[:], e2_woven[:])
            quantize_e(i + 1)
            if i == 0:
                quantize(wq[0][:], wq_sc[0][:], w_woven[0][:])
            else:
                quantize_h(i - 1)
            widen(scalar_cast, max((i + AHEAD + 1) * ROW - widened[-1], scalar_columns(i)))
            if i >= NO_WIDENING:
                weigh(i - 2, 1, u0_z[(i - 2) % 3])
            if i == 0:
                widen(nc.gpsimd.tensor_copy, D)
            weave_h(i, nc.gpsimd.tensor_copy, vector_blocks(i) * P, T * GROUP, "p (c i) t")
            if i >= 1:
                widen(nc.gpsimd.tensor_copy, gpsimd_columns(i))
            if i == 0:
                nc.scalar.copy(out=u_f32[:], in_=u_sb[:])
            for h in (1,) if i == 0 else (1, 0):
                read_e(i + 2, h)
            rest = list(range(PACK, len(scalar_banks(i + 1))))
            if i == 0:
                for c in range(2):
                    block(i, c)
                for c in range(PACK):
                    planes_bank(i + 1, c)
                    if c in (1, 2):
                        block(i, c + 1)
                nc.scalar.activation(out=u0_ident[:], in_=ident[:], func=ACT.Copy, scale=u_f32[:, 0:1])
            elif long_period(i):
                both = i >= 2 and not weighed(i - 2)
                for c in range(PACK):
                    if c == PACK - 1 and both:
                        fill_sum(i - 2, 1)
                    planes_bank(i + 1, c)
                fill_block(i, 0)
                if both:
                    for h in range(2):
                        read_sum(i - 2, h)
                read_block(i, 0)
                if i >= 2 and not both:
                    read_sum(i - 2, 0)
                scores(i - 1, 0, 0)
                if both:
                    block(i, 1)
                scores(i - 1, 0, 1)
                if not both:
                    block(i, 1)
                for c in range(2):
                    if rest:
                        planes_bank(i + 1, rest[c])
                    block(i, 2 + c)
                for h in range(2):
                    scores(i - 1, 1, h)
            else:
                for c in range(PACK):
                    if c == PACK - 1 and i >= 2 and not weighed(i - 2):
                        fill_sum(i - 2, 1)
                    planes_bank(i + 1, c)
                if i >= NO_WIDENING:
                    fill_sum(i - 2, 0)
                fill_block(i, 0)
                for h in range(0 if i < 2 else 1 if weighed(i - 2) else 2):
                    read_sum(i - 2, h)
                read_block(i, 0)
                scores(i - 1, 0, 0)
                block(i, 1)
                scores(i - 1, 0, 1)
                for n, c in enumerate(rest):
                    planes_bank(i + 1, c)
                    if i + AHEAD > LAST:
                        fill_block(i + 1, n)
                for h in range(2):
                    scores(i - 1, 1, h)
            if i >= 2 and weighed(i - 2):
                add_slices(i - 2, 1, u0_z[(i - 2) % 3])
            if 1 <= i < NO_WIDENING - 1 and weighed(i - 1):
                weigh(i - 1, 1, u0_z[(i - 1) % 3])
            for n in range(2):
                if i + AHEAD <= LAST:
                    turn_e(i + AHEAD, n)
            if 1 <= i < NO_WIDENING - 1 or i == LAST - 2:
                fill_sum(i - 1, 0)

        g8, g9, g10, g11 = range(LAST - 3, LAST + 1)
        quantize_e(g11)
        quantize_h(g9)
        weave_h(g10, nc.gpsimd.tensor_copy, vector_blocks(g10) * P, T * GROUP, "p (c i) t")
        for c in range(PACK):
            planes_bank(g11, c)
        fill_block(g11, 0)
        for c in range(2):
            read_block(g10, c)
        read_sum(g8, 0)
        for c in range(1, PACK):
            fill_block(g11, c)
            scores(g9, *divmod(c - 1, 2))
            read_block(g11, c - 1)
        scores(g9, 1, 1)
        read_block(g11, PACK - 1)
        fill_sum(g8, 1)
        fill_sum(g9, 0)
        weave_h(g11, nc.scalar.copy, GROUP, SPLIT, "p c t i")
        quantize_h(g10)
        quantize_h(g11, 0, GROUP)
        weave_h(g11, nc.gpsimd.tensor_copy, SPLIT, T * GROUP, "p (c i) t")
        for c in range(PACK):
            scores(g10, *divmod(c, 2))
        fill_sum(g10, 0)
        read_sum(g8, 1)
        read_sum(g9, 0)
        for h in range(2):
            scores(g11, 0, h)
        quantize_h(g11, GROUP, SPLIT)
        quantize_h(g11, SPLIT, T * GROUP)
        for h in range(2):
            scores(g11, 1, h)
        nc.vector.tensor_scalar(out=u0_z[0][:], in0=z(g9, 0, 1)[:], scalar1=u_f32[:, 0:1], scalar2=None, op0=MULT)
        nc.vector.tensor_scalar(out=u0_z[1][:], in0=z(g10, 0, 1)[:], scalar1=u_f32[:, 0:1], scalar2=None, op0=MULT)
        add_slices(g9, 1, u0_z[0])
        fill_sum(g11, 0)
        read_sum(g10, 0)
        add_slices(g10, 1, u0_z[1])
        nc.vector.tensor_scalar(out=u0_z[2][:], in0=z(g11, 0, 1)[:], scalar1=u_f32[:, 0:1], scalar2=None, op0=MULT)
        read_sum(g11, 0)
        add_slices(g11, 1, u0_z[2])
